import numpy as np
import ml_dtypes


def mxq(x, axis, fmt="e4m3"):
    dtype, down = {"e4m3": (ml_dtypes.float8_e4m3fn, 7), "e5m2": (ml_dtypes.float8_e5m2, 14)}[fmt]
    v = np.moveaxis(np.asarray(x, np.float32).astype(ml_dtypes.bfloat16).astype(np.float64), axis, -1)
    blocks = v.reshape(v.shape[:-1] + (-1, 32))
    amax = np.abs(blocks).max(-1, keepdims=True)
    byte = np.maximum(np.where(amax > 0, np.frexp(amax)[1] - 1 + 127, 0) - down, 1)
    scale = np.exp2(byte - 127.0)
    codes = (blocks / scale).astype(np.float32).astype(dtype).astype(np.float64)
    return np.moveaxis((codes * scale).reshape(v.shape), -1, axis)


WIDE = False


def mx_kscale(k):
    if not WIDE:
        return np.ones(k)
    levels = np.array([10, -10, 5, -5, 0])
    if k % 512:
        return np.exp2(np.random.permutation(np.resize(levels, k // 32))).repeat(32)
    a = np.empty((k // 512, 16))
    for p in range(k // 512):
        a[p, :8] = np.random.permutation(np.resize(levels, 8))
        for g in range(8):
            far = levels[np.abs(levels - a[p, g]) >= 10]
            a[p, g + 8] = far[np.random.randint(len(far))]
    return np.exp2(a.ravel()).repeat(32)


BF16 = ml_dtypes.bfloat16


def bf(x):
    return np.asarray(x, np.float32).astype(BF16)


def f64(x):
    return np.asarray(x).astype(np.float64)


E2M1 = np.array([0.0, 0.5, 1.0, 1.5, 2.0, 3.0, 4.0, 6.0, -0.0, -0.5, -1.0, -1.5, -2.0, -3.0, -4.0, -6.0])


def pack_weight(w, fmt):
    k, n = w.shape
    w = f64(bf(w)).reshape(k // 32, 32, n)
    amax = np.abs(w).max(1)
    if fmt == "e4m3":
        byte = np.frexp(amax)[1] - 1 + 127 - 7
    else:
        mant, ex = np.frexp(amax / 6.0)
        byte = np.where(mant > 0.5, ex, ex - 1) + 127
    byte = np.clip(np.where(amax > 0, byte, 1), 1, 254)
    scaled = (w * np.exp2(127.0 - byte)[:, None, :]).reshape(k, n).astype(np.float32)
    by_word = np.ascontiguousarray(scaled.reshape(k // 512, 128, 4, n).transpose(0, 1, 3, 2))
    if fmt == "e4m3":
        words = by_word.astype(ml_dtypes.float8_e4m3fn).view(np.uint8)
    else:
        c = by_word.astype(ml_dtypes.float4_e2m1fn).view(np.uint8) & 0xF
        words = c[..., 0::2] | (c[..., 1::2] << 4)
    return np.ascontiguousarray(words), np.ascontiguousarray(byte.astype(np.uint8).reshape(k // 512, 16, n))


def unpack_weight(words, scales, fmt):
    g, p, n, _ = words.shape
    if fmt == "e4m3":
        vals = np.ascontiguousarray(words).view(ml_dtypes.float8_e4m3fn).astype(np.float64)
    else:
        nib = np.empty((g, p, n, 4), np.uint8)
        nib[..., 0::2] = words & 0xF
        nib[..., 1::2] = words >> 4
        vals = E2M1[nib]
    vals = vals * np.repeat(np.exp2(scales.astype(np.float64) - 127.0), 8, axis=1)[..., None]
    return vals.transpose(0, 1, 3, 2).reshape(g * 512, n)
def pack4(w):
    words, scales = pack_weight(w, "e2m1")
    return words.reshape(words.shape[0], 128, -1), scales


def unpack4(words, scales):
    return unpack_weight(words.reshape(words.shape[0], 128, -1, 2), scales, "e2m1")


M, K, N = 512, 2048, 1536

MEAN = 0.5
SPREAD = 0.3


def setup_inputs():
    s = mx_kscale(K)
    hap = np.random.beta(0.5, 0.5, (M, K)) + np.random.beta(0.5, 0.5, (M, K))
    dosage = (hap - 1.0) * 2.0
    effect = np.random.standard_normal((K, N)) / np.sqrt(K)
    ancestry = MEAN * np.random.standard_normal((K, N)) / np.sqrt(K)
    spread = SPREAD * np.random.standard_normal((K, N)) / np.sqrt(K)
    effect_words, effect_scales = pack4(effect / s[:, None])
    ancestry_words, ancestry_scales = pack_weight(ancestry / s[:, None], "e4m3")
    return {"dosage": bf(dosage * s),
            "effect_words": effect_words,
            "effect_scales": effect_scales,
            "ancestry_words": ancestry_words,
            "ancestry_scales": ancestry_scales,
            "spread": bf(spread / s[:, None]),
            "offset": bf(0.3 * np.random.standard_normal(N))}


def reference(dosage, effect_words, effect_scales, ancestry_words, ancestry_scales, spread, offset):
    d = mxq(f64(dosage), 1, "e4m3")
    raw = d @ unpack4(effect_words, effect_scales)
    mean = d @ unpack_weight(ancestry_words, ancestry_scales, "e4m3")
    logp = (d @ mxq(f64(spread), 0, "e4m3")) + f64(offset)
    return (raw - mean) * np.exp(logp)

@@ -1,0 +1,283 @@
+from contextlib import ExitStack
+
+import concourse.mybir as mybir
+from concourse.masks import make_identity
+
+M, K, N = 512, 2048, 1536
+FLOPS = 3 * 2 * M * K * N
+
+F32 = mybir.dt.float32
+BF16 = mybir.dt.bfloat16
+I32 = mybir.dt.int32
+U32 = mybir.dt.uint32
+U8 = mybir.dt.uint8
+FP8X4 = mybir.dt.float8_e4m3fn_x4
+FP4X4 = mybir.dt.float4_e2m1fn_x4
+ALU = mybir.AluOpType
+EXP = mybir.ActivationFunctionType.Exp
+
+P = 128
+PACK = 4
+KP = P * PACK
+G = K // KP
+NT = 512
+MT = M // P
+NTILES = N // NT
+BANKS = 8
+
+
+def tile_ancestry_adjusted_scores_s10_kernel(
+    tc, dosage, effect_words, effect_scales, ancestry_words, ancestry_scales, spread, offset, out
+):
+    nc = tc.nc
+    with ExitStack() as ctx:
+        keep = ctx.enter_context(tc.tile_pool(name="keep", bufs=1))
+        ring = ctx.enter_context(tc.tile_pool(name="ring", bufs=1))
+        psum = ctx.enter_context(tc.psum_pool(name="psum", bufs=1))
+        ctx.enter_context(tc.manual_schedule())
+
+        def kept(name, shape, dtype):
+            return keep.tile(shape, dtype, name=name, align_bytes=64)
+
+        banks_taken = []
+
+        def next_bank():
+            i = len(banks_taken)
+            banks_taken.append(i)
+            return psum.tile([P, NT], F32, name="bank_use%d" % i, tag="bank%d" % (i % BANKS))
+
+        def cols(nt):
+            return slice(nt * NT, (nt + 1) * NT)
+
+        ident = kept("ident", [P, P], F32)
+        off_rows = kept("off_rows", [P, 2, 6], BF16)
+        off_all = kept("off_all", [P, N], BF16)
+        warm = kept("warm", [P, 1], F32)
+        warm_out = kept("warm_out", [P, 1], F32)
+        d_raw = [kept("d_raw%d" % m, [P, K], BF16) for m in range(MT)]
+        d_grp = [kept("d_grp%d" % m, [P, K], BF16) for m in range(MT)]
+        d_codes = [kept("d_codes%d" % m, [P, G * P], U32) for m in range(MT)]
+        d_scales = [kept("d_scales%d" % m, [P, G * P], U8) for m in range(MT)]
+        e_words = [kept("e_words%d" % nt, [P, G, 2 * NT], U8) for nt in range(NTILES)]
+        e_scales_first = kept("e_scales_first", [P, G, NT], U8)
+        e_scales_rest = kept("e_scales_rest", [P, G, N - NT], U8)
+        a_words = [kept("a_words%d" % nt, [P, G, NT], U32) for nt in range(NTILES)]
+        a_scales = kept("a_scales", [P, N], U8)
+        chunks = [(nt, g) for nt in range(NTILES) for g in range(G)]
+        v_raw = [kept("v_raw%d" % c, [P, PACK, NT], BF16) for c in range(len(chunks))]
+        v_codes = [kept("v_codes%d" % c, [P, NT], U32) for c in range(len(chunks))]
+        v_scales = [kept("v_scales%d" % c, [P, NT], U8) for c in range(len(chunks))]
+        acc = {(nt, m): kept("acc%d_%d" % (nt, m), [P, NT], F32) for nt in range(NTILES) for m in range(MT)}
+        v_grp = {}
+        expo = {}
+
+        def load_d(m):
+            nc.sync.dma_start(out=d_raw[m][:], in_=dosage[m * P : (m + 1) * P, :])
+
+        def load_e(nt):
+            src = effect_words[:, :, 2 * nt * NT : 2 * (nt + 1) * NT].rearrange("g p b -> p g b")
+            nc.sync.dma_start(out=e_words[nt][:].bitcast(I32), in_=src.bitcast(I32))
+
+        def load_e_scales(plane, n0, n1):
+            for q in range(4):
+                src = effect_scales[:, 4 * q : 4 * q + 4, n0:n1].rearrange("g r n -> r g n")
+                nc.sync.dma_start(out=plane[32 * q : 32 * q + 4, :, :].bitcast(I32), in_=src.bitcast(I32))
+
+        def load_a(nt):
+            src = ancestry_words[:, :, cols(nt), :].rearrange("g p n t -> p g (n t)")
+            nc.sync.dma_start(out=a_words[nt][:].bitcast(I32), in_=src.bitcast(I32))
+
+        def load_a_scales():
+            for q in range(4):
+                src = ancestry_scales[:, 4 * q : 4 * q + 4, :]
+                nc.sync.dma_start(out=a_scales[32 * q : 32 * q + 16, :].bitcast(I32), in_=src.bitcast(I32))
+
+        def load_v(c):
+            nt, g = chunks[c]
+            src = spread[g * KP : (g + 1) * KP, cols(nt)].rearrange("(p j) n -> p j n", j=PACK)
+            nc.sync.dma_start(out=v_raw[c][:], in_=src)
+
+        nc.scalar.dma_start(out=off_rows[:], in_=offset.rearrange("(h p c) -> p h c", h=2, p=P))
+        nc.vector.memset(warm[:], 0.0)
+        nc.vector.memset(e_scales_first[:].bitcast(I32), 0)
+        nc.vector.memset(e_scales_rest[:].bitcast(I32), 0)
+        nc.vector.memset(a_scales[:].bitcast(I32), 0)
+        make_identity(nc, ident[:])
+        nc.scalar.activation(out=warm_out[:], in_=warm[:], func=EXP)
+
+        load_d(0)
+        load_e_scales(e_scales_first, 0, NT)
+        load_d(1)
+        load_e(0)
+        load_d(2)
+        load_d(3)
+        load_e_scales(e_scales_rest, NT, N)
+        load_a_scales()
+        load_e(1)
+        load_v(0)
+        load_v(1)
+        load_e(2)
+        for c in (2, 3, 4, 5):
+            load_v(c)
+        load_a(0)
+        for c in (6, 7, 8, 9):
+            load_v(c)
+        load_a(1)
+        load_v(10)
+        load_v(11)
+        load_a(2)
+
+        def spread_offset(h):
+            bank = next_bank()
+            words = off_rows[:, h, :].bitcast(F32)
+            for c in range(3):
+                nc.tensor.transpose(bank[:, c * P : (c + 1) * P], words[:, c : c + 1].to_broadcast([P, P]), ident[:])
+            dst = off_all[:].bitcast(F32)[:, h * 3 * P : (h + 1) * 3 * P]
+            nc.scalar.copy(
+                out=dst.rearrange("q (p c) -> q p c", c=3),
+                in_=bank[:, 0 : 3 * P].rearrange("q (c p) -> q p c", c=3),
+            )
+
+        def quantize_d(m):
+            words = d_raw[m][:].bitcast(F32)
+            grouped = d_grp[m][:].bitcast(F32)
+            for h in range(2):
+                bank = next_bank()
+                for gl in range(2):
+                    g = 2 * h + gl
+                    for u in range(2):
+                        j = 2 * gl + u
+                        nc.tensor.transpose(
+                            bank[:, j * P : (j + 1) * P], words[:, 256 * g + u : 256 * (g + 1) : 2], ident[:]
+                        )
+                dst = grouped[:, h * NT : (h + 1) * NT].rearrange("p (g r u) -> p g r u", g=2, u=2)
+                src = bank[:].rearrange("p (g u r) -> p g r u", g=2, u=2)
+                if h == 0:
+                    nc.scalar.copy(out=dst, in_=src)
+                else:
+                    nc.vector.tensor_copy(out=dst, in_=src)
+            for h in range(2):
+                nc.vector.quantize_mx(
+                    out=d_codes[m][:, 256 * h : 256 * (h + 1)].bitcast(FP8X4),
+                    scales=d_scales[m][:, 256 * h : 256 * (h + 1)],
+                    in_=d_grp[m][:, 1024 * h : 1024 * (h + 1)],
+                )
+
+        def interleave(on_scalar, c, n0, n1):
+            if c not in v_grp:
+                v_grp[c] = ring.tile([P, NT, PACK], BF16, name="v_grp%d" % c, tag="v_grp", bufs=4, align_bytes=64)
+            dst = v_grp[c][:, n0:n1, :].rearrange("p (c i) t -> p c t i", i=4)
+            src = v_raw[c][:, :, n0:n1].rearrange("p t (c i) -> p c t i", i=4)
+            if on_scalar:
+                nc.scalar.copy(out=dst, in_=src)
+            else:
+                nc.vector.tensor_copy(out=dst, in_=src)
+
+        def quantize_v(c):
+            nc.vector.quantize_mx(
+                out=v_codes[c][:].bitcast(FP8X4),
+                scales=v_scales[c][:],
+                in_=v_grp[c][:].rearrange("p n t -> p (n t)"),
+            )
+
+        def background(items):
+            for kind, c in items:
+                if kind == "q":
+                    quantize_v(c)
+                elif kind == "v":
+                    interleave(False, c, 0, NT)
+                elif kind == "s":
+                    interleave(True, c, 0, NT)
+                elif kind == "s0":
+                    interleave(True, c, 0, NT // 2)
+                else:
+                    interleave(True, c, NT // 2, NT)
+
+        def product(m, operand):
+            bank = next_bank()
+            for g in range(G):
+                rhs, rhs_scale = operand(g)
+                nc.tensor.matmul_mx(
+                    out=bank[:],
+                    lhsT=d_codes[m][:, g * P : (g + 1) * P].bitcast(FP8X4),
+                    lhsT_scale=d_scales[m][:, g * P : (g + 1) * P],
+                    rhs=rhs,
+                    rhs_scale=rhs_scale,
+                    start=(g == 0),
+                    stop=(g == G - 1),
+                )
+            return bank
+
+        def effect_product(nt, m, items):
+            def operand(g):
+                if nt == 0:
+                    plane = e_scales_first[:, g, :]
+                else:
+                    plane = e_scales_rest[:, g, cols(nt - 1)]
+                return e_words[nt][:, g, :].bitcast(FP4X4), plane
+
+            bank = product(m, operand)
+            nc.scalar.copy(out=acc[nt, m][:], in_=bank[:])
+            background(items)
+
+        def finish(nt, m):
+            nc.vector.tensor_tensor(out=acc[nt, m][:], in0=acc[nt, m][:], in1=expo[nt, m][:], op=ALU.mult)
+            nc.sync.dma_start(out=out[m * P : (m + 1) * P, cols(nt)], in_=acc[nt, m][:])
+
+        def ancestry_product(nt, m, items):
+            bank = product(m, lambda g: (a_words[nt][:, g, :].bitcast(FP8X4), a_scales[4 * g :, cols(nt)]))
+            nc.vector.tensor_tensor(out=acc[nt, m][:], in0=acc[nt, m][:], in1=bank[:], op=ALU.subtract)
+            if m == 0 and nt > 0:
+                finish(nt - 1, MT - 1)
+            background(items)
+
+        def spread_product(nt, m, items):
+            bank = product(m, lambda g: (v_codes[nt * G + g][:].bitcast(FP8X4), v_scales[nt * G + g][:]))
+            logp = ring.tile([P, NT], F32, name="logp%d_%d" % (nt, m), tag="logp", bufs=3)
+            expo[nt, m] = ring.tile([P, NT], F32, name="expo%d_%d" % (nt, m), tag="expo", bufs=3)
+            nc.vector.tensor_tensor(out=logp[:], in0=bank[:], in1=off_all[:, cols(nt)], op=ALU.add)
+            nc.scalar.activation(out=expo[nt, m][:], in_=logp[:], func=EXP)
+            if m > 0:
+                finish(nt, m - 1)
+            background(items)
+
+        spread_offset(0)
+        spread_offset(1)
+        quantize_d(0)
+        quantize_d(1)
+        effect_product(0, 0, [])
+        effect_product(0, 1, [])
+        quantize_d(2)
+        quantize_d(3)
+        effect_product(1, 0, [("v", 0)])
+        effect_product(1, 1, [("v", 1)])
+        effect_product(0, 2, [("q", 0)])
+        effect_product(0, 3, [("q", 1), ("v", 2)])
+        effect_product(1, 2, [("v", 3)])
+        effect_product(1, 3, [("q", 2)])
+        effect_product(2, 0, [("v", 4), ("q", 3)])
+        effect_product(2, 1, [("q", 4), ("s0", 5)])
+        effect_product(2, 2, [])
+        effect_product(2, 3, [("s1", 5)])
+
+        beside_ancestry = {
+            (0, 0): [("q", 5), ("s", 6)],
+            (0, 2): [("q", 6), ("s", 7)],
+            (1, 0): [("q", 8), ("s", 9)],
+            (1, 2): [("s0", 10)],
+            (1, 3): [("q", 9)],
+            (2, 1): [("q", 11)],
+        }
+        beside_spread = {
+            (0, 0): [("q", 7), ("s0", 8)],
+            (0, 2): [("s1", 8)],
+            (1, 0): [("s1", 10)],
+            (1, 2): [("q", 10), ("s0", 11)],
+            (1, 3): [("s1", 11)],
+        }
+        for nt in range(NTILES):
+            for m in range(MT):
+                ancestry_product(nt, m, beside_ancestry.get((nt, m), []))
+            for m in range(MT):
+                spread_product(nt, m, beside_spread.get((nt, m), []))
+        finish(NTILES - 1, MT - 1)

@@ -24,6 +24,7 @@ NT = 512
 MT = M // P
 NTILES = N // NT
 BANKS = 8
+WARM_PASSES = 20
 
 
 def tile_ancestry_adjusted_scores_s10_kernel(
@@ -52,10 +53,13 @@ def tile_ancestry_adjusted_scores_s10_kernel(
         ident = kept("ident", [P, P], F32)
         off_rows = kept("off_rows", [P, 2, 6], BF16)
         off_all = kept("off_all", [P, N], BF16)
-        warm = kept("warm", [P, 1], F32)
         warm_out = kept("warm_out", [P, 1], F32)
         d_raw = [kept("d_raw%d" % m, [P, K], BF16) for m in range(MT)]
-        d_grp = [kept("d_grp%d" % m, [P, K], BF16) for m in range(MT)]
+        d_perm = {}
+        d_grp = {}
+        warm_in = kept("warm_in", [P, KP], BF16)
+        warm_codes = kept("warm_codes", [P, P], U32)
+        warm_scales = kept("warm_scales", [P, P], U8)
         d_codes = [kept("d_codes%d" % m, [P, G * P], U32) for m in range(MT)]
         d_scales = [kept("d_scales%d" % m, [P, G * P], U8) for m in range(MT)]
         e_words = [kept("e_words%d" % nt, [P, G, 2 * NT], U8) for nt in range(NTILES)]
@@ -71,12 +75,12 @@ def tile_ancestry_adjusted_scores_s10_kernel(
         v_grp = {}
         expo = {}
 
-        def load_d(m):
-            nc.sync.dma_start(out=d_raw[m][:], in_=dosage[m * P : (m + 1) * P, :])
+        def load_d(m, k0, k1):
+            nc.sync.dma_start(out=d_raw[m][:, k0:k1], in_=dosage[m * P : (m + 1) * P, k0:k1])
 
-        def load_e(nt):
-            src = effect_words[:, :, 2 * nt * NT : 2 * (nt + 1) * NT].rearrange("g p b -> p g b")
-            nc.sync.dma_start(out=e_words[nt][:].bitcast(I32), in_=src.bitcast(I32))
+        def load_e(nt, g0, g1):
+            src = effect_words[g0:g1, :, 2 * nt * NT : 2 * (nt + 1) * NT].rearrange("g p b -> p g b")
+            nc.sync.dma_start(out=e_words[nt][:, g0:g1, :].bitcast(I32), in_=src.bitcast(I32))
 
         def load_e_scales(plane, n0, n1):
             for q in range(4):
@@ -98,74 +102,94 @@ def tile_ancestry_adjusted_scores_s10_kernel(
             nc.sync.dma_start(out=v_raw[c][:], in_=src)
 
         nc.scalar.dma_start(out=off_rows[:], in_=offset.rearrange("(h p c) -> p h c", h=2, p=P))
-        nc.vector.memset(warm[:], 0.0)
+        nc.vector.memset(warm_in[:], 1.0)
         nc.vector.memset(e_scales_first[:].bitcast(I32), 0)
+        nc.vector.quantize_mx(out=warm_codes[:].bitcast(FP8X4), scales=warm_scales[:], in_=warm_in[:])
         nc.vector.memset(e_scales_rest[:].bitcast(I32), 0)
         nc.vector.memset(a_scales[:].bitcast(I32), 0)
         make_identity(nc, ident[:])
-        nc.scalar.activation(out=warm_out[:], in_=warm[:], func=EXP)
+        nc.scalar.activation(out=warm_out[:], in_=warm_in[:, 0:1], func=EXP)
+        warm_bank = next_bank()
+        for i in range(WARM_PASSES):
+            nc.tensor.matmul_mx(
+                out=warm_bank[:, 0:P],
+                lhsT=warm_codes[:].bitcast(FP8X4),
+                lhsT_scale=warm_scales[:],
+                rhs=warm_codes[:].bitcast(FP8X4),
+                rhs_scale=warm_scales[:],
+                start=(i == 0),
+                stop=(i == WARM_PASSES - 1),
+            )
 
-        load_d(0)
+        load_d(0, 0, K // 2)
+        load_d(0, K // 2, K)
+        load_d(1, 0, K)
         load_e_scales(e_scales_first, 0, NT)
-        load_d(1)
-        load_e(0)
-        load_d(2)
-        load_d(3)
+        load_e(0, 0, 2)
+        load_e(0, 2, 4)
+        load_d(2, 0, K)
+        load_d(3, 0, K)
         load_e_scales(e_scales_rest, NT, N)
-        load_a_scales()
-        load_e(1)
-        load_v(0)
-        load_v(1)
-        load_e(2)
-        for c in (2, 3, 4, 5):
-            load_v(c)
-        load_a(0)
-        for c in (6, 7, 8, 9):
-            load_v(c)
-        load_a(1)
-        load_v(10)
-        load_v(11)
-        load_a(2)
+        for kind, i in (
+            [("e", 1), ("v", 0), ("v", 1), ("e", 2)]
+            + [("v", c) for c in (2, 3, 4, 5)]
+            + [("a", 0), ("v", 6), ("v", 7), ("a", 1)]
+            + [("v", c) for c in (8, 9, 10, 11)]
+            + [("a", 2)]
+        ):
+            if kind == "e":
+                load_e(i, 0, G)
+            elif kind == "v":
+                load_v(i)
+            else:
+                if i == 0:
+                    load_a_scales()
+                load_a(i)
 
-        def spread_offset(h):
+        def transpose_offset(h):
             bank = next_bank()
             words = off_rows[:, h, :].bitcast(F32)
             for c in range(3):
                 nc.tensor.transpose(bank[:, c * P : (c + 1) * P], words[:, c : c + 1].to_broadcast([P, P]), ident[:])
+            return bank
+
+        def copy_offset(h, bank):
             dst = off_all[:].bitcast(F32)[:, h * 3 * P : (h + 1) * 3 * P]
             nc.scalar.copy(
                 out=dst.rearrange("q (p c) -> q p c", c=3),
                 in_=bank[:, 0 : 3 * P].rearrange("q (c p) -> q p c", c=3),
             )
 
-        def quantize_d(m):
-            words = d_raw[m][:].bitcast(F32)
-            grouped = d_grp[m][:].bitcast(F32)
-            for h in range(2):
-                bank = next_bank()
-                for gl in range(2):
-                    g = 2 * h + gl
-                    for u in range(2):
-                        j = 2 * gl + u
-                        nc.tensor.transpose(
-                            bank[:, j * P : (j + 1) * P], words[:, 256 * g + u : 256 * (g + 1) : 2], ident[:]
-                        )
-                dst = grouped[:, h * NT : (h + 1) * NT].rearrange("p (g r u) -> p g r u", g=2, u=2)
-                src = bank[:].rearrange("p (g u r) -> p g r u", g=2, u=2)
-                if h == 0:
-                    nc.scalar.copy(out=dst, in_=src)
-                else:
-                    nc.vector.tensor_copy(out=dst, in_=src)
-            for h in range(2):
-                nc.vector.quantize_mx(
-                    out=d_codes[m][:, 256 * h : 256 * (h + 1)].bitcast(FP8X4),
-                    scales=d_scales[m][:, 256 * h : 256 * (h + 1)],
-                    in_=d_grp[m][:, 1024 * h : 1024 * (h + 1)],
+        def order_words(m, h):
+            half = slice(h * NT, (h + 1) * NT)
+            nc.vector.tensor_copy(
+                out=d_perm[m][:, half].rearrange("r (g u p) -> r g u p", g=2, u=2),
+                in_=d_raw[m][:].bitcast(F32)[:, half].rearrange("r (g p u) -> r g u p", g=2, u=2),
+            )
+
+        def transpose_d(m, h):
+            bank = next_bank()
+            for j in range(4):
+                nc.tensor.transpose(
+                    bank[:, j * P : (j + 1) * P], d_perm[m][:, h * NT + j * P : h * NT + (j + 1) * P], ident[:]
                 )
+            dst = d_grp[m][:].bitcast(F32)[:, h * NT : (h + 1) * NT].rearrange("p (g r u) -> p g r u", g=2, u=2)
+            nc.scalar.copy(out=dst, in_=bank[:].rearrange("p (g u r) -> p g r u", g=2, u=2))
+
+        def quantize_d(m, h):
+            nc.vector.quantize_mx(
+                out=d_codes[m][:, 256 * h : 256 * (h + 1)].bitcast(FP8X4),
+                scales=d_scales[m][:, 256 * h : 256 * (h + 1)],
+                in_=d_grp[m][:, 1024 * h : 1024 * (h + 1)],
+            )
+
+        def new_d_tiles(m):
+            d_perm[m] = ring.tile([P, K // 2], F32, name="d_perm%d" % m, tag="d_perm", bufs=2, align_bytes=64)
+            d_grp[m] = ring.tile([P, K], BF16, name="d_grp%d" % m, tag="d_grp", bufs=2, align_bytes=64)
 
         def interleave(on_scalar, c, n0, n1):
             if c not in v_grp:
-                v_grp[c] = ring.tile([P, NT, PACK], BF16, name="v_grp%d" % c, tag="v_grp", bufs=4, align_bytes=64)
+                v_grp[c] = ring.tile([P, NT, PACK], BF16, name="v_grp%d" % c, tag="v_grp", bufs=5, align_bytes=64)
             dst = v_grp[c][:, n0:n1, :].rearrange("p (c i) t -> p c t i", i=4)
             src = v_raw[c][:, :, n0:n1].rearrange("p t (c i) -> p c t i", i=4)
             if on_scalar:
@@ -188,17 +212,21 @@ def tile_ancestry_adjusted_scores_s10_kernel(
                     interleave(False, c, 0, NT)
                 elif kind == "s":
                     interleave(True, c, 0, NT)
+                elif kind == "v0":
+                    interleave(False, c, 0, NT // 2)
+                elif kind == "v1":
+                    interleave(False, c, NT // 2, NT)
                 elif kind == "s0":
                     interleave(True, c, 0, NT // 2)
                 else:
                     interleave(True, c, NT // 2, NT)
 
-        def product(m, operand):
+        def product(m, width, operand):
             bank = next_bank()
             for g in range(G):
                 rhs, rhs_scale = operand(g)
                 nc.tensor.matmul_mx(
-                    out=bank[:],
+                    out=bank[:, 0:width],
                     lhsT=d_codes[m][:, g * P : (g + 1) * P].bitcast(FP8X4),
                     lhsT_scale=d_scales[m][:, g * P : (g + 1) * P],
                     rhs=rhs,
@@ -206,9 +234,9 @@ def tile_ancestry_adjusted_scores_s10_kernel(
                     start=(g == 0),
                     stop=(g == G - 1),
                 )
-            return bank
+            return bank[:, 0:width]
 
-        def effect_product(nt, m, items):
+        def effect_product(nt, m):
             def operand(g):
                 if nt == 0:
                     plane = e_scales_first[:, g, :]
@@ -216,68 +244,100 @@ def tile_ancestry_adjusted_scores_s10_kernel(
                     plane = e_scales_rest[:, g, cols(nt - 1)]
                 return e_words[nt][:, g, :].bitcast(FP4X4), plane
 
-            bank = product(m, operand)
-            nc.scalar.copy(out=acc[nt, m][:], in_=bank[:])
-            background(items)
+            return product(m, NT, operand)
 
-        def finish(nt, m):
-            nc.vector.tensor_tensor(out=acc[nt, m][:], in0=acc[nt, m][:], in1=expo[nt, m][:], op=ALU.mult)
-            nc.sync.dma_start(out=out[m * P : (m + 1) * P, cols(nt)], in_=acc[nt, m][:])
+        def keep_raw(nt, m, raw):
+            nc.scalar.copy(out=acc[nt, m][:], in_=raw)
 
-        def ancestry_product(nt, m, items):
-            bank = product(m, lambda g: (a_words[nt][:, g, :].bitcast(FP8X4), a_scales[4 * g :, cols(nt)]))
-            nc.vector.tensor_tensor(out=acc[nt, m][:], in0=acc[nt, m][:], in1=bank[:], op=ALU.subtract)
-            if m == 0 and nt > 0:
-                finish(nt - 1, MT - 1)
-            background(items)
+        def ancestry_product(nt, m, n0, n1):
+            mean = product(
+                m,
+                n1 - n0,
+                lambda g: (a_words[nt][:, g, n0:n1].bitcast(FP8X4), a_scales[4 * g :, nt * NT + n0 : nt * NT + n1]),
+            )
+            part = acc[nt, m][:, n0:n1]
+            nc.vector.tensor_tensor(out=part, in0=part, in1=mean, op=ALU.subtract)
 
-        def spread_product(nt, m, items):
-            bank = product(m, lambda g: (v_codes[nt * G + g][:].bitcast(FP8X4), v_scales[nt * G + g][:]))
-            logp = ring.tile([P, NT], F32, name="logp%d_%d" % (nt, m), tag="logp", bufs=3)
-            expo[nt, m] = ring.tile([P, NT], F32, name="expo%d_%d" % (nt, m), tag="expo", bufs=3)
-            nc.vector.tensor_tensor(out=logp[:], in0=bank[:], in1=off_all[:, cols(nt)], op=ALU.add)
-            nc.scalar.activation(out=expo[nt, m][:], in_=logp[:], func=EXP)
-            if m > 0:
-                finish(nt, m - 1)
-            background(items)
+        def spread_product(nt, m, n0, n1):
+            sums = product(
+                m, n1 - n0, lambda g: (v_codes[nt * G + g][:, n0:n1].bitcast(FP8X4), v_scales[nt * G + g][:, n0:n1])
+            )
+            if n0 == 0:
+                expo[nt, m] = ring.tile([P, NT], F32, name="expo%d_%d" % (nt, m), tag="expo", bufs=6)
+            nc.vector.tensor_tensor(
+                out=expo[nt, m][:, n0:n1], in0=sums, in1=off_all[:, nt * NT + n0 : nt * NT + n1], op=ALU.add
+            )
+            nc.scalar.activation(out=expo[nt, m][:, n0:n1], in_=expo[nt, m][:, n0:n1], func=EXP)
 
-        spread_offset(0)
-        spread_offset(1)
-        quantize_d(0)
-        quantize_d(1)
-        effect_product(0, 0, [])
-        effect_product(0, 1, [])
-        quantize_d(2)
-        quantize_d(3)
-        effect_product(1, 0, [("v", 0)])
-        effect_product(1, 1, [("v", 1)])
-        effect_product(0, 2, [("q", 0)])
-        effect_product(0, 3, [("q", 1), ("v", 2)])
-        effect_product(1, 2, [("v", 3)])
-        effect_product(1, 3, [("q", 2)])
-        effect_product(2, 0, [("v", 4), ("q", 3)])
-        effect_product(2, 1, [("q", 4), ("s0", 5)])
-        effect_product(2, 2, [])
-        effect_product(2, 3, [("s1", 5)])
+        def finish(engine, nt, m, n0, n1):
+            part = acc[nt, m][:, n0:n1]
+            engine.tensor_tensor(out=part, in0=part, in1=expo[nt, m][:, n0:n1], op=ALU.mult)
+            nc.sync.dma_start(out=out[m * P : (m + 1) * P, nt * NT + n0 : nt * NT + n1], in_=part)
 
-        beside_ancestry = {
-            (0, 0): [("q", 5), ("s", 6)],
-            (0, 2): [("q", 6), ("s", 7)],
-            (1, 0): [("q", 8), ("s", 9)],
-            (1, 2): [("s0", 10)],
-            (1, 3): [("q", 9)],
-            (2, 1): [("q", 11)],
+        new_d_tiles(0)
+        new_d_tiles(1)
+        for h in range(2):
+            order_words(0, h)
+            transpose_d(0, h)
+        offset_banks = [transpose_offset(h) for h in range(2)]
+        for h in range(2):
+            order_words(1, h)
+            transpose_d(1, h)
+        for m in (0, 1):
+            for h in range(2):
+                quantize_d(m, h)
+        for h in range(2):
+            copy_offset(h, offset_banks[h])
+        new_d_tiles(2)
+        new_d_tiles(3)
+        order_words(2, 0)
+        order_words(2, 1)
+        keep_raw(0, 0, effect_product(0, 0))
+        order_words(3, 0)
+        order_words(3, 1)
+        raw_held = effect_product(0, 1)
+        for m in (2, 3):
+            for h in range(2):
+                transpose_d(m, h)
+                quantize_d(m, h)
+        keep_raw(0, 1, raw_held)
+        beside_effect = {
+            (0, 3): [("v", 0), ("v", 1), ("q", 0), ("v", 2), ("q", 1), ("v", 3), ("q", 2), ("q", 3)],
+            (2, 2): [("s0", 5)],
+            (2, 3): [("s1", 5)],
         }
-        beside_spread = {
-            (0, 0): [("q", 7), ("s0", 8)],
-            (0, 2): [("s1", 8)],
-            (1, 0): [("s1", 10)],
-            (1, 2): [("q", 10), ("s0", 11)],
-            (1, 3): [("s1", 11)],
+        for nt, m in [(0, 2), (0, 3)] + [(nt, m) for nt in (1, 2) for m in range(MT)]:
+            keep_raw(nt, m, effect_product(nt, m))
+            background(beside_effect.get((nt, m), []))
+
+        steps = [("V", 0, m) for m in range(MT)] + [("A", 0, m) for m in range(MT)]
+        steps += [("A", 1, m) for m in range(MT)] + [("V", 1, m) for m in range(MT)]
+        steps += [("A", 2, 0), ("A", 2, 1), ("A", 2, 2), ("V", 2, 0), ("V", 2, 1), ("V", 2, 2), ("V", 2, 3)]
+        beside = {
+            ("V", 0, 0): [("v", 4)],
+            ("V", 0, 1): [("q", 4), ("s0", 6)],
+            ("V", 0, 2): [("q", 5)],
+            ("V", 0, 3): [("s1", 6), ("s", 7), ("s", 8), ("s", 9)],
+            ("A", 1, 1): [("q", 6), ("q", 7)],
+            ("A", 1, 2): [("q", 8), ("s0", 10), ("s0", 11)],
+            ("A", 1, 3): [("v1", 10), ("v1", 11), ("q", 9)],
+            ("V", 1, 0): [("q", 10), ("q", 11)],
         }
-        for nt in range(NTILES):
-            for m in range(MT):
-                ancestry_product(nt, m, beside_ancestry.get((nt, m), []))
-            for m in range(MT):
-                spread_product(nt, m, beside_spread.get((nt, m), []))
-        finish(NTILES - 1, MT - 1)
+        seen = set()
+        ready = []
+        for step in steps:
+            kind, nt, m = step
+            if kind == "A":
+                ancestry_product(nt, m, 0, NT)
+            else:
+                spread_product(nt, m, 0, NT)
+            for done in ready:
+                finish(nc.gpsimd if done != (2, 1) else nc.vector, done[0], done[1], 0, NT)
+            ready = [(nt, m)] if (nt, m) in seen else []
+            seen.add((nt, m))
+            background(beside.get(step, []))
+        last = (NTILES - 1, MT - 1)
+        ancestry_product(*last, 0, NT // 2)
+        ancestry_product(*last, NT // 2, NT)
+        finish(nc.vector, *last, 0, NT // 2)
+        finish(nc.vector, *last, NT // 2, NT)

@@ -24,7 +24,10 @@ NT = 512
 MT = M // P
 NTILES = N // NT
 BANKS = 8
-WARM_PASSES = 20
+HALF = K // 2
+SCALAR_COLS = 0
+WARM_FIRST = 6
+WARM_SECOND = 4
 
 
 def tile_ancestry_adjusted_scores_s10_kernel(
@@ -51,20 +54,19 @@ def tile_ancestry_adjusted_scores_s10_kernel(
             return slice(nt * NT, (nt + 1) * NT)
 
         ident = kept("ident", [P, P], F32)
-        off_rows = kept("off_rows", [P, 2, 6], BF16)
+        off_rows = kept("off_rows", [P, 48], BF16)
+        off_wide = kept("off_wide", [P, 24, 32], F32)
+        off_turned = kept("off_turned", [P, 24, 32], F32)
         off_all = kept("off_all", [P, N], BF16)
+        warm_in = kept("warm_in", [P, 2 * NT], BF16)
         warm_out = kept("warm_out", [P, 1], F32)
+        warm_codes = kept("warm_codes", [P, 256], U32)
+        warm_scales = kept("warm_scales", [P, 256], U8)
         d_raw = [kept("d_raw%d" % m, [P, K], BF16) for m in range(MT)]
-        d_perm = {}
-        d_grp = {}
-        warm_in = kept("warm_in", [P, KP], BF16)
-        warm_codes = kept("warm_codes", [P, P], U32)
-        warm_scales = kept("warm_scales", [P, P], U8)
         d_codes = [kept("d_codes%d" % m, [P, G * P], U32) for m in range(MT)]
         d_scales = [kept("d_scales%d" % m, [P, G * P], U8) for m in range(MT)]
         e_words = [kept("e_words%d" % nt, [P, G, 2 * NT], U8) for nt in range(NTILES)]
-        e_scales_first = kept("e_scales_first", [P, G, NT], U8)
-        e_scales_rest = kept("e_scales_rest", [P, G, N - NT], U8)
+        e_scales = [kept("e_scales%d" % nt, [P, G, NT], U8) for nt in range(NTILES)]
         a_words = [kept("a_words%d" % nt, [P, G, NT], U32) for nt in range(NTILES)]
         a_scales = kept("a_scales", [P, N], U8)
         chunks = [(nt, g) for nt in range(NTILES) for g in range(G)]
@@ -72,8 +74,7 @@ def tile_ancestry_adjusted_scores_s10_kernel(
         v_codes = [kept("v_codes%d" % c, [P, NT], U32) for c in range(len(chunks))]
         v_scales = [kept("v_scales%d" % c, [P, NT], U8) for c in range(len(chunks))]
         acc = {(nt, m): kept("acc%d_%d" % (nt, m), [P, NT], F32) for nt in range(NTILES) for m in range(MT)}
-        v_grp = {}
-        expo = {}
+        d_sorted, d_banks, d_grp, v_grp, expo = {}, {}, {}, {}, {}
 
         def load_d(m, k0, k1):
             nc.sync.dma_start(out=d_raw[m][:, k0:k1], in_=dosage[m * P : (m + 1) * P, k0:k1])
@@ -82,10 +83,10 @@ def tile_ancestry_adjusted_scores_s10_kernel(
             src = effect_words[g0:g1, :, 2 * nt * NT : 2 * (nt + 1) * NT].rearrange("g p b -> p g b")
             nc.sync.dma_start(out=e_words[nt][:, g0:g1, :].bitcast(I32), in_=src.bitcast(I32))
 
-        def load_e_scales(plane, n0, n1):
-            for q in range(4):
-                src = effect_scales[:, 4 * q : 4 * q + 4, n0:n1].rearrange("g r n -> r g n")
-                nc.sync.dma_start(out=plane[32 * q : 32 * q + 4, :, :].bitcast(I32), in_=src.bitcast(I32))
+        def load_e_scales(nt):
+            for r in range(4):
+                src = effect_scales[:, r:16:4, cols(nt)].rearrange("g q n -> q g n")
+                nc.sync.dma_start(out=e_scales[nt][r:P:32, :, :].bitcast(I32), in_=src.bitcast(I32))
 
         def load_a(nt):
             src = ancestry_words[:, :, cols(nt), :].rearrange("g p n t -> p g (n t)")
@@ -101,101 +102,70 @@ def tile_ancestry_adjusted_scores_s10_kernel(
             src = spread[g * KP : (g + 1) * KP, cols(nt)].rearrange("(p j) n -> p j n", j=PACK)
             nc.sync.dma_start(out=v_raw[c][:], in_=src)
 
-        nc.scalar.dma_start(out=off_rows[:], in_=offset.rearrange("(h p c) -> p h c", h=2, p=P))
-        nc.vector.memset(warm_in[:], 1.0)
-        nc.vector.memset(e_scales_first[:].bitcast(I32), 0)
-        nc.vector.quantize_mx(out=warm_codes[:].bitcast(FP8X4), scales=warm_scales[:], in_=warm_in[:])
-        nc.vector.memset(e_scales_rest[:].bitcast(I32), 0)
-        nc.vector.memset(a_scales[:].bitcast(I32), 0)
-        make_identity(nc, ident[:])
-        nc.scalar.activation(out=warm_out[:], in_=warm_in[:, 0:1], func=EXP)
-        warm_bank = next_bank()
-        for i in range(WARM_PASSES):
-            nc.tensor.matmul_mx(
-                out=warm_bank[:, 0:P],
-                lhsT=warm_codes[:].bitcast(FP8X4),
-                lhsT_scale=warm_scales[:],
-                rhs=warm_codes[:].bitcast(FP8X4),
-                rhs_scale=warm_scales[:],
-                start=(i == 0),
-                stop=(i == WARM_PASSES - 1),
-            )
+        def clear(plane):
+            nc.vector.memset(plane[:].bitcast(I32), 0)
 
-        load_d(0, 0, K // 2)
-        load_d(0, K // 2, K)
-        load_d(1, 0, K)
-        load_e_scales(e_scales_first, 0, NT)
-        load_e(0, 0, 2)
-        load_e(0, 2, 4)
-        load_d(2, 0, K)
-        load_d(3, 0, K)
-        load_e_scales(e_scales_rest, NT, N)
-        for kind, i in (
-            [("e", 1), ("v", 0), ("v", 1), ("e", 2)]
-            + [("v", c) for c in (2, 3, 4, 5)]
-            + [("a", 0), ("v", 6), ("v", 7), ("a", 1)]
-            + [("v", c) for c in (8, 9, 10, 11)]
-            + [("a", 2)]
-        ):
-            if kind == "e":
-                load_e(i, 0, G)
-            elif kind == "v":
-                load_v(i)
-            else:
-                if i == 0:
-                    load_a_scales()
-                load_a(i)
-
-        def transpose_offset(h):
+        def warm_up(passes):
             bank = next_bank()
-            words = off_rows[:, h, :].bitcast(F32)
-            for c in range(3):
-                nc.tensor.transpose(bank[:, c * P : (c + 1) * P], words[:, c : c + 1].to_broadcast([P, P]), ident[:])
-            return bank
+            for i in range(passes):
+                nc.tensor.matmul_mx(
+                    out=bank[:, 0:256],
+                    lhsT=warm_codes[:, 0:P].bitcast(FP8X4),
+                    lhsT_scale=warm_scales[:, 0:P],
+                    rhs=warm_codes[:].bitcast(FP8X4),
+                    rhs_scale=warm_scales[:],
+                    start=(i == 0),
+                    stop=(i == passes - 1),
+                )
 
-        def copy_offset(h, bank):
-            dst = off_all[:].bitcast(F32)[:, h * 3 * P : (h + 1) * 3 * P]
-            nc.scalar.copy(
-                out=dst.rearrange("q (p c) -> q p c", c=3),
-                in_=bank[:, 0 : 3 * P].rearrange("q (c p) -> q p c", c=3),
+        def load_offset():
+            src = offset.rearrange("(i c) -> i c", c=48).unsqueeze(0).to_broadcast([4, 32, 48])
+            nc.sync.dma_start(out=off_rows[:], in_=src)
+
+        def turn_offset():
+            words = off_rows[:].bitcast(F32)
+            nc.vector.tensor_copy(out=off_wide[:], in_=words.unsqueeze(2).to_broadcast([P, 24, 32]))
+            nc.vector.transpose(
+                off_turned[:].rearrange("p c i -> p (c i)"), off_wide[:].rearrange("p c j -> p (c j)")
             )
 
-        def order_words(m, h):
-            half = slice(h * NT, (h + 1) * NT)
+        def order_offset():
             nc.vector.tensor_copy(
-                out=d_perm[m][:, half].rearrange("r (g u p) -> r g u p", g=2, u=2),
-                in_=d_raw[m][:].bitcast(F32)[:, half].rearrange("r (g p u) -> r g u p", g=2, u=2),
+                out=off_all[:].bitcast(F32).rearrange("p (i c) -> p i c", c=24),
+                in_=off_turned[:].rearrange("p c i -> p i c"),
+            )
+
+        def sort_d(m, h):
+            d_sorted[m, h] = ring.tile([P, NT], F32, name="d_sorted%d_%d" % (m, h), tag="d_sorted", bufs=4, align_bytes=64)
+            nc.vector.tensor_copy(
+                out=d_sorted[m, h][:].rearrange("r (g u p) -> r g u p", g=2, u=2),
+                in_=d_raw[m][:].bitcast(F32)[:, h * NT : (h + 1) * NT].rearrange("r (g p u) -> r g u p", g=2, u=2),
             )
 
         def transpose_d(m, h):
             bank = next_bank()
             for j in range(4):
-                nc.tensor.transpose(
-                    bank[:, j * P : (j + 1) * P], d_perm[m][:, h * NT + j * P : h * NT + (j + 1) * P], ident[:]
-                )
-            dst = d_grp[m][:].bitcast(F32)[:, h * NT : (h + 1) * NT].rearrange("p (g r u) -> p g r u", g=2, u=2)
-            nc.scalar.copy(out=dst, in_=bank[:].rearrange("p (g u r) -> p g r u", g=2, u=2))
+                nc.tensor.transpose(bank[:, j * P : (j + 1) * P], d_sorted[m, h][:, j * P : (j + 1) * P], ident[:])
+            d_grp[m, h] = ring.tile([P, HALF], BF16, name="d_grp%d_%d" % (m, h), tag="d_grp", bufs=4, align_bytes=64)
+            nc.scalar.copy(
+                out=d_grp[m, h][:].bitcast(F32).rearrange("p (g r u) -> p g r u", g=2, u=2),
+                in_=bank[:].rearrange("p (g u r) -> p g r u", g=2, u=2),
+            )
 
         def quantize_d(m, h):
             nc.vector.quantize_mx(
                 out=d_codes[m][:, 256 * h : 256 * (h + 1)].bitcast(FP8X4),
                 scales=d_scales[m][:, 256 * h : 256 * (h + 1)],
-                in_=d_grp[m][:, 1024 * h : 1024 * (h + 1)],
+                in_=d_grp[m, h][:],
             )
 
-        def new_d_tiles(m):
-            d_perm[m] = ring.tile([P, K // 2], F32, name="d_perm%d" % m, tag="d_perm", bufs=2, align_bytes=64)
-            d_grp[m] = ring.tile([P, K], BF16, name="d_grp%d" % m, tag="d_grp", bufs=2, align_bytes=64)
-
-        def interleave(on_scalar, c, n0, n1):
+        def interleave(engine_copy, c, n0, n1):
             if c not in v_grp:
                 v_grp[c] = ring.tile([P, NT, PACK], BF16, name="v_grp%d" % c, tag="v_grp", bufs=5, align_bytes=64)
-            dst = v_grp[c][:, n0:n1, :].rearrange("p (c i) t -> p c t i", i=4)
-            src = v_raw[c][:, :, n0:n1].rearrange("p t (c i) -> p c t i", i=4)
-            if on_scalar:
-                nc.scalar.copy(out=dst, in_=src)
-            else:
-                nc.vector.tensor_copy(out=dst, in_=src)
+            engine_copy(
+                out=v_grp[c][:, n0:n1, :].rearrange("p (c i) t -> p c t i", i=4),
+                in_=v_raw[c][:, :, n0:n1].rearrange("p t (c i) -> p c t i", i=4),
+            )
 
         def quantize_v(c):
             nc.vector.quantize_mx(
@@ -203,23 +173,6 @@ def tile_ancestry_adjusted_scores_s10_kernel(
                 scales=v_scales[c][:],
                 in_=v_grp[c][:].rearrange("p n t -> p (n t)"),
             )
-
-        def background(items):
-            for kind, c in items:
-                if kind == "q":
-                    quantize_v(c)
-                elif kind == "v":
-                    interleave(False, c, 0, NT)
-                elif kind == "s":
-                    interleave(True, c, 0, NT)
-                elif kind == "v0":
-                    interleave(False, c, 0, NT // 2)
-                elif kind == "v1":
-                    interleave(False, c, NT // 2, NT)
-                elif kind == "s0":
-                    interleave(True, c, 0, NT // 2)
-                else:
-                    interleave(True, c, NT // 2, NT)
 
         def product(m, width, operand):
             bank = next_bank()
@@ -237,16 +190,9 @@ def tile_ancestry_adjusted_scores_s10_kernel(
             return bank[:, 0:width]
 
         def effect_product(nt, m):
-            def operand(g):
-                if nt == 0:
-                    plane = e_scales_first[:, g, :]
-                else:
-                    plane = e_scales_rest[:, g, cols(nt - 1)]
-                return e_words[nt][:, g, :].bitcast(FP4X4), plane
+            return product(m, NT, lambda g: (e_words[nt][:, g, :].bitcast(FP4X4), e_scales[nt][:, g, :]))
 
-            return product(m, NT, operand)
-
-        def keep_raw(nt, m, raw):
+        def park_raw(nt, m, raw):
             nc.scalar.copy(out=acc[nt, m][:], in_=raw)
 
         def ancestry_product(nt, m, n0, n1):
@@ -258,57 +204,110 @@ def tile_ancestry_adjusted_scores_s10_kernel(
             part = acc[nt, m][:, n0:n1]
             nc.vector.tensor_tensor(out=part, in0=part, in1=mean, op=ALU.subtract)
 
-        def spread_product(nt, m, n0, n1):
-            sums = product(
-                m, n1 - n0, lambda g: (v_codes[nt * G + g][:, n0:n1].bitcast(FP8X4), v_scales[nt * G + g][:, n0:n1])
-            )
-            if n0 == 0:
-                expo[nt, m] = ring.tile([P, NT], F32, name="expo%d_%d" % (nt, m), tag="expo", bufs=6)
-            nc.vector.tensor_tensor(
-                out=expo[nt, m][:, n0:n1], in0=sums, in1=off_all[:, nt * NT + n0 : nt * NT + n1], op=ALU.add
-            )
-            nc.scalar.activation(out=expo[nt, m][:, n0:n1], in_=expo[nt, m][:, n0:n1], func=EXP)
+        def spread_product(nt, m):
+            sums = product(m, NT, lambda g: (v_codes[nt * G + g][:].bitcast(FP8X4), v_scales[nt * G + g][:]))
+            expo[nt, m] = ring.tile([P, NT], F32, name="expo%d_%d" % (nt, m), tag="expo", bufs=6)
+            nc.vector.tensor_tensor(out=expo[nt, m][:], in0=sums, in1=off_all[:, cols(nt)], op=ALU.add)
+
+        def exponential(nt, m):
+            nc.scalar.activation(out=expo[nt, m][:], in_=expo[nt, m][:], func=EXP)
 
         def finish(engine, nt, m, n0, n1):
             part = acc[nt, m][:, n0:n1]
             engine.tensor_tensor(out=part, in0=part, in1=expo[nt, m][:, n0:n1], op=ALU.mult)
             nc.sync.dma_start(out=out[m * P : (m + 1) * P, nt * NT + n0 : nt * NT + n1], in_=part)
 
-        new_d_tiles(0)
-        new_d_tiles(1)
+        for m in (0, 1):
+            load_d(m, 0, HALF)
+            load_d(m, HALF, K)
+        clear(warm_in)
+        clear(e_scales[0])
+        nc.vector.quantize_mx(out=warm_codes[:].bitcast(FP8X4), scales=warm_scales[:], in_=warm_in[:])
+        nc.vector.memset(ident[:], 0.0)
+        make_identity(nc, ident[:], nomemset=True)
+        nc.scalar.activation(out=warm_out[:], in_=warm_in[:, 0:1], func=EXP)
+        for plane in (e_scales[1], e_scales[2], a_scales):
+            clear(plane)
+        load_e_scales(0)
+        for g in range(G):
+            load_e(0, g, g + 1)
+        load_d(2, 0, K)
+        load_offset()
+        load_e_scales(1)
+        load_e(1, 0, 2)
+        load_e(1, 2, 4)
+        load_d(3, 0, K)
+
+        warm_up(WARM_FIRST)
         for h in range(2):
-            order_words(0, h)
+            sort_d(0, h)
             transpose_d(0, h)
-        offset_banks = [transpose_offset(h) for h in range(2)]
+        warm_up(WARM_SECOND)
         for h in range(2):
-            order_words(1, h)
+            sort_d(1, h)
             transpose_d(1, h)
         for m in (0, 1):
             for h in range(2):
                 quantize_d(m, h)
-        for h in range(2):
-            copy_offset(h, offset_banks[h])
-        new_d_tiles(2)
-        new_d_tiles(3)
-        order_words(2, 0)
-        order_words(2, 1)
-        keep_raw(0, 0, effect_product(0, 0))
-        order_words(3, 0)
-        order_words(3, 1)
-        raw_held = effect_product(0, 1)
+        load_v(0)
+        load_v(1)
+        load_e_scales(2)
+        load_e(2, 0, G)
+        for c in (2, 3, 4, 5):
+            load_v(c)
+        load_a_scales()
+        load_a(0)
+        for c in (6, 7):
+            load_v(c)
+        load_a(1)
+        for c in (8, 9, 10, 11):
+            load_v(c)
+        load_a(2)
+
         for m in (2, 3):
+            nt = m - 2
+            park_raw(nt, 0, effect_product(nt, 0))
+            for h in range(2):
+                sort_d(m, h)
+            if m == 2:
+                turn_offset()
+            else:
+                order_offset()
+            raw_held = effect_product(nt, 1)
             for h in range(2):
                 transpose_d(m, h)
+            park_raw(nt, 1, raw_held)
+            if m == 3:
+                interleave(nc.vector.tensor_copy, 0, 0, NT)
+            for h in range(2):
                 quantize_d(m, h)
-        keep_raw(0, 1, raw_held)
-        beside_effect = {
-            (0, 3): [("v", 0), ("v", 1), ("q", 0), ("v", 2), ("q", 1), ("v", 3), ("q", 2), ("q", 3)],
-            (2, 2): [("s0", 5)],
-            (2, 3): [("s1", 5)],
-        }
-        for nt, m in [(0, 2), (0, 3)] + [(nt, m) for nt in (1, 2) for m in range(MT)]:
-            keep_raw(nt, m, effect_product(nt, m))
-            background(beside_effect.get((nt, m), []))
+        vec, sca = nc.vector.tensor_copy, nc.scalar.copy
+        last = (NTILES - 1, MT - 1)
+        rest = [(0, 2), (1, 2), (0, 3), (1, 3)] + [(2, m) for m in range(MT)]
+        quantize_v(0)
+        interleave(vec, 1, 0, NT)
+        for i, (nt, m) in enumerate(rest):
+            park_raw(nt, m, effect_product(nt, m))
+            if (nt, m) == (2, 0):
+                interleave(sca, 3, 0, 192)
+            if (nt, m) == (2, 2):
+                interleave(sca, 5, 0, 256)
+            if (nt, m) == (2, 3):
+                interleave(sca, 5, 256, NT)
+        quantize_v(1)
+        interleave(vec, 2, 0, NT)
+        interleave(vec, 3, 192, NT)
+        quantize_v(2)
+        quantize_v(3)
+
+        def background(items):
+            for kind, c in items:
+                if kind == "q":
+                    quantize_v(c)
+                else:
+                    n0 = NT // 2 if kind[1:] == "1" else 0
+                    n1 = NT // 2 if kind[1:] == "0" else NT
+                    interleave(vec if kind[0] == "v" else sca, c, n0, n1)
 
         steps = [("V", 0, m) for m in range(MT)] + [("A", 0, m) for m in range(MT)]
         steps += [("A", 1, m) for m in range(MT)] + [("V", 1, m) for m in range(MT)]
@@ -330,13 +329,13 @@ def tile_ancestry_adjusted_scores_s10_kernel(
             if kind == "A":
                 ancestry_product(nt, m, 0, NT)
             else:
-                spread_product(nt, m, 0, NT)
+                spread_product(nt, m)
+                exponential(nt, m)
             for done in ready:
                 finish(nc.gpsimd if done != (2, 1) else nc.vector, done[0], done[1], 0, NT)
             ready = [(nt, m)] if (nt, m) in seen else []
             seen.add((nt, m))
             background(beside.get(step, []))
-        last = (NTILES - 1, MT - 1)
         ancestry_product(*last, 0, NT // 2)
         ancestry_product(*last, NT // 2, NT)
         finish(nc.vector, *last, 0, NT // 2)

@@ -54,9 +54,9 @@ def tile_ancestry_adjusted_scores_s10_kernel(
             return slice(nt * NT, (nt + 1) * NT)
 
         ident = kept("ident", [P, P], F32)
-        off_rows = kept("off_rows", [P, 48], BF16)
-        off_wide = kept("off_wide", [P, 24, 32], F32)
-        off_turned = kept("off_turned", [P, 24, 32], F32)
+        off_row = kept("off_row", [P, N], BF16)
+        off_cols = kept("off_cols", [P, N // 64, 32], F32)
+        off_wide = kept("off_wide", [P, N // 64, 32], F32)
         off_all = kept("off_all", [P, N], BF16)
         warm_in = kept("warm_in", [P, 2 * NT], BF16)
         warm_out = kept("warm_out", [P, 1], F32)
@@ -66,7 +66,8 @@ def tile_ancestry_adjusted_scores_s10_kernel(
         d_codes = [kept("d_codes%d" % m, [P, G * P], U32) for m in range(MT)]
         d_scales = [kept("d_scales%d" % m, [P, G * P], U8) for m in range(MT)]
         e_words = [kept("e_words%d" % nt, [P, G, 2 * NT], U8) for nt in range(NTILES)]
-        e_scales = [kept("e_scales%d" % nt, [P, G, NT], U8) for nt in range(NTILES)]
+        e_scales_first = kept("e_scales_first", [P, G, NT], U8)
+        e_scales_rest = kept("e_scales_rest", [P, G, N - NT], U8)
         a_words = [kept("a_words%d" % nt, [P, G, NT], U32) for nt in range(NTILES)]
         a_scales = kept("a_scales", [P, N], U8)
         chunks = [(nt, g) for nt in range(NTILES) for g in range(G)]
@@ -83,10 +84,10 @@ def tile_ancestry_adjusted_scores_s10_kernel(
             src = effect_words[g0:g1, :, 2 * nt * NT : 2 * (nt + 1) * NT].rearrange("g p b -> p g b")
             nc.sync.dma_start(out=e_words[nt][:, g0:g1, :].bitcast(I32), in_=src.bitcast(I32))
 
-        def load_e_scales(nt):
+        def load_e_scales(plane, n0, n1):
             for r in range(4):
-                src = effect_scales[:, r:16:4, cols(nt)].rearrange("g q n -> q g n")
-                nc.sync.dma_start(out=e_scales[nt][r:P:32, :, :].bitcast(I32), in_=src.bitcast(I32))
+                src = effect_scales[:, r:16:4, n0:n1].rearrange("g q n -> q g n")
+                nc.sync.dma_start(out=plane[r:P:32, :, :].bitcast(I32), in_=src.bitcast(I32))
 
         def load_a(nt):
             src = ancestry_words[:, :, cols(nt), :].rearrange("g p n t -> p g (n t)")
@@ -119,44 +120,39 @@ def tile_ancestry_adjusted_scores_s10_kernel(
                 )
 
         def load_offset():
-            src = offset.rearrange("(i c) -> i c", c=48).unsqueeze(0).to_broadcast([4, 32, 48])
-            nc.sync.dma_start(out=off_rows[:], in_=src)
+            nc.sync.dma_start(out=off_row[0:P:32, :], in_=offset.partition_broadcast(4))
 
-        def turn_offset():
-            words = off_rows[:].bitcast(F32)
-            nc.vector.tensor_copy(out=off_wide[:], in_=words.unsqueeze(2).to_broadcast([P, 24, 32]))
-            nc.vector.transpose(
-                off_turned[:].rearrange("p c i -> p (c i)"), off_wide[:].rearrange("p c j -> p (c j)")
-            )
+        def offset_to_partitions():
+            nc.vector.transpose(off_cols[:].rearrange("p b i -> p (b i)"), off_row[:].bitcast(F32))
 
-        def order_offset():
+        def offset_repeat():
+            nc.vector.tensor_copy(out=off_wide[:], in_=off_cols[:, :, 0:1].to_broadcast([P, N // 64, 32]))
+
+        def offset_to_rows():
+            nc.vector.transpose(off_all[:].bitcast(F32), off_wide[:].rearrange("p b i -> p (b i)"))
+
+        def sort_d(m, g):
+            d_sorted[m, g] = ring.tile([P, 2, P], F32, name="d_sorted%d_%d" % (m, g), tag="d_sorted", bufs=8, align_bytes=64)
             nc.vector.tensor_copy(
-                out=off_all[:].bitcast(F32).rearrange("p (i c) -> p i c", c=24),
-                in_=off_turned[:].rearrange("p c i -> p i c"),
+                out=d_sorted[m, g][:],
+                in_=d_raw[m][:].bitcast(F32)[:, 2 * P * g : 2 * P * (g + 1)].rearrange("r (p u) -> r u p", u=2),
             )
 
-        def sort_d(m, h):
-            d_sorted[m, h] = ring.tile([P, NT], F32, name="d_sorted%d_%d" % (m, h), tag="d_sorted", bufs=4, align_bytes=64)
-            nc.vector.tensor_copy(
-                out=d_sorted[m, h][:].rearrange("r (g u p) -> r g u p", g=2, u=2),
-                in_=d_raw[m][:].bitcast(F32)[:, h * NT : (h + 1) * NT].rearrange("r (g p u) -> r g u p", g=2, u=2),
-            )
-
-        def transpose_d(m, h):
+        def transpose_d(m, g):
             bank = next_bank()
-            for j in range(4):
-                nc.tensor.transpose(bank[:, j * P : (j + 1) * P], d_sorted[m, h][:, j * P : (j + 1) * P], ident[:])
-            d_grp[m, h] = ring.tile([P, HALF], BF16, name="d_grp%d_%d" % (m, h), tag="d_grp", bufs=4, align_bytes=64)
+            for u in range(2):
+                nc.tensor.transpose(bank[:, u * P : (u + 1) * P], d_sorted[m, g][:, u, :], ident[:])
+            d_grp[m, g] = ring.tile([P, KP], BF16, name="d_grp%d_%d" % (m, g), tag="d_grp", bufs=8, align_bytes=64)
             nc.scalar.copy(
-                out=d_grp[m, h][:].bitcast(F32).rearrange("p (g r u) -> p g r u", g=2, u=2),
-                in_=bank[:].rearrange("p (g u r) -> p g r u", g=2, u=2),
+                out=d_grp[m, g][:].bitcast(F32).rearrange("p (r u) -> p r u", u=2),
+                in_=bank[:, 0 : 2 * P].rearrange("p (u r) -> p r u", u=2),
             )
 
-        def quantize_d(m, h):
+        def quantize_d(m, g):
             nc.vector.quantize_mx(
-                out=d_codes[m][:, 256 * h : 256 * (h + 1)].bitcast(FP8X4),
-                scales=d_scales[m][:, 256 * h : 256 * (h + 1)],
-                in_=d_grp[m, h][:],
+                out=d_codes[m][:, g * P : (g + 1) * P].bitcast(FP8X4),
+                scales=d_scales[m][:, g * P : (g + 1) * P],
+                in_=d_grp[m, g][:],
             )
 
         def interleave(engine_copy, c, n0, n1):
@@ -190,7 +186,8 @@ def tile_ancestry_adjusted_scores_s10_kernel(
             return bank[:, 0:width]
 
         def effect_product(nt, m):
-            return product(m, NT, lambda g: (e_words[nt][:, g, :].bitcast(FP4X4), e_scales[nt][:, g, :]))
+            plane = e_scales_first[:] if nt == 0 else e_scales_rest[:, :, cols(nt - 1)]
+            return product(m, NT, lambda g: (e_words[nt][:, g, :].bitcast(FP4X4), plane[:, g, :]))
 
         def park_raw(nt, m, raw):
             nc.scalar.copy(out=acc[nt, m][:], in_=raw)
@@ -204,13 +201,15 @@ def tile_ancestry_adjusted_scores_s10_kernel(
             part = acc[nt, m][:, n0:n1]
             nc.vector.tensor_tensor(out=part, in0=part, in1=mean, op=ALU.subtract)
 
-        def spread_product(nt, m):
+        def spread_product(nt, m, parts):
             sums = product(m, NT, lambda g: (v_codes[nt * G + g][:].bitcast(FP8X4), v_scales[nt * G + g][:]))
             expo[nt, m] = ring.tile([P, NT], F32, name="expo%d_%d" % (nt, m), tag="expo", bufs=6)
-            nc.vector.tensor_tensor(out=expo[nt, m][:], in0=sums, in1=off_all[:, cols(nt)], op=ALU.add)
-
-        def exponential(nt, m):
-            nc.scalar.activation(out=expo[nt, m][:], in_=expo[nt, m][:], func=EXP)
+            for n0, n1 in parts:
+                part = expo[nt, m][:, n0:n1]
+                nc.vector.tensor_tensor(
+                    out=part, in0=sums[:, n0:n1], in1=off_all[:, nt * NT + n0 : nt * NT + n1], op=ALU.add
+                )
+                nc.scalar.activation(out=part, in_=part, func=EXP)
 
         def finish(engine, nt, m, n0, n1):
             part = acc[nt, m][:, n0:n1]
@@ -221,37 +220,23 @@ def tile_ancestry_adjusted_scores_s10_kernel(
             load_d(m, 0, HALF)
             load_d(m, HALF, K)
         clear(warm_in)
-        clear(e_scales[0])
+        clear(e_scales_first)
         nc.vector.quantize_mx(out=warm_codes[:].bitcast(FP8X4), scales=warm_scales[:], in_=warm_in[:])
         nc.vector.memset(ident[:], 0.0)
         make_identity(nc, ident[:], nomemset=True)
         nc.scalar.activation(out=warm_out[:], in_=warm_in[:, 0:1], func=EXP)
-        for plane in (e_scales[1], e_scales[2], a_scales):
+        for plane in (e_scales_rest, a_scales, off_row):
             clear(plane)
-        load_e_scales(0)
-        for g in range(G):
-            load_e(0, g, g + 1)
+        load_e_scales(e_scales_first, 0, NT)
+        load_e(0, 0, 2)
+        load_e(0, 2, 4)
         load_d(2, 0, K)
-        load_offset()
-        load_e_scales(1)
-        load_e(1, 0, 2)
-        load_e(1, 2, 4)
         load_d(3, 0, K)
-
-        warm_up(WARM_FIRST)
-        for h in range(2):
-            sort_d(0, h)
-            transpose_d(0, h)
-        warm_up(WARM_SECOND)
-        for h in range(2):
-            sort_d(1, h)
-            transpose_d(1, h)
-        for m in (0, 1):
-            for h in range(2):
-                quantize_d(m, h)
+        load_offset()
+        load_e_scales(e_scales_rest, NT, N)
+        load_e(1, 0, G)
         load_v(0)
         load_v(1)
-        load_e_scales(2)
         load_e(2, 0, G)
         for c in (2, 3, 4, 5):
             load_v(c)
@@ -264,28 +249,36 @@ def tile_ancestry_adjusted_scores_s10_kernel(
             load_v(c)
         load_a(2)
 
+        warm_up(WARM_FIRST)
+        for g in range(G):
+            sort_d(0, g)
+            transpose_d(0, g)
+        warm_up(WARM_SECOND)
+        for g in range(G):
+            sort_d(1, g)
+            transpose_d(1, g)
+        for m in (0, 1):
+            for g in range(G):
+                quantize_d(m, g)
+
+        park_raw(0, 0, effect_product(0, 0))
+        park_raw(0, 1, effect_product(0, 1))
         for m in (2, 3):
-            nt = m - 2
-            park_raw(nt, 0, effect_product(nt, 0))
-            for h in range(2):
-                sort_d(m, h)
-            if m == 2:
-                turn_offset()
-            else:
-                order_offset()
-            raw_held = effect_product(nt, 1)
-            for h in range(2):
-                transpose_d(m, h)
-            park_raw(nt, 1, raw_held)
-            if m == 3:
-                interleave(nc.vector.tensor_copy, 0, 0, NT)
-            for h in range(2):
-                quantize_d(m, h)
+            for g in range(G):
+                sort_d(m, g)
+        for m in (2, 3):
+            for g in range(G):
+                transpose_d(m, g)
+                quantize_d(m, g)
+        offset_to_partitions()
+        offset_repeat()
         vec, sca = nc.vector.tensor_copy, nc.scalar.copy
         last = (NTILES - 1, MT - 1)
-        rest = [(0, 2), (1, 2), (0, 3), (1, 3)] + [(2, m) for m in range(MT)]
-        quantize_v(0)
+        rest = [(0, 2), (0, 3)] + [(nt, m) for nt in (1, 2) for m in range(MT)]
+        interleave(vec, 0, 0, NT)
+        offset_to_rows()
         interleave(vec, 1, 0, NT)
+        quantize_v(0)
         for i, (nt, m) in enumerate(rest):
             park_raw(nt, m, effect_product(nt, m))
             if (nt, m) == (2, 0):
@@ -329,8 +322,7 @@ def tile_ancestry_adjusted_scores_s10_kernel(
             if kind == "A":
                 ancestry_product(nt, m, 0, NT)
             else:
-                spread_product(nt, m)
-                exponential(nt, m)
+                spread_product(nt, m, [(0, NT)])
             for done in ready:
                 finish(nc.gpsimd if done != (2, 1) else nc.vector, done[0], done[1], 0, NT)
             ready = [(nt, m)] if (nt, m) in seen else []

@@ -25,7 +25,6 @@ MT = M // P
 NTILES = N // NT
 BANKS = 8
 HALF = K // 2
-SCALAR_COLS = 0
 WARM_FIRST = 6
 WARM_SECOND = 4
 
@@ -43,6 +42,9 @@ def tile_ancestry_adjusted_scores_s10_kernel(
         def kept(name, shape, dtype):
             return keep.tile(shape, dtype, name=name, align_bytes=64)
 
+        def staged(name, shape, dtype):
+            return ring.tile(shape, dtype, name=name, tag="staged", bufs=6, align_bytes=64)
+
         banks_taken = []
 
         def next_bank():
@@ -54,9 +56,9 @@ def tile_ancestry_adjusted_scores_s10_kernel(
             return slice(nt * NT, (nt + 1) * NT)
 
         ident = kept("ident", [P, P], F32)
-        off_row = kept("off_row", [P, N], BF16)
-        off_cols = kept("off_cols", [P, N // 64, 32], F32)
-        off_wide = kept("off_wide", [P, N // 64, 32], F32)
+        off_row = staged("off_row", [P, N], BF16)
+        off_cols = staged("off_cols", [P, N // 64, 32], F32)
+        off_wide = staged("off_wide", [P, N // 64, 32], F32)
         off_all = kept("off_all", [P, N], BF16)
         warm_in = kept("warm_in", [P, 2 * NT], BF16)
         warm_out = kept("warm_out", [P, 1], F32)
@@ -75,7 +77,7 @@ def tile_ancestry_adjusted_scores_s10_kernel(
         v_codes = [kept("v_codes%d" % c, [P, NT], U32) for c in range(len(chunks))]
         v_scales = [kept("v_scales%d" % c, [P, NT], U8) for c in range(len(chunks))]
         acc = {(nt, m): kept("acc%d_%d" % (nt, m), [P, NT], F32) for nt in range(NTILES) for m in range(MT)}
-        d_sorted, d_banks, d_grp, v_grp, expo = {}, {}, {}, {}, {}
+        d_sorted, d_grp, v_grp, expo = {}, {}, {}, {}
 
         def load_d(m, k0, k1):
             nc.sync.dma_start(out=d_raw[m][:, k0:k1], in_=dosage[m * P : (m + 1) * P, k0:k1])
@@ -157,7 +159,7 @@ def tile_ancestry_adjusted_scores_s10_kernel(
 
         def interleave(engine_copy, c, n0, n1):
             if c not in v_grp:
-                v_grp[c] = ring.tile([P, NT, PACK], BF16, name="v_grp%d" % c, tag="v_grp", bufs=5, align_bytes=64)
+                v_grp[c] = staged("v_grp%d" % c, [P, NT, PACK], BF16)
             engine_copy(
                 out=v_grp[c][:, n0:n1, :].rearrange("p (c i) t -> p c t i", i=4),
                 in_=v_raw[c][:, :, n0:n1].rearrange("p t (c i) -> p c t i", i=4),
@@ -203,13 +205,16 @@ def tile_ancestry_adjusted_scores_s10_kernel(
 
         def spread_product(nt, m, parts):
             sums = product(m, NT, lambda g: (v_codes[nt * G + g][:].bitcast(FP8X4), v_scales[nt * G + g][:]))
-            expo[nt, m] = ring.tile([P, NT], F32, name="expo%d_%d" % (nt, m), tag="expo", bufs=6)
+            expo[nt, m] = ring.tile([P, NT], F32, name="expo%d_%d" % (nt, m), tag="expo", bufs=8)
             for n0, n1 in parts:
                 part = expo[nt, m][:, n0:n1]
                 nc.vector.tensor_tensor(
                     out=part, in0=sums[:, n0:n1], in1=off_all[:, nt * NT + n0 : nt * NT + n1], op=ALU.add
                 )
-                nc.scalar.activation(out=part, in_=part, func=EXP)
+
+        def exponential(nt, m, n0, n1):
+            part = expo[nt, m][:, n0:n1]
+            nc.scalar.activation(out=part, in_=part, func=EXP)
 
         def finish(engine, nt, m, n0, n1):
             part = acc[nt, m][:, n0:n1]
@@ -231,23 +236,21 @@ def tile_ancestry_adjusted_scores_s10_kernel(
         load_e(0, 0, 2)
         load_e(0, 2, 4)
         load_d(2, 0, K)
-        load_d(3, 0, K)
+        load_d(3, 0, HALF)
+        load_d(3, HALF, K)
         load_offset()
         load_e_scales(e_scales_rest, NT, N)
         load_e(1, 0, G)
         load_v(0)
         load_v(1)
         load_e(2, 0, G)
-        for c in (2, 3, 4, 5):
+        for c in range(2, 6):
             load_v(c)
         load_a_scales()
-        load_a(0)
-        for c in (6, 7):
-            load_v(c)
-        load_a(1)
-        for c in (8, 9, 10, 11):
-            load_v(c)
-        load_a(2)
+        for nt in range(NTILES):
+            load_a(nt)
+            for c in range(6 + 3 * nt, min(9 + 3 * nt, len(chunks))):
+                load_v(c)
 
         warm_up(WARM_FIRST)
         for g in range(G):
@@ -272,63 +275,58 @@ def tile_ancestry_adjusted_scores_s10_kernel(
                 quantize_d(m, g)
         offset_to_partitions()
         offset_repeat()
-        vec, sca = nc.vector.tensor_copy, nc.scalar.copy
-        last = (NTILES - 1, MT - 1)
-        rest = [(0, 2), (0, 3)] + [(nt, m) for nt in (1, 2) for m in range(MT)]
-        interleave(vec, 0, 0, NT)
+        on_vector, on_scalar = nc.vector.tensor_copy, nc.scalar.copy
+        whole = (0, NT)
+        low, high = (0, NT // 2), (NT // 2, NT)
+
+        interleave(on_vector, 0, *whole)
         offset_to_rows()
-        interleave(vec, 1, 0, NT)
         quantize_v(0)
-        for i, (nt, m) in enumerate(rest):
+        interleave(on_vector, 1, *whole)
+        scalar_half_after = {(1, 3): (2, low), (2, 0): (3, low), (2, 2): (5, low), (2, 3): (5, high)}
+        for nt, m in [(0, 2), (0, 3)] + [(nt, m) for nt in (1, 2) for m in range(MT)]:
             park_raw(nt, m, effect_product(nt, m))
-            if (nt, m) == (2, 0):
-                interleave(sca, 3, 0, 192)
-            if (nt, m) == (2, 2):
-                interleave(sca, 5, 0, 256)
-            if (nt, m) == (2, 3):
-                interleave(sca, 5, 256, NT)
+            if (nt, m) in scalar_half_after:
+                c, half = scalar_half_after[nt, m]
+                interleave(on_scalar, c, *half)
         quantize_v(1)
-        interleave(vec, 2, 0, NT)
-        interleave(vec, 3, 192, NT)
+        interleave(on_vector, 2, *high)
+        interleave(on_vector, 3, *high)
         quantize_v(2)
         quantize_v(3)
+        interleave(on_vector, 4, *whole)
 
-        def background(items):
-            for kind, c in items:
-                if kind == "q":
-                    quantize_v(c)
-                else:
-                    n0 = NT // 2 if kind[1:] == "1" else 0
-                    n1 = NT // 2 if kind[1:] == "0" else NT
-                    interleave(vec if kind[0] == "v" else sca, c, n0, n1)
+        for nt in range(NTILES - 1):
+            first = (nt + 1) * G
+            for m in range(MT):
+                spread_product(nt, m, [whole])
+            for c in (first, first + 1):
+                quantize_v(c)
+                interleave(on_scalar, c + 2, *low)
+                interleave(on_vector, c + 2, *high)
+            for m in range(MT):
+                exponential(nt, m, *whole)
+            for c in (first + 2, first + 3):
+                quantize_v(c)
+            for c in range(first + G, min(first + G + 2, len(chunks))):
+                interleave(on_scalar, c, *whole)
+            for m in range(MT):
+                ancestry_product(nt, m, *whole)
+                finish(nc.gpsimd, nt, m, *whole)
 
-        steps = [("V", 0, m) for m in range(MT)] + [("A", 0, m) for m in range(MT)]
-        steps += [("A", 1, m) for m in range(MT)] + [("V", 1, m) for m in range(MT)]
-        steps += [("A", 2, 0), ("A", 2, 1), ("A", 2, 2), ("V", 2, 0), ("V", 2, 1), ("V", 2, 2), ("V", 2, 3)]
-        beside = {
-            ("V", 0, 0): [("v", 4)],
-            ("V", 0, 1): [("q", 4), ("s0", 6)],
-            ("V", 0, 2): [("q", 5)],
-            ("V", 0, 3): [("s1", 6), ("s", 7), ("s", 8), ("s", 9)],
-            ("A", 1, 1): [("q", 6), ("q", 7)],
-            ("A", 1, 2): [("q", 8), ("s0", 10), ("s0", 11)],
-            ("A", 1, 3): [("v1", 10), ("v1", 11), ("q", 9)],
-            ("V", 1, 0): [("q", 10), ("q", 11)],
-        }
-        seen = set()
-        ready = []
-        for step in steps:
-            kind, nt, m = step
-            if kind == "A":
-                ancestry_product(nt, m, 0, NT)
-            else:
-                spread_product(nt, m, [(0, NT)])
-            for done in ready:
-                finish(nc.gpsimd if done != (2, 1) else nc.vector, done[0], done[1], 0, NT)
-            ready = [(nt, m)] if (nt, m) in seen else []
-            seen.add((nt, m))
-            background(beside.get(step, []))
-        ancestry_product(*last, 0, NT // 2)
-        ancestry_product(*last, NT // 2, NT)
-        finish(nc.vector, *last, 0, NT // 2)
-        finish(nc.vector, *last, NT // 2, NT)
+        nt = NTILES - 1
+        for m in range(MT - 1):
+            spread_product(nt, m, [whole])
+            exponential(nt, m, *whole)
+        for m in range(MT - 1):
+            ancestry_product(nt, m, *whole)
+            if m > 0:
+                finish(nc.vector, nt, m - 1, *whole)
+        finish(nc.vector, nt, MT - 2, *whole)
+        spread_product(nt, MT - 1, [low, high])
+        for half in (low, high):
+            exponential(nt, MT - 1, *half)
+        for piece in (low, (256, 384), (384, NT)):
+            ancestry_product(nt, MT - 1, *piece)
+        for half in (low, high):
+            finish(nc.vector, nt, MT - 1, *half)

@@ -24,9 +24,8 @@ NT = 512
 MT = M // P
 NTILES = N // NT
 BANKS = 8
-HALF = K // 2
-WARM_FIRST = 6
-WARM_SECOND = 4
+WARM_N = 256
+WARM_PASSES = (6, 4)
 
 
 def tile_ancestry_adjusted_scores_s10_kernel(
@@ -42,9 +41,6 @@ def tile_ancestry_adjusted_scores_s10_kernel(
         def kept(name, shape, dtype):
             return keep.tile(shape, dtype, name=name, align_bytes=64)
 
-        def staged(name, shape, dtype):
-            return ring.tile(shape, dtype, name=name, tag="staged", bufs=6, align_bytes=64)
-
         banks_taken = []
 
         def next_bank():
@@ -55,15 +51,14 @@ def tile_ancestry_adjusted_scores_s10_kernel(
         def cols(nt):
             return slice(nt * NT, (nt + 1) * NT)
 
+        chunks = [(nt, g) for nt in range(NTILES) for g in range(G)]
         ident = kept("ident", [P, P], F32)
-        off_row = staged("off_row", [P, N], BF16)
-        off_cols = staged("off_cols", [P, N // 64, 32], F32)
-        off_wide = staged("off_wide", [P, N // 64, 32], F32)
-        off_all = kept("off_all", [P, N], BF16)
-        warm_in = kept("warm_in", [P, 2 * NT], BF16)
+        warm_in = kept("warm_in", [P, PACK * WARM_N], BF16)
         warm_out = kept("warm_out", [P, 1], F32)
-        warm_codes = kept("warm_codes", [P, 256], U32)
-        warm_scales = kept("warm_scales", [P, 256], U8)
+        warm_codes = kept("warm_codes", [P, WARM_N], U32)
+        warm_scales = kept("warm_scales", [P, WARM_N], U8)
+        off_rows = kept("off_rows", [P, 2, 16], BF16)
+        off_all = kept("off_all", [P, N], BF16)
         d_raw = [kept("d_raw%d" % m, [P, K], BF16) for m in range(MT)]
         d_codes = [kept("d_codes%d" % m, [P, G * P], U32) for m in range(MT)]
         d_scales = [kept("d_scales%d" % m, [P, G * P], U8) for m in range(MT)]
@@ -72,7 +67,6 @@ def tile_ancestry_adjusted_scores_s10_kernel(
         e_scales_rest = kept("e_scales_rest", [P, G, N - NT], U8)
         a_words = [kept("a_words%d" % nt, [P, G, NT], U32) for nt in range(NTILES)]
         a_scales = kept("a_scales", [P, N], U8)
-        chunks = [(nt, g) for nt in range(NTILES) for g in range(G)]
         v_raw = [kept("v_raw%d" % c, [P, PACK, NT], BF16) for c in range(len(chunks))]
         v_codes = [kept("v_codes%d" % c, [P, NT], U32) for c in range(len(chunks))]
         v_scales = [kept("v_scales%d" % c, [P, NT], U8) for c in range(len(chunks))]
@@ -82,9 +76,17 @@ def tile_ancestry_adjusted_scores_s10_kernel(
         def load_d(m, k0, k1):
             nc.sync.dma_start(out=d_raw[m][:, k0:k1], in_=dosage[m * P : (m + 1) * P, k0:k1])
 
+        def load_d_halves(m):
+            load_d(m, 0, K // 2)
+            load_d(m, K // 2, K)
+
         def load_e(nt, g0, g1):
             src = effect_words[g0:g1, :, 2 * nt * NT : 2 * (nt + 1) * NT].rearrange("g p b -> p g b")
             nc.sync.dma_start(out=e_words[nt][:, g0:g1, :].bitcast(I32), in_=src.bitcast(I32))
+
+        def load_e_halves(nt):
+            load_e(nt, 0, G // 2)
+            load_e(nt, G // 2, G)
 
         def load_e_scales(plane, n0, n1):
             for r in range(4):
@@ -105,14 +107,17 @@ def tile_ancestry_adjusted_scores_s10_kernel(
             src = spread[g * KP : (g + 1) * KP, cols(nt)].rearrange("(p j) n -> p j n", j=PACK)
             nc.sync.dma_start(out=v_raw[c][:], in_=src)
 
-        def clear(plane):
-            nc.vector.memset(plane[:].bitcast(I32), 0)
+        def load_offset():
+            nc.sync.dma_start(out=off_rows[:, :, 0:6], in_=offset.rearrange("(h p c) -> p h c", h=2, p=P))
+
+        def clear(tile):
+            nc.vector.memset(tile[:].bitcast(I32), 0)
 
         def warm_up(passes):
             bank = next_bank()
             for i in range(passes):
                 nc.tensor.matmul_mx(
-                    out=bank[:, 0:256],
+                    out=bank[:, 0:WARM_N],
                     lhsT=warm_codes[:, 0:P].bitcast(FP8X4),
                     lhsT_scale=warm_scales[:, 0:P],
                     rhs=warm_codes[:].bitcast(FP8X4),
@@ -121,20 +126,21 @@ def tile_ancestry_adjusted_scores_s10_kernel(
                     stop=(i == passes - 1),
                 )
 
-        def load_offset():
-            nc.sync.dma_start(out=off_row[0:P:32, :], in_=offset.partition_broadcast(4))
-
-        def offset_to_partitions():
-            nc.vector.transpose(off_cols[:].rearrange("p b i -> p (b i)"), off_row[:].bitcast(F32))
-
-        def offset_repeat():
-            nc.vector.tensor_copy(out=off_wide[:], in_=off_cols[:, :, 0:1].to_broadcast([P, N // 64, 32]))
-
-        def offset_to_rows():
-            nc.vector.transpose(off_all[:].bitcast(F32), off_wide[:].rearrange("p b i -> p (b i)"))
+        def spread_offset(h):
+            bank = next_bank()
+            words = off_rows[:, h, 0:6].bitcast(F32)
+            for c in range(3):
+                nc.tensor.transpose(bank[:, c * P : (c + 1) * P], words[:, c : c + 1].to_broadcast([P, P]), ident[:])
+            dst = off_all[:].bitcast(F32)[:, h * 3 * P : (h + 1) * 3 * P]
+            nc.scalar.copy(
+                out=dst.rearrange("q (p c) -> q p c", c=3),
+                in_=bank[:, 0 : 3 * P].rearrange("q (c p) -> q p c", c=3),
+            )
 
         def sort_d(m, g):
-            d_sorted[m, g] = ring.tile([P, 2, P], F32, name="d_sorted%d_%d" % (m, g), tag="d_sorted", bufs=8, align_bytes=64)
+            d_sorted[m, g] = ring.tile(
+                [P, 2, P], F32, name="d_sorted%d_%d" % (m, g), tag="d_sorted", bufs=2 * G, align_bytes=64
+            )
             nc.vector.tensor_copy(
                 out=d_sorted[m, g][:],
                 in_=d_raw[m][:].bitcast(F32)[:, 2 * P * g : 2 * P * (g + 1)].rearrange("r (p u) -> r u p", u=2),
@@ -144,7 +150,9 @@ def tile_ancestry_adjusted_scores_s10_kernel(
             bank = next_bank()
             for u in range(2):
                 nc.tensor.transpose(bank[:, u * P : (u + 1) * P], d_sorted[m, g][:, u, :], ident[:])
-            d_grp[m, g] = ring.tile([P, KP], BF16, name="d_grp%d_%d" % (m, g), tag="d_grp", bufs=8, align_bytes=64)
+            d_grp[m, g] = ring.tile(
+                [P, KP], BF16, name="d_grp%d_%d" % (m, g), tag="d_grp", bufs=2 * G, align_bytes=64
+            )
             nc.scalar.copy(
                 out=d_grp[m, g][:].bitcast(F32).rearrange("p (r u) -> p r u", u=2),
                 in_=bank[:, 0 : 2 * P].rearrange("p (u r) -> p r u", u=2),
@@ -159,7 +167,9 @@ def tile_ancestry_adjusted_scores_s10_kernel(
 
         def interleave(engine_copy, c, n0, n1):
             if c not in v_grp:
-                v_grp[c] = staged("v_grp%d" % c, [P, NT, PACK], BF16)
+                v_grp[c] = ring.tile(
+                    [P, NT, PACK], BF16, name="v_grp%d" % c, tag="v_grp", bufs=G + 2, align_bytes=64
+                )
             engine_copy(
                 out=v_grp[c][:, n0:n1, :].rearrange("p (c i) t -> p c t i", i=4),
                 in_=v_raw[c][:, :, n0:n1].rearrange("p t (c i) -> p c t i", i=4),
@@ -189,9 +199,7 @@ def tile_ancestry_adjusted_scores_s10_kernel(
 
         def effect_product(nt, m):
             plane = e_scales_first[:] if nt == 0 else e_scales_rest[:, :, cols(nt - 1)]
-            return product(m, NT, lambda g: (e_words[nt][:, g, :].bitcast(FP4X4), plane[:, g, :]))
-
-        def park_raw(nt, m, raw):
+            raw = product(m, NT, lambda g: (e_words[nt][:, g, :].bitcast(FP4X4), plane[:, g, :]))
             nc.scalar.copy(out=acc[nt, m][:], in_=raw)
 
         def ancestry_product(nt, m, n0, n1):
@@ -205,11 +213,13 @@ def tile_ancestry_adjusted_scores_s10_kernel(
 
         def spread_product(nt, m, parts):
             sums = product(m, NT, lambda g: (v_codes[nt * G + g][:].bitcast(FP8X4), v_scales[nt * G + g][:]))
-            expo[nt, m] = ring.tile([P, NT], F32, name="expo%d_%d" % (nt, m), tag="expo", bufs=8)
+            expo[nt, m] = ring.tile([P, NT], F32, name="expo%d_%d" % (nt, m), tag="expo", bufs=2 * MT)
             for n0, n1 in parts:
-                part = expo[nt, m][:, n0:n1]
                 nc.vector.tensor_tensor(
-                    out=part, in0=sums[:, n0:n1], in1=off_all[:, nt * NT + n0 : nt * NT + n1], op=ALU.add
+                    out=expo[nt, m][:, n0:n1],
+                    in0=sums[:, n0:n1],
+                    in1=off_all[:, nt * NT + n0 : nt * NT + n1],
+                    op=ALU.add,
                 )
 
         def exponential(nt, m, n0, n1):
@@ -221,51 +231,44 @@ def tile_ancestry_adjusted_scores_s10_kernel(
             engine.tensor_tensor(out=part, in0=part, in1=expo[nt, m][:, n0:n1], op=ALU.mult)
             nc.sync.dma_start(out=out[m * P : (m + 1) * P, nt * NT + n0 : nt * NT + n1], in_=part)
 
-        for m in (0, 1):
-            load_d(m, 0, HALF)
-            load_d(m, HALF, K)
+        load_d_halves(0)
+        load_d_halves(1)
         clear(warm_in)
         clear(e_scales_first)
         nc.vector.quantize_mx(out=warm_codes[:].bitcast(FP8X4), scales=warm_scales[:], in_=warm_in[:])
         nc.vector.memset(ident[:], 0.0)
         make_identity(nc, ident[:], nomemset=True)
         nc.scalar.activation(out=warm_out[:], in_=warm_in[:, 0:1], func=EXP)
-        for plane in (e_scales_rest, a_scales, off_row):
-            clear(plane)
+        clear(e_scales_rest)
+        clear(a_scales)
         load_e_scales(e_scales_first, 0, NT)
-        load_e(0, 0, 2)
-        load_e(0, 2, 4)
+        load_e_halves(0)
         load_d(2, 0, K)
-        load_d(3, 0, HALF)
-        load_d(3, HALF, K)
+        load_d_halves(3)
         load_offset()
         load_e_scales(e_scales_rest, NT, N)
-        load_e(1, 0, G)
+        load_e_halves(1)
         load_v(0)
         load_v(1)
         load_e(2, 0, G)
-        for c in range(2, 6):
+        for c in range(2, G + 2):
             load_v(c)
         load_a_scales()
         for nt in range(NTILES):
             load_a(nt)
-            for c in range(6 + 3 * nt, min(9 + 3 * nt, len(chunks))):
+            for c in range(G + 2 + 3 * nt, min(G + 5 + 3 * nt, len(chunks))):
                 load_v(c)
 
-        warm_up(WARM_FIRST)
-        for g in range(G):
-            sort_d(0, g)
-            transpose_d(0, g)
-        warm_up(WARM_SECOND)
-        for g in range(G):
-            sort_d(1, g)
-            transpose_d(1, g)
+        for m in (0, 1):
+            warm_up(WARM_PASSES[m])
+            for g in range(G):
+                sort_d(m, g)
+                transpose_d(m, g)
         for m in (0, 1):
             for g in range(G):
                 quantize_d(m, g)
-
-        park_raw(0, 0, effect_product(0, 0))
-        park_raw(0, 1, effect_product(0, 1))
+        for m in (0, 1):
+            effect_product(0, m)
         for m in (2, 3):
             for g in range(G):
                 sort_d(m, g)
@@ -273,28 +276,28 @@ def tile_ancestry_adjusted_scores_s10_kernel(
             for g in range(G):
                 transpose_d(m, g)
                 quantize_d(m, g)
-        offset_to_partitions()
-        offset_repeat()
-        on_vector, on_scalar = nc.vector.tensor_copy, nc.scalar.copy
-        whole = (0, NT)
-        low, high = (0, NT // 2), (NT // 2, NT)
+        for h in range(2):
+            spread_offset(h)
 
+        on_vector, on_scalar = nc.vector.tensor_copy, nc.scalar.copy
+        whole, low, high = (0, NT), (0, NT // 2), (NT // 2, NT)
         interleave(on_vector, 0, *whole)
-        offset_to_rows()
         quantize_v(0)
         interleave(on_vector, 1, *whole)
-        scalar_half_after = {(1, 3): (2, low), (2, 0): (3, low), (2, 2): (5, low), (2, 3): (5, high)}
-        for nt, m in [(0, 2), (0, 3)] + [(nt, m) for nt in (1, 2) for m in range(MT)]:
-            park_raw(nt, m, effect_product(nt, m))
-            if (nt, m) in scalar_half_after:
-                c, half = scalar_half_after[nt, m]
+        scalar_halves = [(2, low), (3, low), (4, low), (5, low), (5, high)]
+        rest = [(0, 2), (0, 3)] + [(nt, m) for nt in (1, 2) for m in range(MT)]
+        for i, (nt, m) in enumerate(rest):
+            effect_product(nt, m)
+            j = i - (len(rest) - len(scalar_halves))
+            if j >= 0:
+                c, half = scalar_halves[j]
                 interleave(on_scalar, c, *half)
         quantize_v(1)
-        interleave(on_vector, 2, *high)
-        interleave(on_vector, 3, *high)
-        quantize_v(2)
-        quantize_v(3)
-        interleave(on_vector, 4, *whole)
+        for c in (2, 3):
+            interleave(on_vector, c, *high)
+        for c in (2, 3):
+            quantize_v(c)
+        interleave(on_vector, 4, *high)
 
         for nt in range(NTILES - 1):
             first = (nt + 1) * G
@@ -314,19 +317,19 @@ def tile_ancestry_adjusted_scores_s10_kernel(
                 ancestry_product(nt, m, *whole)
                 finish(nc.gpsimd, nt, m, *whole)
 
-        nt = NTILES - 1
-        for m in range(MT - 1):
+        nt, last = NTILES - 1, MT - 1
+        for m in range(last):
             spread_product(nt, m, [whole])
             exponential(nt, m, *whole)
-        for m in range(MT - 1):
+        for m in range(last):
             ancestry_product(nt, m, *whole)
             if m > 0:
                 finish(nc.vector, nt, m - 1, *whole)
-        finish(nc.vector, nt, MT - 2, *whole)
-        spread_product(nt, MT - 1, [low, high])
+        finish(nc.vector, nt, last - 1, *whole)
+        spread_product(nt, last, [low, high])
         for half in (low, high):
-            exponential(nt, MT - 1, *half)
-        for piece in (low, (256, 384), (384, NT)):
-            ancestry_product(nt, MT - 1, *piece)
+            exponential(nt, last, *half)
+        for piece in (low, (NT // 2, 3 * NT // 4), (3 * NT // 4, NT)):
+            ancestry_product(nt, last, *piece)
         for half in (low, high):
-            finish(nc.vector, nt, MT - 1, *half)
+            finish(nc.vector, nt, last, *half)

@@ -25,7 +25,7 @@ MT = M // P
 NTILES = N // NT
 BANKS = 8
 WARM_N = 256
-WARM_PASSES = (6, 4)
+WARM_PASSES = (6, 4, 4)
 
 
 def tile_ancestry_adjusted_scores_s10_kernel(
@@ -264,6 +264,7 @@ def tile_ancestry_adjusted_scores_s10_kernel(
             for g in range(G):
                 sort_d(m, g)
                 transpose_d(m, g)
+        warm_up(WARM_PASSES[2])
         for m in (0, 1):
             for g in range(G):
                 quantize_d(m, g)
@@ -325,7 +326,7 @@ def tile_ancestry_adjusted_scores_s10_kernel(
             ancestry_product(nt, m, *whole)
             if m > 0:
                 finish(nc.vector, nt, m - 1, *whole)
-        finish(nc.vector, nt, last - 1, *whole)
+        finish(nc.gpsimd, nt, last - 1, *whole)
         spread_product(nt, last, [low, high])
         for half in (low, high):
             exponential(nt, last, *half)

@@ -24,8 +24,9 @@ NT = 512
 MT = M // P
 NTILES = N // NT
 BANKS = 8
+SPLIT = 192
 WARM_N = 256
-WARM_PASSES = (6, 4, 4)
+WARM_PASSES = (6, 4)
 
 
 def tile_ancestry_adjusted_scores_s10_kernel(
@@ -42,11 +43,16 @@ def tile_ancestry_adjusted_scores_s10_kernel(
             return keep.tile(shape, dtype, name=name, align_bytes=64)
 
         banks_taken = []
+        free_banks = list(range(BANKS))
 
         def next_bank():
-            i = len(banks_taken)
-            banks_taken.append(i)
-            return psum.tile([P, NT], F32, name="bank_use%d" % i, tag="bank%d" % (i % BANKS))
+            tag = free_banks.pop(0)
+            free_banks.append(tag)
+            banks_taken.append(tag)
+            return psum.tile([P, NT], F32, name="bank_use%d" % len(banks_taken), tag="bank%d" % tag)
+
+        def pass_over_bank():
+            free_banks.append(free_banks.pop(0))
 
         def cols(nt):
             return slice(nt * NT, (nt + 1) * NT)
@@ -93,9 +99,9 @@ def tile_ancestry_adjusted_scores_s10_kernel(
                 src = effect_scales[:, r:16:4, n0:n1].rearrange("g q n -> q g n")
                 nc.sync.dma_start(out=plane[r:P:32, :, :].bitcast(I32), in_=src.bitcast(I32))
 
-        def load_a(nt):
-            src = ancestry_words[:, :, cols(nt), :].rearrange("g p n t -> p g (n t)")
-            nc.sync.dma_start(out=a_words[nt][:].bitcast(I32), in_=src.bitcast(I32))
+        def load_a(nt, g0, g1):
+            src = ancestry_words[g0:g1, :, cols(nt), :].rearrange("g p n t -> p g (n t)")
+            nc.sync.dma_start(out=a_words[nt][:, g0:g1, :].bitcast(I32), in_=src.bitcast(I32))
 
         def load_a_scales():
             for q in range(4):
@@ -108,7 +114,7 @@ def tile_ancestry_adjusted_scores_s10_kernel(
             nc.sync.dma_start(out=v_raw[c][:], in_=src)
 
         def load_offset():
-            nc.sync.dma_start(out=off_rows[:, :, 0:6], in_=offset.rearrange("(h p c) -> p h c", h=2, p=P))
+            nc.scalar.dma_start(out=off_rows[:, :, 0:6], in_=offset.rearrange("(h p c) -> p h c", h=2, p=P))
 
         def clear(tile):
             nc.vector.memset(tile[:].bitcast(I32), 0)
@@ -146,17 +152,20 @@ def tile_ancestry_adjusted_scores_s10_kernel(
                 in_=d_raw[m][:].bitcast(F32)[:, 2 * P * g : 2 * P * (g + 1)].rearrange("r (p u) -> r u p", u=2),
             )
 
-        def transpose_d(m, g):
+        def transpose_d(m, passes):
             bank = next_bank()
-            for u in range(2):
-                nc.tensor.transpose(bank[:, u * P : (u + 1) * P], d_sorted[m, g][:, u, :], ident[:])
-            d_grp[m, g] = ring.tile(
-                [P, KP], BF16, name="d_grp%d_%d" % (m, g), tag="d_grp", bufs=2 * G, align_bytes=64
-            )
-            nc.scalar.copy(
-                out=d_grp[m, g][:].bitcast(F32).rearrange("p (r u) -> p r u", u=2),
-                in_=bank[:, 0 : 2 * P].rearrange("p (u r) -> p r u", u=2),
-            )
+            for i, g in enumerate(passes):
+                for u in range(2):
+                    col = (2 * i + u) * P
+                    nc.tensor.transpose(bank[:, col : col + P], d_sorted[m, g][:, u, :], ident[:])
+            for i, g in enumerate(passes):
+                d_grp[m, g] = ring.tile(
+                    [P, KP], BF16, name="d_grp%d_%d" % (m, g), tag="d_grp", bufs=2 * G, align_bytes=64
+                )
+                nc.scalar.copy(
+                    out=d_grp[m, g][:].bitcast(F32).rearrange("p (r u) -> p r u", u=2),
+                    in_=bank[:, 2 * i * P : 2 * (i + 1) * P].rearrange("p (u r) -> p r u", u=2),
+                )
 
         def quantize_d(m, g):
             nc.vector.quantize_mx(
@@ -182,9 +191,10 @@ def tile_ancestry_adjusted_scores_s10_kernel(
                 in_=v_grp[c][:].rearrange("p n t -> p (n t)"),
             )
 
-        def product(m, width, operand):
-            bank = next_bank()
-            for g in range(G):
+        def product(m, width, operand, bank=None, passes=range(G)):
+            if bank is None:
+                bank = next_bank()
+            for g in passes:
                 rhs, rhs_scale = operand(g)
                 nc.tensor.matmul_mx(
                     out=bank[:, 0:width],
@@ -195,24 +205,45 @@ def tile_ancestry_adjusted_scores_s10_kernel(
                     start=(g == 0),
                     stop=(g == G - 1),
                 )
-            return bank[:, 0:width]
+            return bank
+
+        def effect_passes(nt, m):
+            plane = e_scales_first[:] if nt == 0 else e_scales_rest[:, :, cols(nt - 1)]
+            return product(m, NT, lambda g: (e_words[nt][:, g, :].bitcast(FP4X4), plane[:, g, :]))
+
+        def park(nt, m, raw):
+            nc.scalar.copy(out=acc[nt, m][:], in_=raw[:])
 
         def effect_product(nt, m):
-            plane = e_scales_first[:] if nt == 0 else e_scales_rest[:, :, cols(nt - 1)]
-            raw = product(m, NT, lambda g: (e_words[nt][:, g, :].bitcast(FP4X4), plane[:, g, :]))
-            nc.scalar.copy(out=acc[nt, m][:], in_=raw)
+            park(nt, m, effect_passes(nt, m))
 
-        def ancestry_product(nt, m, n0, n1):
-            mean = product(
+        def ancestry_passes(nt, m, n0, n1):
+            return product(
                 m,
                 n1 - n0,
                 lambda g: (a_words[nt][:, g, n0:n1].bitcast(FP8X4), a_scales[4 * g :, nt * NT + n0 : nt * NT + n1]),
             )
+
+        def subtract(nt, m, n0, n1, mean):
             part = acc[nt, m][:, n0:n1]
-            nc.vector.tensor_tensor(out=part, in0=part, in1=mean, op=ALU.subtract)
+            nc.vector.tensor_tensor(out=part, in0=part, in1=mean[:, 0 : n1 - n0], op=ALU.subtract)
+
+        def ancestry_product(nt, m, n0, n1):
+            subtract(nt, m, n0, n1, ancestry_passes(nt, m, n0, n1))
+
+        def spread_passes(nt, m, bank, passes):
+            return product(
+                m, NT, lambda g: (v_codes[nt * G + g][:].bitcast(FP8X4), v_scales[nt * G + g][:]), bank, passes
+            )
 
         def spread_product(nt, m, parts):
-            sums = product(m, NT, lambda g: (v_codes[nt * G + g][:].bitcast(FP8X4), v_scales[nt * G + g][:]))
+            add_offset(nt, m, spread_passes(nt, m, None, range(G)), parts)
+
+        def spread_pair(nt):
+            open_banks = [spread_passes(nt, m, None, range(G - 1)) for m in (0, 1)]
+            return [spread_passes(nt, m, open_banks[m], [G - 1]) for m in (0, 1)]
+
+        def add_offset(nt, m, sums, parts):
             expo[nt, m] = ring.tile([P, NT], F32, name="expo%d_%d" % (nt, m), tag="expo", bufs=2 * MT)
             for n0, n1 in parts:
                 nc.vector.tensor_tensor(
@@ -226,111 +257,156 @@ def tile_ancestry_adjusted_scores_s10_kernel(
             part = expo[nt, m][:, n0:n1]
             nc.scalar.activation(out=part, in_=part, func=EXP)
 
-        def finish(engine, nt, m, n0, n1):
+        def multiply(engine, nt, m, n0, n1):
             part = acc[nt, m][:, n0:n1]
             engine.tensor_tensor(out=part, in0=part, in1=expo[nt, m][:, n0:n1], op=ALU.mult)
-            nc.sync.dma_start(out=out[m * P : (m + 1) * P, nt * NT + n0 : nt * NT + n1], in_=part)
 
+        def store(nt, m, n0, n1):
+            nc.sync.dma_start(out=out[m * P : (m + 1) * P, nt * NT + n0 : nt * NT + n1], in_=acc[nt, m][:, n0:n1])
+
+        def finish(engine, nt, m, n0, n1):
+            multiply(engine, nt, m, n0, n1)
+            store(nt, m, n0, n1)
+
+        load_offset()
         load_d_halves(0)
         load_d_halves(1)
-        clear(warm_in)
-        clear(e_scales_first)
+        load_e(0, 0, G // 2)
+        nc.gpsimd.memset(warm_in[:].bitcast(I32), 0)
         nc.vector.quantize_mx(out=warm_codes[:].bitcast(FP8X4), scales=warm_scales[:], in_=warm_in[:])
-        nc.vector.memset(ident[:], 0.0)
-        make_identity(nc, ident[:], nomemset=True)
+        make_identity(nc, ident[:])
+        clear(e_scales_first)
         nc.scalar.activation(out=warm_out[:], in_=warm_in[:, 0:1], func=EXP)
         clear(e_scales_rest)
-        clear(a_scales)
         load_e_scales(e_scales_first, 0, NT)
-        load_e_halves(0)
+        load_e(0, G // 2, G)
         load_d(2, 0, K)
         load_d_halves(3)
-        load_offset()
         load_e_scales(e_scales_rest, NT, N)
         load_e_halves(1)
         load_v(0)
+        load_e(2, 0, G // 2)
         load_v(1)
-        load_e(2, 0, G)
+        load_e(2, G // 2, G)
         for c in range(2, G + 2):
             load_v(c)
-        load_a_scales()
-        for nt in range(NTILES):
-            load_a(nt)
-            for c in range(G + 2 + 3 * nt, min(G + 5 + 3 * nt, len(chunks))):
-                load_v(c)
 
         for m in (0, 1):
             warm_up(WARM_PASSES[m])
             for g in range(G):
                 sort_d(m, g)
-                transpose_d(m, g)
-        warm_up(WARM_PASSES[2])
+                transpose_d(m, [g])
+        for h in range(2):
+            spread_offset(h)
         for m in (0, 1):
             for g in range(G):
                 quantize_d(m, g)
-        for m in (0, 1):
-            effect_product(0, m)
+        clear(a_scales)
+        load_a_scales()
+        load_a(0, 0, G // 2)
+        load_a(0, G // 2, G)
+        for c in (6, 7, 8, 9):
+            load_v(c)
+        load_a(1, 0, G // 2)
+        load_a(1, G // 2, G)
+        for c in (10, 11):
+            load_v(c)
+        load_a(2, 0, G)
+        first_two = [effect_passes(0, m) for m in (0, 1)]
+        park(0, 0, first_two[0])
         for m in (2, 3):
             for g in range(G):
                 sort_d(m, g)
-        for m in (2, 3):
-            for g in range(G):
-                transpose_d(m, g)
-                quantize_d(m, g)
-        for h in range(2):
-            spread_offset(h)
+        for g in range(G):
+            transpose_d(2, [g])
+            quantize_d(2, g)
+        for passes in ([0, 1], [2, 3]):
+            transpose_d(3, passes)
+            for g in passes:
+                quantize_d(3, g)
+        park(0, 1, first_two[1])
 
         on_vector, on_scalar = nc.vector.tensor_copy, nc.scalar.copy
         whole, low, high = (0, NT), (0, NT // 2), (NT // 2, NT)
         interleave(on_vector, 0, *whole)
+        interleave(on_vector, 1, *low)
         quantize_v(0)
-        interleave(on_vector, 1, *whole)
-        scalar_halves = [(2, low), (3, low), (4, low), (5, low), (5, high)]
-        rest = [(0, 2), (0, 3)] + [(nt, m) for nt in (1, 2) for m in range(MT)]
-        for i, (nt, m) in enumerate(rest):
-            effect_product(nt, m)
-            j = i - (len(rest) - len(scalar_halves))
-            if j >= 0:
-                c, half = scalar_halves[j]
-                interleave(on_scalar, c, *half)
+        interleave(on_vector, 1, *high)
+        interleave(on_vector, 2, *low)
         quantize_v(1)
-        for c in (2, 3):
-            interleave(on_vector, c, *high)
-        for c in (2, 3):
-            quantize_v(c)
+        interleave(on_vector, 2, *high)
+        rest = [(0, 2), (0, 3)] + [(nt, m) for nt in (1, 2) for m in range(MT)]
+        for nt, m in rest:
+            effect_product(nt, m)
+            if (nt, m) == (0, 2):
+                pass_over_bank()
+            if (nt, m) == (2, 0):
+                interleave(on_scalar, 3, *low)
+        interleave(on_vector, 3, *high)
+        quantize_v(2)
+        interleave(on_vector, 4, *low)
+        quantize_v(3)
         interleave(on_vector, 4, *high)
+        interleave(on_scalar, 5, *whole)
 
-        for nt in range(NTILES - 1):
-            first = (nt + 1) * G
-            for m in range(MT):
-                spread_product(nt, m, [whole])
-            for c in (first, first + 1):
-                quantize_v(c)
-                interleave(on_scalar, c + 2, *low)
-                interleave(on_vector, c + 2, *high)
-            for m in range(MT):
-                exponential(nt, m, *whole)
-            for c in (first + 2, first + 3):
-                quantize_v(c)
-            for c in range(first + G, min(first + G + 2, len(chunks))):
-                interleave(on_scalar, c, *whole)
-            for m in range(MT):
-                ancestry_product(nt, m, *whole)
-                finish(nc.gpsimd, nt, m, *whole)
+        pair = spread_pair(0)
+        add_offset(0, 0, pair[0], [whole])
+        add_offset(0, 1, pair[1], [whole])
+        quantize_v(4)
+        spread_product(0, 2, [whole])
+        quantize_v(5)
+        spread_product(0, 3, [whole])
+        for m in range(MT - 1):
+            exponential(0, m, *whole)
+        for c in (6, 7):
+            interleave(on_scalar, c, 0, SPLIT)
+            interleave(on_vector, c, SPLIT, NT)
+        exponential(0, MT - 1, *whole)
+        for c in (6, 7):
+            quantize_v(c)
+        for m in range(MT):
+            ancestry_product(0, m, *whole)
+            finish(nc.gpsimd, 0, m, *whole)
+        interleave(on_scalar, 8, *whole)
+        pair = spread_pair(1)
+        add_offset(1, 0, pair[0], [whole])
+        add_offset(1, 1, pair[1], [whole])
+        interleave(on_scalar, 9, *whole)
+        spread_product(1, 2, [whole])
+        spread_product(1, 3, [whole])
+        quantize_v(8)
+        quantize_v(9)
+        interleave(on_scalar, 10, *whole)
+        interleave(on_scalar, 11, 0, NT // 4)
+        interleave(on_vector, 11, NT // 4, NT)
+        for m in range(MT):
+            exponential(1, m, *whole)
+        for c in (10, 11):
+            quantize_v(c)
+        for m in range(MT):
+            ancestry_product(1, m, *whole)
+            if m == 1:
+                finish(nc.vector, 1, 0, *whole)
+            if m > 0:
+                finish(nc.gpsimd, 1, m, *whole)
 
         nt, last = NTILES - 1, MT - 1
-        for m in range(last):
-            spread_product(nt, m, [whole])
+        pair = spread_pair(nt)
+        for m in (0, 1):
+            add_offset(nt, m, pair[m], [whole])
             exponential(nt, m, *whole)
+        spread_product(nt, 2, [whole])
+        exponential(nt, 2, *whole)
         for m in range(last):
             ancestry_product(nt, m, *whole)
-            if m > 0:
-                finish(nc.vector, nt, m - 1, *whole)
-        finish(nc.gpsimd, nt, last - 1, *whole)
+            finish(nc.gpsimd, nt, m, *whole)
         spread_product(nt, last, [low, high])
         for half in (low, high):
             exponential(nt, last, *half)
-        for piece in (low, (NT // 2, 3 * NT // 4), (3 * NT // 4, NT)):
+        for piece in (low, (NT // 2, 3 * NT // 4)):
             ancestry_product(nt, last, *piece)
-        for half in (low, high):
-            finish(nc.vector, nt, last, *half)
+        finish(nc.vector, nt, last, *low)
+        ancestry_product(nt, last, 3 * NT // 4, NT)
+        multiply(nc.vector, nt, last, NT // 2, 3 * NT // 4)
+        multiply(nc.vector, nt, last, 3 * NT // 4, NT)
+        store(nt, last, *high)

@@ -24,7 +24,7 @@ NT = 512
 MT = M // P
 NTILES = N // NT
 BANKS = 8
-SPLIT = 192
+SPLIT = 176
 WARM_N = 256
 WARM_PASSES = (6, 4)
 
@@ -177,7 +177,7 @@ def tile_ancestry_adjusted_scores_s10_kernel(
         def interleave(engine_copy, c, n0, n1):
             if c not in v_grp:
                 v_grp[c] = ring.tile(
-                    [P, NT, PACK], BF16, name="v_grp%d" % c, tag="v_grp", bufs=G + 2, align_bytes=64
+                    [P, NT, PACK], BF16, name="v_grp%d" % c, tag="v_grp", bufs=G + 1, align_bytes=64
                 )
             engine_copy(
                 out=v_grp[c][:, n0:n1, :].rearrange("p (c i) t -> p c t i", i=4),
@@ -217,12 +217,18 @@ def tile_ancestry_adjusted_scores_s10_kernel(
         def effect_product(nt, m):
             park(nt, m, effect_passes(nt, m))
 
-        def ancestry_passes(nt, m, n0, n1):
+        def ancestry_passes(nt, m, n0, n1, bank=None, passes=range(G)):
             return product(
                 m,
                 n1 - n0,
                 lambda g: (a_words[nt][:, g, n0:n1].bitcast(FP8X4), a_scales[4 * g :, nt * NT + n0 : nt * NT + n1]),
+                bank,
+                passes,
             )
+
+        def ancestry_tile(nt):
+            open_banks = [ancestry_passes(nt, m, 0, NT, None, range(G // 2)) for m in range(MT)]
+            return [ancestry_passes(nt, m, 0, NT, open_banks[m], range(G // 2, G)) for m in range(MT)]
 
         def subtract(nt, m, n0, n1, mean):
             part = acc[nt, m][:, n0:n1]
@@ -236,6 +242,16 @@ def tile_ancestry_adjusted_scores_s10_kernel(
                 m, NT, lambda g: (v_codes[nt * G + g][:].bitcast(FP8X4), v_scales[nt * G + g][:]), bank, passes
             )
 
+        def spread_half(nt, m, n0, n1):
+            bank = next_bank()
+            product(
+                m,
+                n1 - n0,
+                lambda g: (v_codes[nt * G + g][:, n0:n1].bitcast(FP8X4), v_scales[nt * G + g][:, n0:n1]),
+                bank[:, n0:n1],
+            )
+            return bank
+
         def spread_product(nt, m, parts):
             add_offset(nt, m, spread_passes(nt, m, None, range(G)), parts)
 
@@ -244,7 +260,8 @@ def tile_ancestry_adjusted_scores_s10_kernel(
             return [spread_passes(nt, m, open_banks[m], [G - 1]) for m in (0, 1)]
 
         def add_offset(nt, m, sums, parts):
-            expo[nt, m] = ring.tile([P, NT], F32, name="expo%d_%d" % (nt, m), tag="expo", bufs=2 * MT)
+            if (nt, m) not in expo:
+                expo[nt, m] = ring.tile([P, NT], F32, name="expo%d_%d" % (nt, m), tag="expo", bufs=2 * MT + 2)
             for n0, n1 in parts:
                 nc.vector.tensor_tensor(
                     out=expo[nt, m][:, n0:n1],
@@ -285,9 +302,8 @@ def tile_ancestry_adjusted_scores_s10_kernel(
         load_e_scales(e_scales_rest, NT, N)
         load_e_halves(1)
         load_v(0)
-        load_e(2, 0, G // 2)
         load_v(1)
-        load_e(2, G // 2, G)
+        load_e_halves(2)
         for c in range(2, G + 2):
             load_v(c)
 
@@ -304,13 +320,14 @@ def tile_ancestry_adjusted_scores_s10_kernel(
         clear(a_scales)
         load_a_scales()
         load_a(0, 0, G // 2)
+        load_v(6)
         load_a(0, G // 2, G)
-        for c in (6, 7, 8, 9):
+        for c in (7, 8, 9):
             load_v(c)
         load_a(1, 0, G // 2)
         load_a(1, G // 2, G)
-        for c in (10, 11):
-            load_v(c)
+        load_v(10)
+        load_v(11)
         load_a(2, 0, G)
         first_two = [effect_passes(0, m) for m in (0, 1)]
         park(0, 0, first_two[0])
@@ -329,43 +346,50 @@ def tile_ancestry_adjusted_scores_s10_kernel(
         on_vector, on_scalar = nc.vector.tensor_copy, nc.scalar.copy
         whole, low, high = (0, NT), (0, NT // 2), (NT // 2, NT)
         interleave(on_vector, 0, *whole)
-        interleave(on_vector, 1, *low)
-        quantize_v(0)
         interleave(on_vector, 1, *high)
-        interleave(on_vector, 2, *low)
-        quantize_v(1)
-        interleave(on_vector, 2, *high)
+        quantize_v(0)
         rest = [(0, 2), (0, 3)] + [(nt, m) for nt in (1, 2) for m in range(MT)]
+        scalar_halves = {(1, 1): 1, (2, 0): 3, (2, 3): 5}
         for nt, m in rest:
             effect_product(nt, m)
             if (nt, m) == (0, 2):
                 pass_over_bank()
-            if (nt, m) == (2, 0):
-                interleave(on_scalar, 3, *low)
+            if (nt, m) in scalar_halves:
+                interleave(on_scalar, scalar_halves[nt, m], *low)
+            if (nt, m) == (1, 1):
+                quantize_v(1)
+        interleave(on_vector, 2, *whole)
         interleave(on_vector, 3, *high)
         quantize_v(2)
         interleave(on_vector, 4, *low)
         quantize_v(3)
         interleave(on_vector, 4, *high)
-        interleave(on_scalar, 5, *whole)
+        interleave(on_vector, 5, *high)
 
         pair = spread_pair(0)
         add_offset(0, 0, pair[0], [whole])
-        add_offset(0, 1, pair[1], [whole])
         quantize_v(4)
-        spread_product(0, 2, [whole])
+        add_offset(0, 1, pair[1], [whole])
         quantize_v(5)
-        spread_product(0, 3, [whole])
-        for m in range(MT - 1):
+        spread_product(0, 2, [whole])
+        for m in range(2):
             exponential(0, m, *whole)
-        for c in (6, 7):
-            interleave(on_scalar, c, 0, SPLIT)
-            interleave(on_vector, c, SPLIT, NT)
-        exponential(0, MT - 1, *whole)
-        for c in (6, 7):
-            quantize_v(c)
-        for m in range(MT):
-            ancestry_product(0, m, *whole)
+        interleave(on_scalar, 6, 0, SPLIT)
+        interleave(on_vector, 6, SPLIT, NT)
+        spread_product(0, 3, [whole])
+        for m in range(2, MT):
+            exponential(0, m, *whole)
+        quantize_v(6)
+        means = ancestry_tile(0)
+        subtract(0, 0, *whole, means[0])
+        interleave(on_scalar, 7, 0, SPLIT)
+        interleave(on_vector, 7, SPLIT, NT)
+        subtract(0, 1, *whole, means[1])
+        quantize_v(7)
+        finish(nc.gpsimd, 0, 1, *whole)
+        finish(nc.gpsimd, 0, 0, *whole)
+        for m in (2, 3):
+            subtract(0, m, *whole, means[m])
             finish(nc.gpsimd, 0, m, *whole)
         interleave(on_scalar, 8, *whole)
         pair = spread_pair(1)
@@ -374,39 +398,42 @@ def tile_ancestry_adjusted_scores_s10_kernel(
         interleave(on_scalar, 9, *whole)
         spread_product(1, 2, [whole])
         spread_product(1, 3, [whole])
+        means = [ancestry_passes(1, m, *whole) for m in range(MT)]
+        subtract(1, 0, *whole, means[0])
+        interleave(on_scalar, 10, *low)
+        exponential(1, 0, *whole)
+        interleave(on_scalar, 11, *whole)
         quantize_v(8)
         quantize_v(9)
-        interleave(on_scalar, 10, *whole)
-        interleave(on_scalar, 11, 0, NT // 4)
-        interleave(on_vector, 11, NT // 4, NT)
-        for m in range(MT):
+        interleave(on_vector, 10, *high)
+        finish(nc.vector, 1, 0, *whole)
+        quantize_v(10)
+        subtract(1, 1, *whole, means[1])
+        quantize_v(11)
+        for m in range(1, MT):
             exponential(1, m, *whole)
-        for c in (10, 11):
-            quantize_v(c)
-        for m in range(MT):
-            ancestry_product(1, m, *whole)
-            if m == 1:
-                finish(nc.vector, 1, 0, *whole)
-            if m > 0:
-                finish(nc.gpsimd, 1, m, *whole)
+        finish(nc.gpsimd, 1, 1, *whole)
+        for m in (2, 3):
+            subtract(1, m, *whole, means[m])
+            finish(nc.gpsimd, 1, m, *whole)
 
         nt, last = NTILES - 1, MT - 1
-        pair = spread_pair(nt)
-        for m in (0, 1):
-            add_offset(nt, m, pair[m], [whole])
+        sums = [next_bank() for m in range(last)]
+        for g in range(G):
+            for m in range(last):
+                spread_passes(nt, m, sums[m], [g])
+        for m in range(last):
+            add_offset(nt, m, sums[m], [whole])
             exponential(nt, m, *whole)
-        spread_product(nt, 2, [whole])
-        exponential(nt, 2, *whole)
         for m in range(last):
             ancestry_product(nt, m, *whole)
-            finish(nc.gpsimd, nt, m, *whole)
-        spread_product(nt, last, [low, high])
+            if m > 0:
+                finish(nc.vector, nt, m - 1, *whole)
+        finish(nc.gpsimd, nt, last - 1, *whole)
         for half in (low, high):
+            add_offset(nt, last, spread_half(nt, last, *half), [half])
             exponential(nt, last, *half)
-        for piece in (low, (NT // 2, 3 * NT // 4)):
+        for piece in (low, (NT // 2, 3 * NT // 4), (3 * NT // 4, NT)):
             ancestry_product(nt, last, *piece)
-        finish(nc.vector, nt, last, *low)
-        ancestry_product(nt, last, 3 * NT // 4, NT)
-        multiply(nc.vector, nt, last, NT // 2, 3 * NT // 4)
-        multiply(nc.vector, nt, last, 3 * NT // 4, NT)
-        store(nt, last, *high)
+        for half in (low, high):
+            finish(nc.vector, nt, last, *half)

@@ -289,16 +289,24 @@ def tile_ancestry_adjusted_scores_s10_kernel(
         load_d_halves(0)
         load_d_halves(1)
         load_e(0, 0, G // 2)
-        nc.gpsimd.memset(warm_in[:].bitcast(I32), 0)
-        nc.vector.quantize_mx(out=warm_codes[:].bitcast(FP8X4), scales=warm_scales[:], in_=warm_in[:])
-        make_identity(nc, ident[:])
+        clear(warm_in)
         clear(e_scales_first)
+        nc.vector.quantize_mx(out=warm_codes[:].bitcast(FP8X4), scales=warm_scales[:], in_=warm_in[:])
+        nc.vector.memset(ident[:], 0.0)
+        make_identity(nc, ident[:], nomemset=True)
         nc.scalar.activation(out=warm_out[:], in_=warm_in[:, 0:1], func=EXP)
-        clear(e_scales_rest)
         load_e_scales(e_scales_first, 0, NT)
         load_e(0, G // 2, G)
         load_d(2, 0, K)
         load_d_halves(3)
+
+        for m in (0, 1):
+            warm_up(WARM_PASSES[m])
+            for g in range(G):
+                sort_d(m, g)
+                transpose_d(m, [g])
+            if m == 0:
+                clear(e_scales_rest)
         load_e_scales(e_scales_rest, NT, N)
         load_e_halves(1)
         load_v(0)
@@ -306,12 +314,6 @@ def tile_ancestry_adjusted_scores_s10_kernel(
         load_e_halves(2)
         for c in range(2, G + 2):
             load_v(c)
-
-        for m in (0, 1):
-            warm_up(WARM_PASSES[m])
-            for g in range(G):
-                sort_d(m, g)
-                transpose_d(m, [g])
         for h in range(2):
             spread_offset(h)
         for m in (0, 1):

@@ -24,7 +24,6 @@ NT = 512
 MT = M // P
 NTILES = N // NT
 BANKS = 8
-SPLIT = 176
 WARM_N = 256
 WARM_PASSES = (6, 4)
 
@@ -68,7 +67,8 @@ def tile_ancestry_adjusted_scores_s10_kernel(
         d_raw = [kept("d_raw%d" % m, [P, K], BF16) for m in range(MT)]
         d_codes = [kept("d_codes%d" % m, [P, G * P], U32) for m in range(MT)]
         d_scales = [kept("d_scales%d" % m, [P, G * P], U8) for m in range(MT)]
-        e_words = [kept("e_words%d" % nt, [P, G, 2 * NT], U8) for nt in range(NTILES)]
+        e_words_first = kept("e_words_first", [P, G, 2 * NT], U8)
+        e_words_rest = kept("e_words_rest", [P, G, 2 * (N - NT)], U8)
         e_scales_first = kept("e_scales_first", [P, G, NT], U8)
         e_scales_rest = kept("e_scales_rest", [P, G, N - NT], U8)
         a_words = [kept("a_words%d" % nt, [P, G, NT], U32) for nt in range(NTILES)]
@@ -86,13 +86,9 @@ def tile_ancestry_adjusted_scores_s10_kernel(
             load_d(m, 0, K // 2)
             load_d(m, K // 2, K)
 
-        def load_e(nt, g0, g1):
-            src = effect_words[g0:g1, :, 2 * nt * NT : 2 * (nt + 1) * NT].rearrange("g p b -> p g b")
-            nc.sync.dma_start(out=e_words[nt][:, g0:g1, :].bitcast(I32), in_=src.bitcast(I32))
-
-        def load_e_halves(nt):
-            load_e(nt, 0, G // 2)
-            load_e(nt, G // 2, G)
+        def load_e(words, n0, n1, g0, g1):
+            src = effect_words[g0:g1, :, 2 * n0 : 2 * n1].rearrange("g p b -> p g b")
+            nc.sync.dma_start(out=words[:, g0:g1, :].bitcast(I32), in_=src.bitcast(I32))
 
         def load_e_scales(plane, n0, n1):
             for r in range(4):
@@ -106,7 +102,7 @@ def tile_ancestry_adjusted_scores_s10_kernel(
         def load_a_scales():
             for q in range(4):
                 src = ancestry_scales[:, 4 * q : 4 * q + 4, :]
-                nc.sync.dma_start(out=a_scales[32 * q : 32 * q + 16, :].bitcast(I32), in_=src.bitcast(I32))
+                nc.gpsimd.dma_start(out=a_scales[32 * q : 32 * q + 16, :].bitcast(I32), in_=src.bitcast(I32))
 
         def load_v(c):
             nt, g = chunks[c]
@@ -207,9 +203,14 @@ def tile_ancestry_adjusted_scores_s10_kernel(
                 )
             return bank
 
-        def effect_passes(nt, m):
-            plane = e_scales_first[:] if nt == 0 else e_scales_rest[:, :, cols(nt - 1)]
-            return product(m, NT, lambda g: (e_words[nt][:, g, :].bitcast(FP4X4), plane[:, g, :]))
+        def effect_operand(nt, g):
+            if nt == 0:
+                return e_words_first[:, g, :].bitcast(FP4X4), e_scales_first[:, g, :]
+            n0 = (nt - 1) * NT
+            return e_words_rest[:, g, 2 * n0 : 2 * (n0 + NT)].bitcast(FP4X4), e_scales_rest[:, g, n0 : n0 + NT]
+
+        def effect_passes(nt, m, bank=None, passes=range(G)):
+            return product(m, NT, lambda g: effect_operand(nt, g), bank, passes)
 
         def park(nt, m, raw):
             nc.scalar.copy(out=acc[nt, m][:], in_=raw[:])
@@ -288,7 +289,7 @@ def tile_ancestry_adjusted_scores_s10_kernel(
         load_offset()
         load_d_halves(0)
         load_d_halves(1)
-        load_e(0, 0, G // 2)
+        load_e(e_words_first, 0, NT, 0, G // 2)
         clear(warm_in)
         clear(e_scales_first)
         nc.vector.quantize_mx(out=warm_codes[:].bitcast(FP8X4), scales=warm_scales[:], in_=warm_in[:])
@@ -296,7 +297,7 @@ def tile_ancestry_adjusted_scores_s10_kernel(
         make_identity(nc, ident[:], nomemset=True)
         nc.scalar.activation(out=warm_out[:], in_=warm_in[:, 0:1], func=EXP)
         load_e_scales(e_scales_first, 0, NT)
-        load_e(0, G // 2, G)
+        load_e(e_words_first, 0, NT, G // 2, G)
         load_d(2, 0, K)
         load_d_halves(3)
 
@@ -308,28 +309,25 @@ def tile_ancestry_adjusted_scores_s10_kernel(
             if m == 0:
                 clear(e_scales_rest)
         load_e_scales(e_scales_rest, NT, N)
-        load_e_halves(1)
-        load_v(0)
-        load_v(1)
-        load_e_halves(2)
-        for c in range(2, G + 2):
+        load_e(e_words_rest, NT, N, 0, G // 2)
+        load_e(e_words_rest, NT, N, G // 2, G)
+        for c in range(G + 2):
             load_v(c)
         for h in range(2):
             spread_offset(h)
         for m in (0, 1):
             for g in range(G):
                 quantize_d(m, g)
-        clear(a_scales)
-        load_a_scales()
-        load_a(0, 0, G // 2)
         load_v(6)
+        load_a(0, 0, G // 2)
+        load_v(7)
         load_a(0, G // 2, G)
-        for c in (7, 8, 9):
+        for c in (8, 9):
             load_v(c)
         load_a(1, 0, G // 2)
-        load_a(1, G // 2, G)
         load_v(10)
         load_v(11)
+        load_a(1, G // 2, G)
         load_a(2, 0, G)
         first_two = [effect_passes(0, m) for m in (0, 1)]
         park(0, 0, first_two[0])
@@ -344,97 +342,95 @@ def tile_ancestry_adjusted_scores_s10_kernel(
             for g in passes:
                 quantize_d(3, g)
         park(0, 1, first_two[1])
+        clear(a_scales)
+        load_a_scales()
 
         on_vector, on_scalar = nc.vector.tensor_copy, nc.scalar.copy
         whole, low, high = (0, NT), (0, NT // 2), (NT // 2, NT)
+        effect_product(0, 2)
+        pass_over_bank()
+        effect_product(0, 3)
+        banks = [effect_passes(1, m, None, range(G // 2)) for m in range(MT)]
         interleave(on_vector, 0, *whole)
         interleave(on_vector, 1, *high)
         quantize_v(0)
-        rest = [(0, 2), (0, 3)] + [(nt, m) for nt in (1, 2) for m in range(MT)]
-        scalar_halves = {(1, 1): 1, (2, 0): 3, (2, 3): 5}
-        for nt, m in rest:
-            effect_product(nt, m)
-            if (nt, m) == (0, 2):
-                pass_over_bank()
-            if (nt, m) in scalar_halves:
-                interleave(on_scalar, scalar_halves[nt, m], *low)
-            if (nt, m) == (1, 1):
-                quantize_v(1)
+        interleave(on_scalar, 1, *low)
         interleave(on_vector, 2, *whole)
+        quantize_v(1)
+        for m in range(MT):
+            park(1, m, effect_passes(1, m, banks[m], range(G // 2, G)))
+        interleave(on_scalar, 3, *low)
         interleave(on_vector, 3, *high)
         quantize_v(2)
-        interleave(on_vector, 4, *low)
-        quantize_v(3)
+        for m in range(MT):
+            effect_product(2, m)
+            if m == 1:
+                interleave(on_scalar, 4, *low)
         interleave(on_vector, 4, *high)
-        interleave(on_vector, 5, *high)
+        quantize_v(3)
+        interleave(on_vector, 5, *whole)
+        quantize_v(4)
 
+        interleave(on_scalar, 6, *low)
         pair = spread_pair(0)
         add_offset(0, 0, pair[0], [whole])
-        quantize_v(4)
-        add_offset(0, 1, pair[1], [whole])
         quantize_v(5)
-        spread_product(0, 2, [whole])
+        add_offset(0, 1, pair[1], [whole])
+        interleave(on_vector, 6, *high)
         for m in range(2):
             exponential(0, m, *whole)
-        interleave(on_scalar, 6, 0, SPLIT)
-        interleave(on_vector, 6, SPLIT, NT)
+        spread_product(0, 2, [whole])
         spread_product(0, 3, [whole])
+        quantize_v(6)
+        interleave(on_scalar, 7, *low)
+        interleave(on_vector, 7, *high)
         for m in range(2, MT):
             exponential(0, m, *whole)
-        quantize_v(6)
-        means = ancestry_tile(0)
-        subtract(0, 0, *whole, means[0])
-        interleave(on_scalar, 7, 0, SPLIT)
-        interleave(on_vector, 7, SPLIT, NT)
-        subtract(0, 1, *whole, means[1])
         quantize_v(7)
-        finish(nc.gpsimd, 0, 1, *whole)
-        finish(nc.gpsimd, 0, 0, *whole)
-        for m in (2, 3):
+        means = ancestry_tile(0)
+        for m in range(MT):
             subtract(0, m, *whole, means[m])
             finish(nc.gpsimd, 0, m, *whole)
         interleave(on_scalar, 8, *whole)
+        interleave(on_scalar, 9, *whole)
         pair = spread_pair(1)
         add_offset(1, 0, pair[0], [whole])
         add_offset(1, 1, pair[1], [whole])
-        interleave(on_scalar, 9, *whole)
         spread_product(1, 2, [whole])
         spread_product(1, 3, [whole])
-        means = [ancestry_passes(1, m, *whole) for m in range(MT)]
-        subtract(1, 0, *whole, means[0])
+        means = ancestry_tile(1)
         interleave(on_scalar, 10, *low)
-        exponential(1, 0, *whole)
         interleave(on_scalar, 11, *whole)
         quantize_v(8)
-        quantize_v(9)
         interleave(on_vector, 10, *high)
-        finish(nc.vector, 1, 0, *whole)
+        quantize_v(9)
         quantize_v(10)
-        subtract(1, 1, *whole, means[1])
+        subtract(1, 0, *whole, means[0])
         quantize_v(11)
-        for m in range(1, MT):
+        for m in range(MT):
             exponential(1, m, *whole)
-        finish(nc.gpsimd, 1, 1, *whole)
-        for m in (2, 3):
-            subtract(1, m, *whole, means[m])
+            if m > 0:
+                subtract(1, m, *whole, means[m])
             finish(nc.gpsimd, 1, m, *whole)
 
         nt, last = NTILES - 1, MT - 1
-        sums = [next_bank() for m in range(last)]
-        for g in range(G):
-            for m in range(last):
-                spread_passes(nt, m, sums[m], [g])
-        for m in range(last):
-            add_offset(nt, m, sums[m], [whole])
+        pair = spread_pair(nt)
+        for m in (0, 1):
+            add_offset(nt, m, pair[m], [whole])
             exponential(nt, m, *whole)
-        for m in range(last):
-            ancestry_product(nt, m, *whole)
-            if m > 0:
-                finish(nc.vector, nt, m - 1, *whole)
-        finish(nc.gpsimd, nt, last - 1, *whole)
-        for half in (low, high):
-            add_offset(nt, last, spread_half(nt, last, *half), [half])
-            exponential(nt, last, *half)
+        ancestry_product(nt, 0, *whole)
+        ancestry_product(nt, 1, *whole)
+        finish(nc.vector, nt, 0, *whole)
+        spread_product(nt, 2, [whole])
+        exponential(nt, 2, *whole)
+        finish(nc.vector, nt, 1, *whole)
+        ancestry_product(nt, 2, *whole)
+        halves = [spread_half(nt, last, *half) for half in (low, high)]
+        add_offset(nt, last, halves[0], [low])
+        exponential(nt, last, *low)
+        finish(nc.vector, nt, 2, *whole)
+        add_offset(nt, last, halves[1], [high])
+        exponential(nt, last, *high)
         for piece in (low, (NT // 2, 3 * NT // 4), (3 * NT // 4, NT)):
             ancestry_product(nt, last, *piece)
         for half in (low, high):

@@ -102,7 +102,7 @@ def tile_ancestry_adjusted_scores_s10_kernel(
         def load_a_scales():
             for q in range(4):
                 src = ancestry_scales[:, 4 * q : 4 * q + 4, :]
-                nc.gpsimd.dma_start(out=a_scales[32 * q : 32 * q + 16, :].bitcast(I32), in_=src.bitcast(I32))
+                nc.sync.dma_start(out=a_scales[32 * q : 32 * q + 16, :].bitcast(I32), in_=src.bitcast(I32))
 
         def load_v(c):
             nt, g = chunks[c]
@@ -318,7 +318,9 @@ def tile_ancestry_adjusted_scores_s10_kernel(
         for m in (0, 1):
             for g in range(G):
                 quantize_d(m, g)
+        clear(a_scales)
         load_v(6)
+        load_a_scales()
         load_a(0, 0, G // 2)
         load_v(7)
         load_a(0, G // 2, G)
@@ -342,8 +344,6 @@ def tile_ancestry_adjusted_scores_s10_kernel(
             for g in passes:
                 quantize_d(3, g)
         park(0, 1, first_two[1])
-        clear(a_scales)
-        load_a_scales()
 
         on_vector, on_scalar = nc.vector.tensor_copy, nc.scalar.copy
         whole, low, high = (0, NT), (0, NT // 2), (NT // 2, NT)

@@ -21,8 +21,9 @@ PACK = 4
 KP = P * PACK
 G = K // KP
 NT = 512
+NH = N // 2
+NY = NH - NT
 MT = M // P
-NTILES = N // NT
 BANKS = 8
 WARM_N = 256
 WARM_PASSES = (6, 4)
@@ -44,19 +45,18 @@ def tile_ancestry_adjusted_scores_s10_kernel(
         banks_taken = []
         free_banks = list(range(BANKS))
 
+        def pass_over_bank():
+            free_banks.append(free_banks.pop(0))
+
         def next_bank():
             tag = free_banks.pop(0)
             free_banks.append(tag)
             banks_taken.append(tag)
             return psum.tile([P, NT], F32, name="bank_use%d" % len(banks_taken), tag="bank%d" % tag)
 
-        def pass_over_bank():
-            free_banks.append(free_banks.pop(0))
+        def shared(name, shape, dtype):
+            return ring.tile(shape, dtype, name=name, tag="shared", bufs=MT, align_bytes=64)
 
-        def cols(nt):
-            return slice(nt * NT, (nt + 1) * NT)
-
-        chunks = [(nt, g) for nt in range(NTILES) for g in range(G)]
         ident = kept("ident", [P, P], F32)
         warm_in = kept("warm_in", [P, PACK * WARM_N], BF16)
         warm_out = kept("warm_out", [P, 1], F32)
@@ -64,19 +64,19 @@ def tile_ancestry_adjusted_scores_s10_kernel(
         warm_scales = kept("warm_scales", [P, WARM_N], U8)
         off_rows = kept("off_rows", [P, 2, 16], BF16)
         off_all = kept("off_all", [P, N], BF16)
-        d_raw = [kept("d_raw%d" % m, [P, K], BF16) for m in range(MT)]
+        d_raw = [shared("d_raw%d" % m, [P, K], BF16) for m in range(MT)]
         d_codes = [kept("d_codes%d" % m, [P, G * P], U32) for m in range(MT)]
         d_scales = [kept("d_scales%d" % m, [P, G * P], U8) for m in range(MT)]
         e_words_first = kept("e_words_first", [P, G, 2 * NT], U8)
         e_words_rest = kept("e_words_rest", [P, G, 2 * (N - NT)], U8)
         e_scales_first = kept("e_scales_first", [P, G, NT], U8)
         e_scales_rest = kept("e_scales_rest", [P, G, N - NT], U8)
-        a_words = [kept("a_words%d" % nt, [P, G, NT], U32) for nt in range(NTILES)]
+        a_words = [kept("a_words%d" % h, [P, G, NH], U32) for h in range(2)]
         a_scales = kept("a_scales", [P, N], U8)
-        v_raw = [kept("v_raw%d" % c, [P, PACK, NT], BF16) for c in range(len(chunks))]
-        v_codes = [kept("v_codes%d" % c, [P, NT], U32) for c in range(len(chunks))]
-        v_scales = [kept("v_scales%d" % c, [P, NT], U8) for c in range(len(chunks))]
-        acc = {(nt, m): kept("acc%d_%d" % (nt, m), [P, NT], F32) for nt in range(NTILES) for m in range(MT)}
+        v_raw = [kept("v_raw%d" % c, [P, PACK, NH], BF16) for c in range(2 * G)]
+        v_codes = [kept("v_codes%d" % c, [P, NH], U32) for c in range(2 * G)]
+        v_scales = [kept("v_scales%d" % c, [P, NH], U8) for c in range(2 * G)]
+        acc = [kept("acc%d" % pair, [P, 2, N], F32) for pair in range(MT // 2)]
         d_sorted, d_grp, v_grp, expo = {}, {}, {}, {}
 
         def load_d(m, k0, k1):
@@ -95,9 +95,9 @@ def tile_ancestry_adjusted_scores_s10_kernel(
                 src = effect_scales[:, r:16:4, n0:n1].rearrange("g q n -> q g n")
                 nc.sync.dma_start(out=plane[r:P:32, :, :].bitcast(I32), in_=src.bitcast(I32))
 
-        def load_a(nt, g0, g1):
-            src = ancestry_words[g0:g1, :, cols(nt), :].rearrange("g p n t -> p g (n t)")
-            nc.sync.dma_start(out=a_words[nt][:, g0:g1, :].bitcast(I32), in_=src.bitcast(I32))
+        def load_a(h, g0, g1):
+            src = ancestry_words[g0:g1, :, h * NH : (h + 1) * NH, :].rearrange("g p n t -> p g (n t)")
+            nc.sync.dma_start(out=a_words[h][:, g0:g1, :].bitcast(I32), in_=src.bitcast(I32))
 
         def load_a_scales():
             for q in range(4):
@@ -105,8 +105,8 @@ def tile_ancestry_adjusted_scores_s10_kernel(
                 nc.sync.dma_start(out=a_scales[32 * q : 32 * q + 16, :].bitcast(I32), in_=src.bitcast(I32))
 
         def load_v(c):
-            nt, g = chunks[c]
-            src = spread[g * KP : (g + 1) * KP, cols(nt)].rearrange("(p j) n -> p j n", j=PACK)
+            h, g = divmod(c, G)
+            src = spread[g * KP : (g + 1) * KP, h * NH : (h + 1) * NH].rearrange("(p j) n -> p j n", j=PACK)
             nc.sync.dma_start(out=v_raw[c][:], in_=src)
 
         def load_offset():
@@ -170,38 +170,38 @@ def tile_ancestry_adjusted_scores_s10_kernel(
                 in_=d_grp[m, g][:],
             )
 
+
         def interleave(engine_copy, c, n0, n1):
-            if c not in v_grp:
-                v_grp[c] = ring.tile(
-                    [P, NT, PACK], BF16, name="v_grp%d" % c, tag="v_grp", bufs=G + 1, align_bytes=64
-                )
+            key = (c, n0 >= NT)
+            base_col = NT if n0 >= NT else 0
+            if key not in v_grp:
+                if n0 >= NT:
+                    v_grp[key] = ring.tile([P, NY, PACK], BF16, name="v_narrow%d" % c, tag="v_narrow", bufs=4, align_bytes=64)
+                else:
+                    v_grp[key] = ring.tile([P, NT, PACK], BF16, name="v_wide%d" % c, tag="v_wide", bufs=4, align_bytes=64)
             engine_copy(
-                out=v_grp[c][:, n0:n1, :].rearrange("p (c i) t -> p c t i", i=4),
+                out=v_grp[key][:, n0 - base_col : n1 - base_col, :].rearrange("p (c i) t -> p c t i", i=4),
                 in_=v_raw[c][:, :, n0:n1].rearrange("p t (c i) -> p c t i", i=4),
             )
 
-        def quantize_v(c):
+        def quantize_v(c, part):
+            n0, n1 = part
             nc.vector.quantize_mx(
-                out=v_codes[c][:].bitcast(FP8X4),
-                scales=v_scales[c][:],
-                in_=v_grp[c][:].rearrange("p n t -> p (n t)"),
+                out=v_codes[c][:, n0:n1].bitcast(FP8X4),
+                scales=v_scales[c][:, n0:n1],
+                in_=v_grp[c, n0 >= NT][:].rearrange("p n t -> p (n t)"),
             )
 
-        def product(m, width, operand, bank=None, passes=range(G)):
-            if bank is None:
-                bank = next_bank()
-            for g in passes:
-                rhs, rhs_scale = operand(g)
-                nc.tensor.matmul_mx(
-                    out=bank[:, 0:width],
-                    lhsT=d_codes[m][:, g * P : (g + 1) * P].bitcast(FP8X4),
-                    lhsT_scale=d_scales[m][:, g * P : (g + 1) * P],
-                    rhs=rhs,
-                    rhs_scale=rhs_scale,
-                    start=(g == 0),
-                    stop=(g == G - 1),
-                )
-            return bank
+        def one_pass(dst, m, g, rhs, rhs_scale, start, stop):
+            nc.tensor.matmul_mx(
+                out=dst,
+                lhsT=d_codes[m][:, g * P : (g + 1) * P].bitcast(FP8X4),
+                lhsT_scale=d_scales[m][:, g * P : (g + 1) * P],
+                rhs=rhs,
+                rhs_scale=rhs_scale,
+                start=start,
+                stop=stop,
+            )
 
         def effect_operand(nt, g):
             if nt == 0:
@@ -209,82 +209,80 @@ def tile_ancestry_adjusted_scores_s10_kernel(
             n0 = (nt - 1) * NT
             return e_words_rest[:, g, 2 * n0 : 2 * (n0 + NT)].bitcast(FP4X4), e_scales_rest[:, g, n0 : n0 + NT]
 
-        def effect_passes(nt, m, bank=None, passes=range(G)):
-            return product(m, NT, lambda g: effect_operand(nt, g), bank, passes)
+        def ancestry_operand(h, g, n0, n1):
+            return a_words[h][:, g, n0:n1].bitcast(FP8X4), a_scales[4 * g :, h * NH + n0 : h * NH + n1]
 
-        def park(nt, m, raw):
-            nc.scalar.copy(out=acc[nt, m][:], in_=raw[:])
+        def spread_operand(h, g, n0, n1):
+            return v_codes[h * G + g][:, n0:n1].bitcast(FP8X4), v_scales[h * G + g][:, n0:n1]
 
-        def effect_product(nt, m):
-            park(nt, m, effect_passes(nt, m))
-
-        def ancestry_passes(nt, m, n0, n1, bank=None, passes=range(G)):
-            return product(
-                m,
-                n1 - n0,
-                lambda g: (a_words[nt][:, g, n0:n1].bitcast(FP8X4), a_scales[4 * g :, nt * NT + n0 : nt * NT + n1]),
-                bank,
-                passes,
-            )
-
-        def ancestry_tile(nt):
-            open_banks = [ancestry_passes(nt, m, 0, NT, None, range(G // 2)) for m in range(MT)]
-            return [ancestry_passes(nt, m, 0, NT, open_banks[m], range(G // 2, G)) for m in range(MT)]
-
-        def subtract(nt, m, n0, n1, mean):
-            part = acc[nt, m][:, n0:n1]
-            nc.vector.tensor_tensor(out=part, in0=part, in1=mean[:, 0 : n1 - n0], op=ALU.subtract)
-
-        def ancestry_product(nt, m, n0, n1):
-            subtract(nt, m, n0, n1, ancestry_passes(nt, m, n0, n1))
-
-        def spread_passes(nt, m, bank, passes):
-            return product(
-                m, NT, lambda g: (v_codes[nt * G + g][:].bitcast(FP8X4), v_scales[nt * G + g][:]), bank, passes
-            )
-
-        def spread_half(nt, m, n0, n1):
-            bank = next_bank()
-            product(
-                m,
-                n1 - n0,
-                lambda g: (v_codes[nt * G + g][:, n0:n1].bitcast(FP8X4), v_scales[nt * G + g][:, n0:n1]),
-                bank[:, n0:n1],
-            )
+        def effect_passes(nt, m, bank, passes):
+            for g in passes:
+                one_pass(bank[:], m, g, *effect_operand(nt, g), g == 0, g == G - 1)
             return bank
 
-        def spread_product(nt, m, parts):
-            add_offset(nt, m, spread_passes(nt, m, None, range(G)), parts)
+        def wide_passes(operand, h, m, bank, passes):
+            for g in passes:
+                one_pass(bank[:], m, g, *operand(h, g, 0, NT), g == 0, g == G - 1)
+            return bank
 
-        def spread_pair(nt):
-            open_banks = [spread_passes(nt, m, None, range(G - 1)) for m in (0, 1)]
-            return [spread_passes(nt, m, open_banks[m], [G - 1]) for m in (0, 1)]
+        def narrow_passes(operand, h, pair, bank, passes):
+            for g in passes:
+                for i in range(2):
+                    dst = bank[:, i * NY : (i + 1) * NY]
+                    one_pass(dst, 2 * pair + i, g, *operand(h, g, NT, NH), g == 0 and i == 0, g == G - 1 and i == 1)
+            return bank
 
-        def add_offset(nt, m, sums, parts):
-            if (nt, m) not in expo:
-                expo[nt, m] = ring.tile([P, NT], F32, name="expo%d_%d" % (nt, m), tag="expo", bufs=2 * MT + 2)
-            for n0, n1 in parts:
-                nc.vector.tensor_tensor(
-                    out=expo[nt, m][:, n0:n1],
-                    in0=sums[:, n0:n1],
-                    in1=off_all[:, nt * NT + n0 : nt * NT + n1],
-                    op=ALU.add,
-                )
+        def piece_passes(operand, h, m, n0, n1):
+            bank = next_bank()
+            for g in range(G):
+                one_pass(bank[:, 0 : n1 - n0], m, g, *operand(h, g, n0, n1), g == 0, g == G - 1)
+            return bank
 
-        def exponential(nt, m, n0, n1):
-            part = expo[nt, m][:, n0:n1]
-            nc.scalar.activation(out=part, in_=part, func=EXP)
+        def park(nt, m, raw):
+            nc.scalar.copy(out=acc[m // 2][:, m % 2, nt * NT : (nt + 1) * NT], in_=raw[:])
 
-        def multiply(engine, nt, m, n0, n1):
-            part = acc[nt, m][:, n0:n1]
-            engine.tensor_tensor(out=part, in0=part, in1=expo[nt, m][:, n0:n1], op=ALU.mult)
+        def wide(h, m):
+            return (h, m // 2, m % 2, m % 2 + 1, 0, NT)
 
-        def store(nt, m, n0, n1):
-            nc.sync.dma_start(out=out[m * P : (m + 1) * P, nt * NT + n0 : nt * NT + n1], in_=acc[nt, m][:, n0:n1])
+        def wide_pair(h, pair):
+            return (h, pair, 0, 2, 0, NT)
 
-        def finish(engine, nt, m, n0, n1):
-            multiply(engine, nt, m, n0, n1)
-            store(nt, m, n0, n1)
+        def narrow(h, pair):
+            return (h, pair, 0, 2, NT, NH)
+
+        def of_acc(part):
+            h, pair, i0, i1, n0, n1 = part
+            return acc[pair][:, i0:i1, h * NH + n0 : h * NH + n1]
+
+        def of_expo(part):
+            h, pair, i0, i1, n0, n1 = part
+            if (h, pair) not in expo:
+                expo[h, pair] = shared("expo%d_%d" % (h, pair), [P, 2, NH], F32)
+            return expo[h, pair][:, i0:i1, n0:n1]
+
+        def of_bank(part, bank):
+            h, pair, i0, i1, n0, n1 = part
+            return bank[:, 0 : (i1 - i0) * (n1 - n0)].rearrange("p (i n) -> p i n", i=i1 - i0)
+
+        def add_offset(part, bank):
+            h, pair, i0, i1, n0, n1 = part
+            row = off_all[:, h * NH + n0 : h * NH + n1].unsqueeze(1).to_broadcast([P, i1 - i0, n1 - n0])
+            nc.vector.tensor_tensor(out=of_expo(part), in0=of_bank(part, bank), in1=row, op=ALU.add)
+
+        def exponential(part):
+            nc.scalar.activation(out=of_expo(part), in_=of_expo(part), func=EXP)
+
+        def subtract(part, bank):
+            nc.vector.tensor_tensor(out=of_acc(part), in0=of_acc(part), in1=of_bank(part, bank), op=ALU.subtract)
+
+        def multiply(engine, part):
+            engine.tensor_tensor(out=of_acc(part), in0=of_acc(part), in1=of_expo(part), op=ALU.mult)
+
+        def store(m, n0, n1):
+            nc.sync.dma_start(out=out[m * P : (m + 1) * P, n0:n1], in_=acc[m // 2][:, m % 2, n0:n1])
+
+        on_vector, on_scalar = nc.vector.tensor_copy, nc.scalar.copy
+        X, Y = (0, NT), (NT, NH)
 
         load_offset()
         load_d_halves(0)
@@ -319,19 +317,14 @@ def tile_ancestry_adjusted_scores_s10_kernel(
             for g in range(G):
                 quantize_d(m, g)
         clear(a_scales)
-        load_v(6)
         load_a_scales()
         load_a(0, 0, G // 2)
-        load_v(7)
         load_a(0, G // 2, G)
-        for c in (8, 9):
+        for c in range(G + 2, 2 * G):
             load_v(c)
         load_a(1, 0, G // 2)
-        load_v(10)
-        load_v(11)
         load_a(1, G // 2, G)
-        load_a(2, 0, G)
-        first_two = [effect_passes(0, m) for m in (0, 1)]
+        first_two = [effect_passes(0, m, next_bank(), range(G)) for m in (0, 1)]
         park(0, 0, first_two[0])
         for m in (2, 3):
             for g in range(G):
@@ -344,94 +337,115 @@ def tile_ancestry_adjusted_scores_s10_kernel(
             for g in passes:
                 quantize_d(3, g)
         park(0, 1, first_two[1])
-
-        on_vector, on_scalar = nc.vector.tensor_copy, nc.scalar.copy
-        whole, low, high = (0, NT), (0, NT // 2), (NT // 2, NT)
-        effect_product(0, 2)
+        park(0, 2, effect_passes(0, 2, next_bank(), range(G)))
         pass_over_bank()
-        effect_product(0, 3)
-        banks = [effect_passes(1, m, None, range(G // 2)) for m in range(MT)]
-        interleave(on_vector, 0, *whole)
-        interleave(on_vector, 1, *high)
-        quantize_v(0)
-        interleave(on_scalar, 1, *low)
-        interleave(on_vector, 2, *whole)
-        quantize_v(1)
+        park(0, 3, effect_passes(0, 3, next_bank(), range(G)))
+
+        banks = [effect_passes(1, m, next_bank(), range(G // 2)) for m in range(MT)]
+        interleave(on_scalar, 0, *Y)
         for m in range(MT):
             park(1, m, effect_passes(1, m, banks[m], range(G // 2, G)))
-        interleave(on_scalar, 3, *low)
-        interleave(on_vector, 3, *high)
-        quantize_v(2)
-        for m in range(MT):
-            effect_product(2, m)
             if m == 1:
-                interleave(on_scalar, 4, *low)
-        interleave(on_vector, 4, *high)
-        quantize_v(3)
-        interleave(on_vector, 5, *whole)
-        quantize_v(4)
+                interleave(on_scalar, 1, *Y)
+        for m in range(MT):
+            park(2, m, effect_passes(2, m, next_bank(), range(G)))
+            if m in (0, 2):
+                interleave(on_scalar, 2 + m // 2, *Y)
+        interleave(on_vector, 0, *X)
+        for c in range(1, G):
+            interleave(on_vector, c, *X)
+            quantize_v(c - 1, X)
+            quantize_v(c - 1, Y)
+        interleave(on_scalar, 4, *Y)
+        interleave(on_scalar, 5, *X)
+        quantize_v(3, X)
+        quantize_v(3, Y)
+        interleave(on_vector, 4, *X)
+        interleave(on_vector, 5, *Y)
+        quantize_v(4, X)
+        quantize_v(4, Y)
 
-        interleave(on_scalar, 6, *low)
-        pair = spread_pair(0)
-        add_offset(0, 0, pair[0], [whole])
-        quantize_v(5)
-        add_offset(0, 1, pair[1], [whole])
-        interleave(on_vector, 6, *high)
+        parts = [wide(0, 0), wide(0, 1), narrow(0, 0), wide(0, 2), wide(0, 3), narrow(0, 1)]
+        banks = [next_bank() for part in parts]
+        for g in range(G):
+            for pair in range(2):
+                for i in range(2):
+                    wide_passes(spread_operand, 0, 2 * pair + i, banks[3 * pair + i], [g])
+                narrow_passes(spread_operand, 0, pair, banks[3 * pair + 2], [g])
+        for part, bank in zip(parts, banks):
+            add_offset(part, bank)
+            exponential(part)
+        quantize_v(5, X)
+        means = [next_bank() for i in range(3)]
+        for passes in (range(G // 2), range(G // 2, G)):
+            for m in (0, 1):
+                wide_passes(ancestry_operand, 0, m, means[m], passes)
+            narrow_passes(ancestry_operand, 0, 0, means[2], passes)
+        for m in (2, 3):
+            means.append(wide_passes(ancestry_operand, 0, m, next_bank(), range(G)))
+        means.append(narrow_passes(ancestry_operand, 0, 1, next_bank(), range(G)))
+        for i in range(2):
+            subtract(parts[i], means[i])
+        quantize_v(5, Y)
+        interleave(on_scalar, 6, *X)
+        interleave(on_scalar, 7, P, NT)
+        interleave(on_scalar, 6, *Y)
+        interleave(on_scalar, 7, *Y)
+        multiply(nc.gpsimd, wide_pair(0, 0))
+        subtract(parts[2], means[2])
+        subtract(parts[3], means[3])
+        quantize_v(6, X)
+        interleave(on_vector, 7, 0, P)
+        subtract(parts[4], means[4])
+        quantize_v(7, X)
+        multiply(nc.gpsimd, wide_pair(0, 1))
+
+        banks = [next_bank() for m in range(3)]
+        for g in range(G):
+            for m in range(3):
+                wide_passes(spread_operand, 1, m, banks[m], [g])
         for m in range(2):
-            exponential(0, m, *whole)
-        spread_product(0, 2, [whole])
-        spread_product(0, 3, [whole])
-        quantize_v(6)
-        interleave(on_scalar, 7, *low)
-        interleave(on_vector, 7, *high)
-        for m in range(2, MT):
-            exponential(0, m, *whole)
-        quantize_v(7)
-        means = ancestry_tile(0)
-        for m in range(MT):
-            subtract(0, m, *whole, means[m])
-            finish(nc.gpsimd, 0, m, *whole)
-        interleave(on_scalar, 8, *whole)
-        interleave(on_scalar, 9, *whole)
-        pair = spread_pair(1)
-        add_offset(1, 0, pair[0], [whole])
-        add_offset(1, 1, pair[1], [whole])
-        spread_product(1, 2, [whole])
-        spread_product(1, 3, [whole])
-        means = ancestry_tile(1)
-        interleave(on_scalar, 10, *low)
-        interleave(on_scalar, 11, *whole)
-        quantize_v(8)
-        interleave(on_vector, 10, *high)
-        quantize_v(9)
-        quantize_v(10)
-        subtract(1, 0, *whole, means[0])
-        quantize_v(11)
-        for m in range(MT):
-            exponential(1, m, *whole)
+            add_offset(wide(1, m), banks[m])
+            exponential(wide(1, m))
+        subtract(parts[5], means[5])
+        multiply(nc.vector, parts[2])
+        store(0, 0, NH)
+        store(1, 0, NH)
+        quantize_v(6, Y)
+        multiply(nc.vector, parts[5])
+        store(2, 0, NH)
+        store(3, 0, NH)
+        sums = banks[2]
+        means = [wide_passes(ancestry_operand, 1, m, next_bank(), range(G)) for m in range(3)]
+        subtract(wide(1, 0), means[0])
+        quantize_v(7, Y)
+        add_offset(wide(1, 2), sums)
+        exponential(wide(1, 2))
+        for m in range(3):
             if m > 0:
-                subtract(1, m, *whole, means[m])
-            finish(nc.gpsimd, 1, m, *whole)
-
-        nt, last = NTILES - 1, MT - 1
-        pair = spread_pair(nt)
-        for m in (0, 1):
-            add_offset(nt, m, pair[m], [whole])
-            exponential(nt, m, *whole)
-        ancestry_product(nt, 0, *whole)
-        ancestry_product(nt, 1, *whole)
-        finish(nc.vector, nt, 0, *whole)
-        spread_product(nt, 2, [whole])
-        exponential(nt, 2, *whole)
-        finish(nc.vector, nt, 1, *whole)
-        ancestry_product(nt, 2, *whole)
-        halves = [spread_half(nt, last, *half) for half in (low, high)]
-        add_offset(nt, last, halves[0], [low])
-        exponential(nt, last, *low)
-        finish(nc.vector, nt, 2, *whole)
-        add_offset(nt, last, halves[1], [high])
-        exponential(nt, last, *high)
-        for piece in (low, (NT // 2, 3 * NT // 4), (3 * NT // 4, NT)):
-            ancestry_product(nt, last, *piece)
-        for half in (low, high):
-            finish(nc.vector, nt, last, *half)
+                subtract(wide(1, m), means[m])
+            multiply(nc.gpsimd, wide(1, m))
+            store(m, NH, NH + NT)
+        add_offset(narrow(1, 0), narrow_passes(spread_operand, 1, 0, next_bank(), range(G)))
+        exponential(narrow(1, 0))
+        subtract(narrow(1, 0), narrow_passes(ancestry_operand, 1, 0, next_bank(), range(G)))
+        add_offset(wide(1, 3), wide_passes(spread_operand, 1, 3, next_bank(), range(G)))
+        exponential(wide(1, 3))
+        multiply(nc.vector, narrow(1, 0))
+        store(0, NH + NT, N)
+        store(1, NH + NT, N)
+        subtract(wide(1, 3), wide_passes(ancestry_operand, 1, 3, next_bank(), range(G)))
+        ends = [(1, 1, i, i + 1, NT, NH) for i in range(2)]
+        sums = [piece_passes(spread_operand, 1, 2 + i, NT, NH) for i in range(2)]
+        add_offset(ends[0], sums[0])
+        exponential(ends[0])
+        multiply(nc.vector, wide(1, 3))
+        store(3, NH, NH + NT)
+        add_offset(ends[1], sums[1])
+        exponential(ends[1])
+        subtract(ends[0], piece_passes(ancestry_operand, 1, 2, NT, NH))
+        for n0 in (NT, NT + P):
+            subtract((1, 1, 1, 2, n0, n0 + P), piece_passes(ancestry_operand, 1, 3, n0, n0 + P))
+        for i in range(2):
+            multiply(nc.vector, ends[i])
+            store(2 + i, NH + NT, N)

@@ -391,41 +391,42 @@ def tile_ancestry_adjusted_scores_s10_kernel(
         interleave(on_scalar, 7, P, NT)
         interleave(on_scalar, 6, *Y)
         interleave(on_scalar, 7, *Y)
-        multiply(nc.gpsimd, wide_pair(0, 0))
+        multiply(nc.vector, parts[0])
         subtract(parts[2], means[2])
+        multiply(nc.vector, parts[1])
         subtract(parts[3], means[3])
         quantize_v(6, X)
         interleave(on_vector, 7, 0, P)
-        subtract(parts[4], means[4])
+        multiply(nc.vector, parts[2])
+        store(0, 0, NH)
+        store(1, 0, NH)
         quantize_v(7, X)
+        subtract(parts[5], means[5])
+        subtract(parts[4], means[4])
+        multiply(nc.vector, parts[5])
         multiply(nc.gpsimd, wide_pair(0, 1))
+        store(2, 0, NH)
+        store(3, 0, NH)
 
         banks = [next_bank() for m in range(3)]
         for g in range(G):
             for m in range(3):
                 wide_passes(spread_operand, 1, m, banks[m], [g])
-        for m in range(2):
+        for m in range(3):
             add_offset(wide(1, m), banks[m])
             exponential(wide(1, m))
-        subtract(parts[5], means[5])
-        multiply(nc.vector, parts[2])
-        store(0, 0, NH)
-        store(1, 0, NH)
-        quantize_v(6, Y)
-        multiply(nc.vector, parts[5])
-        store(2, 0, NH)
-        store(3, 0, NH)
-        sums = banks[2]
         means = [wide_passes(ancestry_operand, 1, m, next_bank(), range(G)) for m in range(3)]
-        subtract(wide(1, 0), means[0])
+        for m in range(2):
+            subtract(wide(1, m), means[m])
+        quantize_v(6, Y)
         quantize_v(7, Y)
-        add_offset(wide(1, 2), sums)
-        exponential(wide(1, 2))
-        for m in range(3):
-            if m > 0:
-                subtract(wide(1, m), means[m])
-            multiply(nc.gpsimd, wide(1, m))
-            store(m, NH, NH + NT)
+        multiply(nc.vector, wide(1, 0))
+        store(0, NH, NH + NT)
+        subtract(wide(1, 2), means[2])
+        multiply(nc.vector, wide(1, 1))
+        store(1, NH, NH + NT)
+        multiply(nc.gpsimd, wide(1, 2))
+        store(2, NH, NH + NT)
         add_offset(narrow(1, 0), narrow_passes(spread_operand, 1, 0, next_bank(), range(G)))
         exponential(narrow(1, 0))
         subtract(narrow(1, 0), narrow_passes(ancestry_operand, 1, 0, next_bank(), range(G)))

@@ -324,7 +324,7 @@ def tile_ancestry_adjusted_scores_s10_kernel(
             load_v(c)
         load_a(1, 0, G // 2)
         load_a(1, G // 2, G)
-        first_two = [effect_passes(0, m, next_bank(), range(G)) for m in (0, 1)]
+        first_two = [effect_passes(0, m, next_bank(), range(G - m)) for m in (0, 1)]
         park(0, 0, first_two[0])
         for m in (2, 3):
             for g in range(G):
@@ -336,7 +336,7 @@ def tile_ancestry_adjusted_scores_s10_kernel(
             transpose_d(3, passes)
             for g in passes:
                 quantize_d(3, g)
-        park(0, 1, first_two[1])
+        park(0, 1, effect_passes(0, 1, first_two[1], [G - 1]))
         park(0, 2, effect_passes(0, 2, next_bank(), range(G)))
         pass_over_bank()
         park(0, 3, effect_passes(0, 3, next_bank(), range(G)))

@@ -99,10 +99,10 @@ def tile_ancestry_adjusted_scores_s10_kernel(
             src = ancestry_words[g0:g1, :, h * NH : (h + 1) * NH, :].rearrange("g p n t -> p g (n t)")
             nc.sync.dma_start(out=a_words[h][:, g0:g1, :].bitcast(I32), in_=src.bitcast(I32))
 
-        def load_a_scales():
+        def load_a_scales(h):
             for q in range(4):
-                src = ancestry_scales[:, 4 * q : 4 * q + 4, :]
-                nc.sync.dma_start(out=a_scales[32 * q : 32 * q + 16, :].bitcast(I32), in_=src.bitcast(I32))
+                src = ancestry_scales[:, 4 * q : 4 * q + 4, h * NH : (h + 1) * NH]
+                nc.sync.dma_start(out=a_scales[32 * q : 32 * q + 16, h * NH : (h + 1) * NH].bitcast(I32), in_=src.bitcast(I32))
 
         def load_v(c):
             h, g = divmod(c, G)
@@ -281,6 +281,10 @@ def tile_ancestry_adjusted_scores_s10_kernel(
         def store(m, n0, n1):
             nc.sync.dma_start(out=out[m * P : (m + 1) * P, n0:n1], in_=acc[m // 2][:, m % 2, n0:n1])
 
+        def store_pair(pair, n0, n1):
+            rows = out[2 * pair * P : 2 * (pair + 1) * P, n0:n1].rearrange("(i p) n -> p i n", p=P)
+            nc.sync.dma_start(out=rows, in_=acc[pair][:, :, n0:n1])
+
         on_vector, on_scalar = nc.vector.tensor_copy, nc.scalar.copy
         X, Y = (0, NT), (NT, NH)
 
@@ -317,11 +321,12 @@ def tile_ancestry_adjusted_scores_s10_kernel(
             for g in range(G):
                 quantize_d(m, g)
         clear(a_scales)
-        load_a_scales()
+        load_a_scales(0)
         load_a(0, 0, G // 2)
         load_a(0, G // 2, G)
         for c in range(G + 2, 2 * G):
             load_v(c)
+        load_a_scales(1)
         load_a(1, 0, G // 2)
         load_a(1, G // 2, G)
         first_two = [effect_passes(0, m, next_bank(), range(G - m)) for m in (0, 1)]
@@ -398,15 +403,13 @@ def tile_ancestry_adjusted_scores_s10_kernel(
         quantize_v(6, X)
         interleave(on_vector, 7, 0, P)
         multiply(nc.vector, parts[2])
-        store(0, 0, NH)
-        store(1, 0, NH)
+        store_pair(0, 0, NH)
         quantize_v(7, X)
         subtract(parts[5], means[5])
         subtract(parts[4], means[4])
         multiply(nc.vector, parts[5])
         multiply(nc.gpsimd, wide_pair(0, 1))
-        store(2, 0, NH)
-        store(3, 0, NH)
+        store_pair(1, 0, NH)
 
         banks = [next_bank() for m in range(3)]
         for g in range(G):
@@ -421,10 +424,9 @@ def tile_ancestry_adjusted_scores_s10_kernel(
         quantize_v(6, Y)
         quantize_v(7, Y)
         multiply(nc.vector, wide(1, 0))
-        store(0, NH, NH + NT)
         subtract(wide(1, 2), means[2])
         multiply(nc.vector, wide(1, 1))
-        store(1, NH, NH + NT)
+        store_pair(0, NH, NH + NT)
         multiply(nc.gpsimd, wide(1, 2))
         store(2, NH, NH + NT)
         add_offset(narrow(1, 0), narrow_passes(spread_operand, 1, 0, next_bank(), range(G)))
@@ -433,8 +435,7 @@ def tile_ancestry_adjusted_scores_s10_kernel(
         add_offset(wide(1, 3), wide_passes(spread_operand, 1, 3, next_bank(), range(G)))
         exponential(wide(1, 3))
         multiply(nc.vector, narrow(1, 0))
-        store(0, NH + NT, N)
-        store(1, NH + NT, N)
+        store_pair(0, NH + NT, N)
         subtract(wide(1, 3), wide_passes(ancestry_operand, 1, 3, next_bank(), range(G)))
         ends = [(1, 1, i, i + 1, NT, NH) for i in range(2)]
         sums = [piece_passes(spread_operand, 1, 2 + i, NT, NH) for i in range(2)]

@@ -25,6 +25,7 @@ NH = N // 2
 NY = NH - NT
 MT = M // P
 BANKS = 8
+SHARE = 192
 WARM_N = 256
 WARM_PASSES = (6, 4)
 
@@ -62,7 +63,8 @@ def tile_ancestry_adjusted_scores_s10_kernel(
         warm_out = kept("warm_out", [P, 1], F32)
         warm_codes = kept("warm_codes", [P, WARM_N], U32)
         warm_scales = kept("warm_scales", [P, WARM_N], U8)
-        off_rows = kept("off_rows", [P, 2, 16], BF16)
+        off_columns = kept("off_columns", [P, N // 2], F32)
+        off_repeated = kept("off_repeated", [P, N // 2], F32)
         off_all = kept("off_all", [P, N], BF16)
         d_raw = [shared("d_raw%d" % m, [P, K], BF16) for m in range(MT)]
         d_codes = [kept("d_codes%d" % m, [P, G * P], U32) for m in range(MT)]
@@ -110,7 +112,7 @@ def tile_ancestry_adjusted_scores_s10_kernel(
             nc.sync.dma_start(out=v_raw[c][:], in_=src)
 
         def load_offset():
-            nc.scalar.dma_start(out=off_rows[:, :, 0:6], in_=offset.rearrange("(h p c) -> p h c", h=2, p=P))
+            nc.scalar.dma_start(out=d_raw[0][0:P:32, 0:N], in_=offset.partition_broadcast(4))
 
         def clear(tile):
             nc.vector.memset(tile[:].bitcast(I32), 0)
@@ -128,16 +130,13 @@ def tile_ancestry_adjusted_scores_s10_kernel(
                     stop=(i == passes - 1),
                 )
 
-        def spread_offset(h):
-            bank = next_bank()
-            words = off_rows[:, h, 0:6].bitcast(F32)
-            for c in range(3):
-                nc.tensor.transpose(bank[:, c * P : (c + 1) * P], words[:, c : c + 1].to_broadcast([P, P]), ident[:])
-            dst = off_all[:].bitcast(F32)[:, h * 3 * P : (h + 1) * 3 * P]
-            nc.scalar.copy(
-                out=dst.rearrange("q (p c) -> q p c", c=3),
-                in_=bank[:, 0 : 3 * P].rearrange("q (c p) -> q p c", c=3),
+        def spread_offset():
+            nc.vector.transpose(out=off_columns[:], in_=d_raw[0][:, 0:N].bitcast(F32))
+            nc.vector.tensor_copy(
+                out=off_repeated[:].rearrange("p (b i) -> p b i", i=32),
+                in_=off_columns[:].rearrange("p (b i) -> p b i", i=32)[:, :, 0:1].to_broadcast([P, N // 64, 32]),
             )
+            nc.vector.transpose(out=off_all[:].bitcast(F32), in_=off_repeated[:])
 
         def sort_d(m, g):
             d_sorted[m, g] = ring.tile(
@@ -288,7 +287,6 @@ def tile_ancestry_adjusted_scores_s10_kernel(
         on_vector, on_scalar = nc.vector.tensor_copy, nc.scalar.copy
         X, Y = (0, NT), (NT, NH)
 
-        load_offset()
         load_d_halves(0)
         load_d_halves(1)
         load_e(e_words_first, 0, NT, 0, G // 2)
@@ -310,30 +308,22 @@ def tile_ancestry_adjusted_scores_s10_kernel(
                 transpose_d(m, [g])
             if m == 0:
                 clear(e_scales_rest)
+        load_offset()
         load_e_scales(e_scales_rest, NT, N)
         load_e(e_words_rest, NT, N, 0, G // 2)
         load_e(e_words_rest, NT, N, G // 2, G)
         for c in range(G + 2):
             load_v(c)
-        for h in range(2):
-            spread_offset(h)
         for m in (0, 1):
-            for g in range(G):
+            for g in range(G - m):
                 quantize_d(m, g)
-        clear(a_scales)
-        load_a_scales(0)
-        load_a(0, 0, G // 2)
-        load_a(0, G // 2, G)
-        for c in range(G + 2, 2 * G):
-            load_v(c)
-        load_a_scales(1)
-        load_a(1, 0, G // 2)
-        load_a(1, G // 2, G)
         first_two = [effect_passes(0, m, next_bank(), range(G - m)) for m in (0, 1)]
         park(0, 0, first_two[0])
-        for m in (2, 3):
-            for g in range(G):
-                sort_d(m, g)
+        for g in range(G):
+            sort_d(2, g)
+        quantize_d(1, G - 1)
+        for g in range(G):
+            sort_d(3, g)
         for g in range(G):
             transpose_d(2, [g])
             quantize_d(2, g)
@@ -356,6 +346,16 @@ def tile_ancestry_adjusted_scores_s10_kernel(
             park(2, m, effect_passes(2, m, next_bank(), range(G)))
             if m in (0, 2):
                 interleave(on_scalar, 2 + m // 2, *Y)
+        clear(a_scales)
+        load_a_scales(0)
+        load_a(0, 0, G // 2)
+        load_a(0, G // 2, G)
+        for c in range(G + 2, 2 * G):
+            load_v(c)
+        load_a_scales(1)
+        load_a(1, 0, G // 2)
+        load_a(1, G // 2, G)
+        spread_offset()
         interleave(on_vector, 0, *X)
         for c in range(1, G):
             interleave(on_vector, c, *X)
@@ -393,7 +393,7 @@ def tile_ancestry_adjusted_scores_s10_kernel(
             subtract(parts[i], means[i])
         quantize_v(5, Y)
         interleave(on_scalar, 6, *X)
-        interleave(on_scalar, 7, P, NT)
+        interleave(on_scalar, 7, SHARE, NT)
         interleave(on_scalar, 6, *Y)
         interleave(on_scalar, 7, *Y)
         multiply(nc.vector, parts[0])
@@ -401,7 +401,7 @@ def tile_ancestry_adjusted_scores_s10_kernel(
         multiply(nc.vector, parts[1])
         subtract(parts[3], means[3])
         quantize_v(6, X)
-        interleave(on_vector, 7, 0, P)
+        interleave(on_vector, 7, 0, SHARE)
         multiply(nc.vector, parts[2])
         store_pair(0, 0, NH)
         quantize_v(7, X)

@@ -25,7 +25,7 @@ NH = N // 2
 NY = NH - NT
 MT = M // P
 BANKS = 8
-SHARE = 192
+SHARE = 256
 WARM_N = 256
 WARM_PASSES = (6, 4)
 
@@ -366,7 +366,6 @@ def tile_ancestry_adjusted_scores_s10_kernel(
         quantize_v(3, X)
         quantize_v(3, Y)
         interleave(on_vector, 4, *X)
-        interleave(on_vector, 5, *Y)
         quantize_v(4, X)
         quantize_v(4, Y)
 
@@ -391,17 +390,17 @@ def tile_ancestry_adjusted_scores_s10_kernel(
         means.append(narrow_passes(ancestry_operand, 0, 1, next_bank(), range(G)))
         for i in range(2):
             subtract(parts[i], means[i])
-        quantize_v(5, Y)
         interleave(on_scalar, 6, *X)
         interleave(on_scalar, 7, SHARE, NT)
+        interleave(on_scalar, 5, *Y)
         interleave(on_scalar, 6, *Y)
         interleave(on_scalar, 7, *Y)
         multiply(nc.vector, parts[0])
+        multiply(nc.gpsimd, parts[1])
         subtract(parts[2], means[2])
-        multiply(nc.vector, parts[1])
         subtract(parts[3], means[3])
-        quantize_v(6, X)
         interleave(on_vector, 7, 0, SHARE)
+        quantize_v(6, X)
         multiply(nc.vector, parts[2])
         store_pair(0, 0, NH)
         quantize_v(7, X)
@@ -419,10 +418,10 @@ def tile_ancestry_adjusted_scores_s10_kernel(
             add_offset(wide(1, m), banks[m])
             exponential(wide(1, m))
         means = [wide_passes(ancestry_operand, 1, m, next_bank(), range(G)) for m in range(3)]
-        for m in range(2):
-            subtract(wide(1, m), means[m])
-        quantize_v(6, Y)
-        quantize_v(7, Y)
+        subtract(wide(1, 0), means[0])
+        for c in (5, 6, 7):
+            quantize_v(c, Y)
+        subtract(wide(1, 1), means[1])
         multiply(nc.vector, wide(1, 0))
         subtract(wide(1, 2), means[2])
         multiply(nc.vector, wide(1, 1))

@@ -81,8 +81,8 @@ def tile_ancestry_adjusted_scores_s10_kernel(
         acc = [kept("acc%d" % pair, [P, 2, N], F32) for pair in range(MT // 2)]
         d_sorted, d_grp, v_grp, expo = {}, {}, {}, {}
 
-        def load_d(m, k0, k1):
-            nc.sync.dma_start(out=d_raw[m][:, k0:k1], in_=dosage[m * P : (m + 1) * P, k0:k1])
+        def load_d(m, k0, k1, queue=nc.sync):
+            queue.dma_start(out=d_raw[m][:, k0:k1], in_=dosage[m * P : (m + 1) * P, k0:k1])
 
         def load_d_halves(m):
             load_d(m, 0, K // 2)
@@ -287,7 +287,8 @@ def tile_ancestry_adjusted_scores_s10_kernel(
         on_vector, on_scalar = nc.vector.tensor_copy, nc.scalar.copy
         X, Y = (0, NT), (NT, NH)
 
-        load_d_halves(0)
+        load_d(0, 0, K // 2, nc.scalar)
+        load_d(0, K // 2, K)
         load_d_halves(1)
         load_e(e_words_first, 0, NT, 0, G // 2)
         clear(warm_in)
@@ -308,17 +309,17 @@ def tile_ancestry_adjusted_scores_s10_kernel(
                 transpose_d(m, [g])
             if m == 0:
                 clear(e_scales_rest)
+        for m in (0, 1):
+            for g in range(G - m):
+                quantize_d(m, g)
+        first_two = [effect_passes(0, m, next_bank(), range(G - m)) for m in (0, 1)]
+        park(0, 0, first_two[0])
         load_offset()
         load_e_scales(e_scales_rest, NT, N)
         load_e(e_words_rest, NT, N, 0, G // 2)
         load_e(e_words_rest, NT, N, G // 2, G)
         for c in range(G + 2):
             load_v(c)
-        for m in (0, 1):
-            for g in range(G - m):
-                quantize_d(m, g)
-        first_two = [effect_passes(0, m, next_bank(), range(G - m)) for m in (0, 1)]
-        park(0, 0, first_two[0])
         for g in range(G):
             sort_d(2, g)
         quantize_d(1, G - 1)

from contextlib import ExitStack

import concourse.mybir as mybir
from concourse.masks import make_identity

M, K, N = 512, 2048, 1536
FLOPS = 3 * 2 * M * K * N

F32 = mybir.dt.float32
BF16 = mybir.dt.bfloat16
I32 = mybir.dt.int32
U32 = mybir.dt.uint32
U8 = mybir.dt.uint8
FP8X4 = mybir.dt.float8_e4m3fn_x4
FP4X4 = mybir.dt.float4_e2m1fn_x4
ALU = mybir.AluOpType
EXP = mybir.ActivationFunctionType.Exp

P = 128
PACK = 4
KP = P * PACK
G = K // KP
NT = 512
NH = N // 2
NY = NH - NT
MT = M // P
BANKS = 8
SHARE = 256
WARM_N = 256
WARM_PASSES = (6, 4)


def tile_ancestry_adjusted_scores_s10_kernel(
    tc, dosage, effect_words, effect_scales, ancestry_words, ancestry_scales, spread, offset, out
):
    nc = tc.nc
    with ExitStack() as ctx:
        keep = ctx.enter_context(tc.tile_pool(name="keep", bufs=1))
        ring = ctx.enter_context(tc.tile_pool(name="ring", bufs=1))
        psum = ctx.enter_context(tc.psum_pool(name="psum", bufs=1))
        ctx.enter_context(tc.manual_schedule())

        def kept(name, shape, dtype):
            return keep.tile(shape, dtype, name=name, align_bytes=64)

        banks_taken = []
        free_banks = list(range(BANKS))

        def pass_over_bank():
            free_banks.append(free_banks.pop(0))

        def next_bank():
            tag = free_banks.pop(0)
            free_banks.append(tag)
            banks_taken.append(tag)
            return psum.tile([P, NT], F32, name="bank_use%d" % len(banks_taken), tag="bank%d" % tag)

        def shared(name, shape, dtype):
            return ring.tile(shape, dtype, name=name, tag="shared", bufs=MT, align_bytes=64)

        ident = kept("ident", [P, P], F32)
        warm_in = kept("warm_in", [P, PACK * WARM_N], BF16)
        warm_out = kept("warm_out", [P, 1], F32)
        warm_codes = kept("warm_codes", [P, WARM_N], U32)
        warm_scales = kept("warm_scales", [P, WARM_N], U8)
        off_columns = kept("off_columns", [P, N // 2], F32)
        off_repeated = kept("off_repeated", [P, N // 2], F32)
        off_all = kept("off_all", [P, N], BF16)
        d_raw = [shared("d_raw%d" % m, [P, K], BF16) for m in range(MT)]
        d_codes = [kept("d_codes%d" % m, [P, G * P], U32) for m in range(MT)]
        d_scales = [kept("d_scales%d" % m, [P, G * P], U8) for m in range(MT)]
        e_words_first = kept("e_words_first", [P, G, 2 * NT], U8)
        e_words_rest = kept("e_words_rest", [P, G, 2 * (N - NT)], U8)
        e_scales_first = kept("e_scales_first", [P, G, NT], U8)
        e_scales_rest = kept("e_scales_rest", [P, G, N - NT], U8)
        a_words = [kept("a_words%d" % h, [P, G, NH], U32) for h in range(2)]
        a_scales = kept("a_scales", [P, N], U8)
        v_raw = [kept("v_raw%d" % c, [P, PACK, NH], BF16) for c in range(2 * G)]
        v_codes = [kept("v_codes%d" % c, [P, NH], U32) for c in range(2 * G)]
        v_scales = [kept("v_scales%d" % c, [P, NH], U8) for c in range(2 * G)]
        acc = [kept("acc%d" % pair, [P, 2, N], F32) for pair in range(MT // 2)]
        d_sorted, d_grp, v_grp, expo = {}, {}, {}, {}

        def load_d(m, k0, k1, queue=nc.sync):
            queue.dma_start(out=d_raw[m][:, k0:k1], in_=dosage[m * P : (m + 1) * P, k0:k1])

        def load_d_halves(m):
            load_d(m, 0, K // 2)
            load_d(m, K // 2, K)

        def load_e(words, n0, n1, g0, g1):
            src = effect_words[g0:g1, :, 2 * n0 : 2 * n1].rearrange("g p b -> p g b")
            nc.sync.dma_start(out=words[:, g0:g1, :].bitcast(I32), in_=src.bitcast(I32))

        def load_e_scales(plane, n0, n1):
            for r in range(4):
                src = effect_scales[:, r:16:4, n0:n1].rearrange("g q n -> q g n")
                nc.sync.dma_start(out=plane[r:P:32, :, :].bitcast(I32), in_=src.bitcast(I32))

        def load_a(h, g0, g1):
            src = ancestry_words[g0:g1, :, h * NH : (h + 1) * NH, :].rearrange("g p n t -> p g (n t)")
            nc.sync.dma_start(out=a_words[h][:, g0:g1, :].bitcast(I32), in_=src.bitcast(I32))

        def load_a_scales(h):
            for q in range(4):
                src = ancestry_scales[:, 4 * q : 4 * q + 4, h * NH : (h + 1) * NH]
                nc.sync.dma_start(out=a_scales[32 * q : 32 * q + 16, h * NH : (h + 1) * NH].bitcast(I32), in_=src.bitcast(I32))

        def load_v(c):
            h, g = divmod(c, G)
            src = spread[g * KP : (g + 1) * KP, h * NH : (h + 1) * NH].rearrange("(p j) n -> p j n", j=PACK)
            nc.sync.dma_start(out=v_raw[c][:], in_=src)

        def load_offset():
            nc.scalar.dma_start(out=d_raw[0][0:P:32, 0:N], in_=offset.partition_broadcast(4))

        def clear(tile):
            nc.vector.memset(tile[:].bitcast(I32), 0)

        def warm_up(passes):
            bank = next_bank()
            for i in range(passes):
                nc.tensor.matmul_mx(
                    out=bank[:, 0:WARM_N],
                    lhsT=warm_codes[:, 0:P].bitcast(FP8X4),
                    lhsT_scale=warm_scales[:, 0:P],
                    rhs=warm_codes[:].bitcast(FP8X4),
                    rhs_scale=warm_scales[:],
                    start=(i == 0),
                    stop=(i == passes - 1),
                )

        def spread_offset():
            nc.vector.transpose(out=off_columns[:], in_=d_raw[0][:, 0:N].bitcast(F32))
            nc.vector.tensor_copy(
                out=off_repeated[:].rearrange("p (b i) -> p b i", i=32),
                in_=off_columns[:].rearrange("p (b i) -> p b i", i=32)[:, :, 0:1].to_broadcast([P, N // 64, 32]),
            )
            nc.vector.transpose(out=off_all[:].bitcast(F32), in_=off_repeated[:])

        def sort_d(m, g):
            d_sorted[m, g] = ring.tile(
                [P, 2, P], F32, name="d_sorted%d_%d" % (m, g), tag="d_sorted", bufs=2 * G, align_bytes=64
            )
            nc.vector.tensor_copy(
                out=d_sorted[m, g][:],
                in_=d_raw[m][:].bitcast(F32)[:, 2 * P * g : 2 * P * (g + 1)].rearrange("r (p u) -> r u p", u=2),
            )

        def transpose_d(m, passes):
            bank = next_bank()
            for i, g in enumerate(passes):
                for u in range(2):
                    col = (2 * i + u) * P
                    nc.tensor.transpose(bank[:, col : col + P], d_sorted[m, g][:, u, :], ident[:])
            for i, g in enumerate(passes):
                d_grp[m, g] = ring.tile(
                    [P, KP], BF16, name="d_grp%d_%d" % (m, g), tag="d_grp", bufs=2 * G, align_bytes=64
                )
                nc.scalar.copy(
                    out=d_grp[m, g][:].bitcast(F32).rearrange("p (r u) -> p r u", u=2),
                    in_=bank[:, 2 * i * P : 2 * (i + 1) * P].rearrange("p (u r) -> p r u", u=2),
                )

        def quantize_d(m, g):
            nc.vector.quantize_mx(
                out=d_codes[m][:, g * P : (g + 1) * P].bitcast(FP8X4),
                scales=d_scales[m][:, g * P : (g + 1) * P],
                in_=d_grp[m, g][:],
            )


        def interleave(engine_copy, c, n0, n1):
            key = (c, n0 >= NT)
            base_col = NT if n0 >= NT else 0
            if key not in v_grp:
                if n0 >= NT:
                    v_grp[key] = ring.tile([P, NY, PACK], BF16, name="v_narrow%d" % c, tag="v_narrow", bufs=4, align_bytes=64)
                else:
                    v_grp[key] = ring.tile([P, NT, PACK], BF16, name="v_wide%d" % c, tag="v_wide", bufs=4, align_bytes=64)
            engine_copy(
                out=v_grp[key][:, n0 - base_col : n1 - base_col, :].rearrange("p (c i) t -> p c t i", i=4),
                in_=v_raw[c][:, :, n0:n1].rearrange("p t (c i) -> p c t i", i=4),
            )

        def quantize_v(c, part):
            n0, n1 = part
            nc.vector.quantize_mx(
                out=v_codes[c][:, n0:n1].bitcast(FP8X4),
                scales=v_scales[c][:, n0:n1],
                in_=v_grp[c, n0 >= NT][:].rearrange("p n t -> p (n t)"),
            )

        def one_pass(dst, m, g, rhs, rhs_scale, start, stop):
            nc.tensor.matmul_mx(
                out=dst,
                lhsT=d_codes[m][:, g * P : (g + 1) * P].bitcast(FP8X4),
                lhsT_scale=d_scales[m][:, g * P : (g + 1) * P],
                rhs=rhs,
                rhs_scale=rhs_scale,
                start=start,
                stop=stop,
            )

        def effect_operand(nt, g):
            if nt == 0:
                return e_words_first[:, g, :].bitcast(FP4X4), e_scales_first[:, g, :]
            n0 = (nt - 1) * NT
            return e_words_rest[:, g, 2 * n0 : 2 * (n0 + NT)].bitcast(FP4X4), e_scales_rest[:, g, n0 : n0 + NT]

        def ancestry_operand(h, g, n0, n1):
            return a_words[h][:, g, n0:n1].bitcast(FP8X4), a_scales[4 * g :, h * NH + n0 : h * NH + n1]

        def spread_operand(h, g, n0, n1):
            return v_codes[h * G + g][:, n0:n1].bitcast(FP8X4), v_scales[h * G + g][:, n0:n1]

        def effect_passes(nt, m, bank, passes):
            for g in passes:
                one_pass(bank[:], m, g, *effect_operand(nt, g), g == 0, g == G - 1)
            return bank

        def wide_passes(operand, h, m, bank, passes):
            for g in passes:
                one_pass(bank[:], m, g, *operand(h, g, 0, NT), g == 0, g == G - 1)
            return bank

        def narrow_passes(operand, h, pair, bank, passes):
            for g in passes:
                for i in range(2):
                    dst = bank[:, i * NY : (i + 1) * NY]
                    one_pass(dst, 2 * pair + i, g, *operand(h, g, NT, NH), g == 0 and i == 0, g == G - 1 and i == 1)
            return bank

        def piece_passes(operand, h, m, n0, n1):
            bank = next_bank()
            for g in range(G):
                one_pass(bank[:, 0 : n1 - n0], m, g, *operand(h, g, n0, n1), g == 0, g == G - 1)
            return bank

        def park(nt, m, raw):
            nc.scalar.copy(out=acc[m // 2][:, m % 2, nt * NT : (nt + 1) * NT], in_=raw[:])

        def wide(h, m):
            return (h, m // 2, m % 2, m % 2 + 1, 0, NT)

        def wide_pair(h, pair):
            return (h, pair, 0, 2, 0, NT)

        def narrow(h, pair):
            return (h, pair, 0, 2, NT, NH)

        def of_acc(part):
            h, pair, i0, i1, n0, n1 = part
            return acc[pair][:, i0:i1, h * NH + n0 : h * NH + n1]

        def of_expo(part):
            h, pair, i0, i1, n0, n1 = part
            if (h, pair) not in expo:
                expo[h, pair] = shared("expo%d_%d" % (h, pair), [P, 2, NH], F32)
            return expo[h, pair][:, i0:i1, n0:n1]

        def of_bank(part, bank):
            h, pair, i0, i1, n0, n1 = part
            return bank[:, 0 : (i1 - i0) * (n1 - n0)].rearrange("p (i n) -> p i n", i=i1 - i0)

        def add_offset(part, bank):
            h, pair, i0, i1, n0, n1 = part
            row = off_all[:, h * NH + n0 : h * NH + n1].unsqueeze(1).to_broadcast([P, i1 - i0, n1 - n0])
            nc.vector.tensor_tensor(out=of_expo(part), in0=of_bank(part, bank), in1=row, op=ALU.add)

        def exponential(part):
            nc.scalar.activation(out=of_expo(part), in_=of_expo(part), func=EXP)

        def subtract(part, bank):
            nc.vector.tensor_tensor(out=of_acc(part), in0=of_acc(part), in1=of_bank(part, bank), op=ALU.subtract)

        def multiply(engine, part):
            engine.tensor_tensor(out=of_acc(part), in0=of_acc(part), in1=of_expo(part), op=ALU.mult)

        def store(m, n0, n1):
            nc.sync.dma_start(out=out[m * P : (m + 1) * P, n0:n1], in_=acc[m // 2][:, m % 2, n0:n1])

        def store_pair(pair, n0, n1):
            rows = out[2 * pair * P : 2 * (pair + 1) * P, n0:n1].rearrange("(i p) n -> p i n", p=P)
            nc.sync.dma_start(out=rows, in_=acc[pair][:, :, n0:n1])

        on_vector, on_scalar = nc.vector.tensor_copy, nc.scalar.copy
        X, Y = (0, NT), (NT, NH)

        load_d(0, 0, K // 2, nc.scalar)
        load_d(0, K // 2, K)
        load_d_halves(1)
        load_e(e_words_first, 0, NT, 0, G // 2)
        clear(warm_in)
        clear(e_scales_first)
        nc.vector.quantize_mx(out=warm_codes[:].bitcast(FP8X4), scales=warm_scales[:], in_=warm_in[:])
        nc.vector.memset(ident[:], 0.0)
        make_identity(nc, ident[:], nomemset=True)
        nc.scalar.activation(out=warm_out[:], in_=warm_in[:, 0:1], func=EXP)
        load_e_scales(e_scales_first, 0, NT)
        load_e(e_words_first, 0, NT, G // 2, G)
        load_d(2, 0, K)
        load_d_halves(3)

        for m in (0, 1):
            warm_up(WARM_PASSES[m])
            for g in range(G):
                sort_d(m, g)
                transpose_d(m, [g])
            if m == 0:
                clear(e_scales_rest)
        for m in (0, 1):
            for g in range(G - m):
                quantize_d(m, g)
        first_two = [effect_passes(0, m, next_bank(), range(G - m)) for m in (0, 1)]
        park(0, 0, first_two[0])
        load_offset()
        load_e_scales(e_scales_rest, NT, N)
        load_e(e_words_rest, NT, N, 0, G // 2)
        load_e(e_words_rest, NT, N, G // 2, G)
        for c in range(G + 2):
            load_v(c)
        for g in range(G):
            sort_d(2, g)
        quantize_d(1, G - 1)
        for g in range(G):
            sort_d(3, g)
        for g in range(G):
            transpose_d(2, [g])
            quantize_d(2, g)
        for passes in ([0, 1], [2, 3]):
            transpose_d(3, passes)
            for g in passes:
                quantize_d(3, g)
        park(0, 1, effect_passes(0, 1, first_two[1], [G - 1]))
        park(0, 2, effect_passes(0, 2, next_bank(), range(G)))
        pass_over_bank()
        park(0, 3, effect_passes(0, 3, next_bank(), range(G)))

        banks = [effect_passes(1, m, next_bank(), range(G // 2)) for m in range(MT)]
        interleave(on_scalar, 0, *Y)
        for m in range(MT):
            park(1, m, effect_passes(1, m, banks[m], range(G // 2, G)))
            if m == 1:
                interleave(on_scalar, 1, *Y)
        for m in range(MT):
            park(2, m, effect_passes(2, m, next_bank(), range(G)))
            if m in (0, 2):
                interleave(on_scalar, 2 + m // 2, *Y)
        clear(a_scales)
        load_a_scales(0)
        load_a(0, 0, G // 2)
        load_a(0, G // 2, G)
        for c in range(G + 2, 2 * G):
            load_v(c)
        load_a_scales(1)
        load_a(1, 0, G // 2)
        load_a(1, G // 2, G)
        spread_offset()
        interleave(on_vector, 0, *X)
        for c in range(1, G):
            interleave(on_vector, c, *X)
            quantize_v(c - 1, X)
            quantize_v(c - 1, Y)
        interleave(on_scalar, 4, *Y)
        interleave(on_scalar, 5, *X)
        quantize_v(3, X)
        quantize_v(3, Y)
        interleave(on_vector, 4, *X)
        quantize_v(4, X)
        quantize_v(4, Y)

        parts = [wide(0, 0), wide(0, 1), narrow(0, 0), wide(0, 2), wide(0, 3), narrow(0, 1)]
        banks = [next_bank() for part in parts]
        for g in range(G):
            for pair in range(2):
                for i in range(2):
                    wide_passes(spread_operand, 0, 2 * pair + i, banks[3 * pair + i], [g])
                narrow_passes(spread_operand, 0, pair, banks[3 * pair + 2], [g])
        for part, bank in zip(parts, banks):
            add_offset(part, bank)
            exponential(part)
        quantize_v(5, X)
        means = [next_bank() for i in range(3)]
        for passes in (range(G // 2), range(G // 2, G)):
            for m in (0, 1):
                wide_passes(ancestry_operand, 0, m, means[m], passes)
            narrow_passes(ancestry_operand, 0, 0, means[2], passes)
        for m in (2, 3):
            means.append(wide_passes(ancestry_operand, 0, m, next_bank(), range(G)))
        means.append(narrow_passes(ancestry_operand, 0, 1, next_bank(), range(G)))
        for i in range(2):
            subtract(parts[i], means[i])
        interleave(on_scalar, 6, *X)
        interleave(on_scalar, 7, SHARE, NT)
        interleave(on_scalar, 5, *Y)
        interleave(on_scalar, 6, *Y)
        interleave(on_scalar, 7, *Y)
        multiply(nc.vector, parts[0])
        multiply(nc.gpsimd, parts[1])
        subtract(parts[2], means[2])
        subtract(parts[3], means[3])
        interleave(on_vector, 7, 0, SHARE)
        quantize_v(6, X)
        multiply(nc.vector, parts[2])
        store_pair(0, 0, NH)
        quantize_v(7, X)
        subtract(parts[5], means[5])
        subtract(parts[4], means[4])
        multiply(nc.vector, parts[5])
        multiply(nc.gpsimd, wide_pair(0, 1))
        store_pair(1, 0, NH)

        banks = [next_bank() for m in range(3)]
        for g in range(G):
            for m in range(3):
                wide_passes(spread_operand, 1, m, banks[m], [g])
        for m in range(3):
            add_offset(wide(1, m), banks[m])
            exponential(wide(1, m))
        means = [wide_passes(ancestry_operand, 1, m, next_bank(), range(G)) for m in range(3)]
        subtract(wide(1, 0), means[0])
        for c in (5, 6, 7):
            quantize_v(c, Y)
        subtract(wide(1, 1), means[1])
        multiply(nc.vector, wide(1, 0))
        subtract(wide(1, 2), means[2])
        multiply(nc.vector, wide(1, 1))
        store_pair(0, NH, NH + NT)
        multiply(nc.gpsimd, wide(1, 2))
        store(2, NH, NH + NT)
        add_offset(narrow(1, 0), narrow_passes(spread_operand, 1, 0, next_bank(), range(G)))
        exponential(narrow(1, 0))
        subtract(narrow(1, 0), narrow_passes(ancestry_operand, 1, 0, next_bank(), range(G)))
        add_offset(wide(1, 3), wide_passes(spread_operand, 1, 3, next_bank(), range(G)))
        exponential(wide(1, 3))
        multiply(nc.vector, narrow(1, 0))
        store_pair(0, NH + NT, N)
        subtract(wide(1, 3), wide_passes(ancestry_operand, 1, 3, next_bank(), range(G)))
        ends = [(1, 1, i, i + 1, NT, NH) for i in range(2)]
        sums = [piece_passes(spread_operand, 1, 2 + i, NT, NH) for i in range(2)]
        add_offset(ends[0], sums[0])
        exponential(ends[0])
        multiply(nc.vector, wide(1, 3))
        store(3, NH, NH + NT)
        add_offset(ends[1], sums[1])
        exponential(ends[1])
        subtract(ends[0], piece_passes(ancestry_operand, 1, 2, NT, NH))
        for n0 in (NT, NT + P):
            subtract((1, 1, 1, 2, n0, n0 + P), piece_passes(ancestry_operand, 1, 3, n0, n0 + P))
        for i in range(2):
            multiply(nc.vector, ends[i])
            store(2 + i, NH + NT, N)
